import numpy as np
import ml_dtypes


def mxq(x, axis, fmt="e4m3"):
    dtype, down = {"e4m3": (ml_dtypes.float8_e4m3fn, 7), "e5m2": (ml_dtypes.float8_e5m2, 14)}[fmt]
    v = np.moveaxis(np.asarray(x, np.float32).astype(ml_dtypes.bfloat16).astype(np.float64), axis, -1)
    blocks = v.reshape(v.shape[:-1] + (-1, 32))
    amax = np.abs(blocks).max(-1, keepdims=True)
    byte = np.maximum(np.where(amax > 0, np.frexp(amax)[1] - 1 + 127, 0) - down, 1)
    scale = np.exp2(byte - 127.0)
    codes = (blocks / scale).astype(np.float32).astype(dtype).astype(np.float64)
    return np.moveaxis((codes * scale).reshape(v.shape), -1, axis)


WIDE = False


def mx_kscale(k):
    if not WIDE:
        return np.ones(k)
    levels = np.array([10, -10, 5, -5, 0])
    if k % 512:
        return np.exp2(np.random.permutation(np.resize(levels, k // 32))).repeat(32)
    a = np.empty((k // 512, 16))
    for p in range(k // 512):
        a[p, :8] = np.random.permutation(np.resize(levels, 8))
        for g in range(8):
            far = levels[np.abs(levels - a[p, g]) >= 10]
            a[p, g + 8] = far[np.random.randint(len(far))]
    return np.exp2(a.ravel()).repeat(32)


def f64(x):
    return np.asarray(x).astype(np.float64)


def striped(idx):
    return np.tile(idx.reshape(-1, 16).T, (8, 1)).astype(np.uint16)


def unstriped(offs):
    return offs[:16].T.reshape(-1).astype(np.int64)


E2M1 = np.array([0.0, 0.5, 1.0, 1.5, 2.0, 3.0, 4.0, 6.0, -0.0, -0.5, -1.0, -1.5, -2.0, -3.0, -4.0, -6.0])


def pack_weight(w, fmt):
    k, n = w.shape
    w = f64(np.asarray(w, np.float32).astype(ml_dtypes.bfloat16)).reshape(k // 32, 32, n)
    amax = np.abs(w).max(1)
    if fmt == "e4m3":
        byte = np.frexp(amax)[1] - 1 + 127 - 7
    else:
        mant, ex = np.frexp(amax / 6.0)
        byte = np.where(mant > 0.5, ex, ex - 1) + 127
    byte = np.clip(np.where(amax > 0, byte, 1), 1, 254)
    scaled = (w * np.exp2(127.0 - byte)[:, None, :]).reshape(k, n).astype(np.float32)
    by_word = np.ascontiguousarray(scaled.reshape(k // 512, 128, 4, n).transpose(0, 1, 3, 2))
    if fmt == "e4m3":
        words = by_word.astype(ml_dtypes.float8_e4m3fn).view(np.uint8)
    else:
        c = by_word.astype(ml_dtypes.float4_e2m1fn).view(np.uint8) & 0xF
        words = (c[..., 0::2] | (c[..., 1::2] << 4)).reshape(k // 512, 128, 2 * n)
    return np.ascontiguousarray(words), np.ascontiguousarray(byte.astype(np.uint8).reshape(k // 512, 16, n))


def unpack_weight(words, scales, fmt):
    g, _, n = scales.shape
    words = np.ascontiguousarray(words).reshape(g, 128, n, -1)
    if fmt == "e4m3":
        vals = words.view(ml_dtypes.float8_e4m3fn).astype(np.float64)
    else:
        nib = np.empty((g, 128, n, 4), np.uint8)
        nib[..., 0::2] = words & 0xF
        nib[..., 1::2] = words >> 4
        vals = E2M1[nib]
    vals = vals * np.repeat(np.exp2(scales.astype(np.float64) - 127.0), 8, axis=1)[..., None]
    return vals.transpose(0, 1, 3, 2).reshape(g * 512, n)


def gelu(v):
    return 0.5 * v * (1.0 + np.tanh(np.sqrt(2.0 / np.pi) * (v + 0.044715 * v**3)))


K, T, S, M, N = 1024, 2048, 1024, 512, 512

def setup_inputs():
    n = np.random.standard_normal
    s = mx_kscale(K)[:, None]
    u = mx_kscale(S)
    idx = np.random.permutation(T)[:S]
    v = n((K, T)) * s / np.sqrt(K)
    w4 = 0.7 * n((K, N)) * s / np.sqrt(K)
    wdT = n((N, T)) / np.sqrt(S)
    wdT[:, idx] /= u
    tab_words, tab_scales = pack_weight(v, "e4m3")
    w4_words, w4_scales = pack_weight(w4, "e2m1")
    return {
        "tab_words": tab_words, "tab_scales": tab_scales,
        "offs": striped(idx),
        "x": (0.7 * n((K, M)) / s).astype(np.float32),
        "dx": (n((K, M)) / s).astype(np.float32),
        "g": (np.exp(0.3 * n(S)) * u).astype(np.float32),
        "wdT": wdT.astype(np.float32),
        "w4_words": w4_words, "w4_scales": w4_scales,
    }

def reference(tab_words, tab_scales, offs, x, dx, g, wdT, w4_words, w4_scales):
    v = unpack_weight(tab_words, tab_scales, "e4m3")[:, unstriped(offs)]
    w4 = unpack_weight(w4_words, w4_scales, "e2m1")
    wd = f64(wdT)[:, unstriped(offs)]
    xq = mxq(f64(x), 0, "e4m3")
    dq = mxq(f64(dx), 0, "e4m3")
    a = v.T @ xq
    b = v.T @ dq
    t = np.tanh(a)
    h = (1.0 - np.square(t)) * b * f64(g)[:, None]
    return mxq(wd, 1, "e4m3") @ mxq(h, 0, "e4m3") + w4.T @ dq

@@ -1,0 +1,241 @@
+from contextlib import ExitStack
+
+import concourse.mybir as mybir
+from concourse.masks import make_identity
+
+K, T, S, M, N = 1024, 2048, 1024, 512, 512
+FLOPS = 2 * (2 * K * S * M + S * N * M + K * N * M)
+
+F32 = mybir.dt.float32
+BF16 = mybir.dt.bfloat16
+I32 = mybir.dt.int32
+U32 = mybir.dt.uint32
+U16 = mybir.dt.uint16
+U8 = mybir.dt.uint8
+FP8X4 = mybir.dt.float8_e4m3fn_x4
+FP4X4 = mybir.dt.float4_e2m1fn_x4
+ACT = mybir.ActivationFunctionType
+ALU = mybir.AluOpType
+
+P = 128
+PASS = 512
+K_PASSES = K // PASS
+J_PASSES = S // PASS
+N_TILES = N // P
+M_CHUNKS = M // P
+
+
+def tile_list_operator_tangent_flow_kernel(
+    tc, tab_words, tab_scales, offs, x, dx, g, wdT, w4_words, w4_scales, out
+):
+    nc = tc.nc
+    with ExitStack() as ctx:
+        keep = ctx.enter_context(tc.tile_pool(name="keep", bufs=1))
+        ring = ctx.enter_context(tc.tile_pool(name="ring", bufs=3))
+        psum = ctx.enter_context(tc.psum_pool(name="psum", bufs=1))
+
+        offsets = keep.tile([P, S // 16], U16, name="offsets")
+        nc.sync.dma_start(offsets[:], offs)
+
+        def list_pass(jp):
+            return offsets[:, jp * (PASS // 16) : (jp + 1) * (PASS // 16)]
+
+        tab_sc = keep.tile([P, T], U8, name="tab_sc", align_bytes=64)
+        nc.gpsimd.memset(tab_sc[:].bitcast(I32), 0)
+        g_rows = keep.tile([P, J_PASSES * P], F32, name="g_rows")
+        nc.gpsimd.memset(g_rows[:], 0.0)
+        ident = keep.tile([P, P], F32, name="ident")
+        make_identity(nc, ident[:])
+
+        for q in range(4):
+            nc.scalar.dma_start(
+                out=tab_sc[32 * q : 32 * q + 8, :].bitcast(I32),
+                in_=tab_scales.bitcast(I32)[:, 4 * q : 4 * q + 4, :],
+            )
+        nc.scalar.dma_start(
+            out=g_rows[0:4, :].rearrange("t (b r) -> t b r", r=8),
+            in_=g.rearrange("(b t r) -> t b r", t=4, r=8),
+        )
+
+        def load_rows(src, a, name, slot):
+            raw = keep.tile([P, 4, M], F32, name=name, tag="stage%d" % slot, align_bytes=64)
+            nc.sync.dma_start(out=raw[:], in_=src[a * PASS : (a + 1) * PASS, :].rearrange("(p t) m -> p t m", t=4))
+            return raw
+
+        def load_table(a):
+            words = keep.tile([P, T], I32, name="tab%d" % a, tag="stage%d" % a, align_bytes=64)
+            nc.sync.dma_start(out=words[:], in_=tab_words[a].rearrange("p n t -> p (n t)").bitcast(I32))
+            return words
+
+        def load_down(nt):
+            rows = keep.tile([P, T], F32, name="wd_raw%d" % nt, tag="stage%d" % ((nt + 2) % 4), align_bytes=64)
+            nc.sync.dma_start(out=rows[:], in_=wdT[nt * P : (nt + 1) * P, :])
+            return rows
+
+        def interleave(raw, name, tag, on_vector):
+            grouped = keep.tile([P, 4 * M], BF16, name=name, tag=tag, align_bytes=64)
+            dst = grouped[:].rearrange("p (c i t) -> p c t i", i=4, t=4)
+            src = raw[:].rearrange("p t (c i) -> p c t i", i=4)
+            if on_vector:
+                nc.vector.tensor_copy(out=dst, in_=src)
+            else:
+                nc.scalar.copy(out=dst, in_=src)
+            return grouped
+
+        def quantize(grouped_ap, width, name):
+            codes = keep.tile([P, width], U32, name=name + "_c", align_bytes=64)
+            scales = keep.tile([P, width], U8, name=name + "_s", align_bytes=64)
+            nc.vector.quantize_mx(out=codes[:].bitcast(FP8X4), scales=scales[:], in_=grouped_ap)
+            return codes, scales
+
+        tab = [load_table(a) for a in range(K_PASSES)]
+        x_raw = [load_rows(x, a, "x_raw%d" % a, 2 + a) for a in range(K_PASSES)]
+
+        v_codes = {}
+        for a in range(K_PASSES):
+            for jp in range(J_PASSES):
+                picked = keep.tile([P, PASS], U32, name="v%d_%d" % (a, jp), align_bytes=64)
+                nc.vector.tensor_copy(
+                    out=picked[:].rearrange("p (t b r) -> p b t r", t=4, r=8),
+                    in_=tab[a][:].bitcast(U32).indirect(list_pass(jp)),
+                )
+                v_codes[a, jp] = picked
+
+        v_sc_list = keep.tile([P, S], U8, name="v_sc_list", align_bytes=64)
+        nc.vector.tensor_copy(out=v_sc_list[:], in_=tab_sc[:].indirect(offsets[:]))
+        v_sc = keep.tile([P, S], U8, name="v_sc", align_bytes=64)
+        nc.vector.tensor_copy(
+            out=v_sc[:].bitcast(I32).rearrange("p (j t b w) -> p j t b w", j=J_PASSES, t=4, w=2),
+            in_=v_sc_list[:].bitcast(I32).rearrange("p (j b t w) -> p j t b w", j=J_PASSES, t=4, w=2),
+        )
+
+        xq = []
+        for a in range(K_PASSES):
+            grouped = interleave(x_raw[a], "x_grp%d" % a, "grp%d" % a, False)
+            xq.append(quantize(grouped[:], M, "xq%d" % a))
+
+        g_ps = psum.tile([P, J_PASSES, P], F32, name="g_ps", tag="x0")
+        for jp in range(J_PASSES):
+            nc.tensor.transpose(g_ps[:, jp, :], g_rows[:, jp * P : (jp + 1) * P], ident[:])
+        g_pos = keep.tile([P, J_PASSES, 4], F32, name="g_pos")
+        g_neg = keep.tile([P, J_PASSES, 4], F32, name="g_neg")
+        nc.scalar.copy(out=g_pos[:], in_=g_ps[:, :, 0:4])
+        nc.scalar.activation(out=g_neg[:], in_=g_ps[:, :, 0:4], func=ACT.Copy, scale=-1.0)
+
+        dx_raw = [load_rows(dx, a, "dx_raw%d" % a, a) for a in range(K_PASSES)]
+        dq = []
+        for a in range(K_PASSES):
+            grouped = interleave(dx_raw[a], "dx_grp%d" % a, "dgrp%d" % a, True)
+            dq.append(quantize(grouped[:], M, "dq%d" % a))
+
+        wd_raw = [load_down(nt) for nt in range(2)]
+        w4w = keep.tile([P, K_PASSES * 2 * N], U8, name="w4w", tag="grp0", align_bytes=64)
+        nc.sync.dma_start(
+            out=w4w[:].bitcast(I32).rearrange("p (a c) -> p a c", a=K_PASSES),
+            in_=w4_words.bitcast(I32).rearrange("a p c -> p a c"),
+        )
+        w4_sc = keep.tile([P, K_PASSES * N], U8, name="w4_sc", tag="grp1", align_bytes=64)
+        nc.gpsimd.memset(w4_sc[:].bitcast(I32), 0)
+        for q in range(4):
+            nc.sync.dma_start(
+                out=w4_sc[32 * q : 32 * q + 4, :].bitcast(I32).rearrange("r (a c) -> r a c", a=K_PASSES),
+                in_=w4_scales.bitcast(I32)[:, 4 * q : 4 * q + 4, :].rearrange("a r c -> r a c"),
+            )
+        wd_raw.extend(load_down(nt) for nt in range(2, N_TILES))
+
+        def first_product(acc, jp, t, act, cols):
+            for a in range(K_PASSES):
+                nc.tensor.matmul_mx(
+                    out=acc,
+                    lhsT=v_codes[a, jp][:, t * P : (t + 1) * P].bitcast(FP8X4),
+                    lhsT_scale=v_sc[4 * a :, jp * PASS + t * P : jp * PASS + (t + 1) * P],
+                    rhs=act[a][0][:, cols].bitcast(FP8X4),
+                    rhs_scale=act[a][1][:, cols],
+                    start=(a == 0),
+                    stop=(a == K_PASSES - 1),
+                )
+
+        hq, slopes = {}, []
+
+        def tangent(jp, c, tag):
+            cols = slice(c * P, (c + 1) * P)
+            b_ps = psum.tile([P, 4, P], F32, name="b_ps", tag=("z%d" % c if jp == 0 else "x%d" % (c % 2)))
+            for t in range(4):
+                first_product(b_ps[:, t, :], jp, t, dq, cols)
+            h_grp = keep.tile([P, 4 * P], BF16, name="h_grp", tag=tag, align_bytes=64)
+            nc.vector.tensor_tensor(
+                out=h_grp[:].rearrange("p (m t) -> p m t", t=4),
+                in0=b_ps[:].rearrange("p t m -> p m t"),
+                in1=slopes[jp][:, :, cols].rearrange("p t m -> p m t"),
+                op=ALU.mult,
+            )
+            hq[jp, c] = quantize(h_grp[:], P, "hq%d_%d" % (jp, c))
+
+        for jp in range(J_PASSES):
+            slope = keep.tile([P, 4, M], F32, name="slope%d" % jp)
+            for t in range(4):
+                a_ps = psum.tile([P, M], F32, name="a_ps", tag="y%d" % (t % 2))
+                first_product(a_ps[:], jp, t, xq, slice(0, M))
+                th = ring.tile([P, M], F32, name="th")
+                nc.scalar.activation(out=th[:], in_=a_ps[:], func=ACT.Tanh)
+                sq = ring.tile([P, M], F32, name="sq")
+                nc.scalar.activation(out=sq[:], in_=th[:], func=ACT.Square)
+                nc.scalar.activation(
+                    out=slope[:, t, :], in_=sq[:], func=ACT.Identity,
+                    scale=g_neg[:, jp, t : t + 1], bias=g_pos[:, jp, t : t + 1],
+                )
+            slopes.append(slope)
+            if jp == 0:
+                for c in range(M_CHUNKS):
+                    tangent(0, c, "h_grp0_%d" % c)
+
+        wq = []
+        for nt in range(N_TILES):
+            turned = psum.tile([P, J_PASSES, 2, P], F32, name="turned", tag="y%d" % (nt % 2))
+            for jp in range(J_PASSES):
+                picked = keep.tile([P, PASS], BF16, name="wd_picked%d_%d" % (nt, jp), align_bytes=64)
+                nc.vector.tensor_copy(
+                    out=picked[:].rearrange("p (u b r e) -> p b u e r", u=2, r=8, e=2),
+                    in_=wd_raw[nt][:].indirect(list_pass(jp)),
+                )
+                words = picked[:].bitcast(F32)
+                for u in range(2):
+                    nc.tensor.transpose(turned[:, jp, u, :], words[:, u * P : (u + 1) * P], ident[:])
+            wd_grp = keep.tile([P, J_PASSES * 4 * P], BF16, name="wd_grp", tag="wd_grp%d" % nt, align_bytes=64)
+            nc.scalar.copy(
+                out=wd_grp[:].bitcast(F32).rearrange("p (j n u) -> p j n u", j=J_PASSES, u=2),
+                in_=turned[:].rearrange("p j u n -> p j n u"),
+            )
+            wq.append(quantize(wd_grp[:], J_PASSES * P, "wq%d" % nt))
+
+        for c in range(M_CHUNKS):
+            tangent(1, c, "wd_grp3" if c == 1 else "h_grp1_%d" % c)
+
+        for c in range(M_CHUNKS):
+            cols = slice(c * P, (c + 1) * P)
+            acc = psum.tile([P, N_TILES, P], F32, name="acc", tag="z%d" % c)
+            for a in range(K_PASSES):
+                for nt in range(N_TILES):
+                    nc.tensor.matmul_mx(
+                        out=acc[:, nt, :],
+                        lhsT=w4w[:, a * 2 * N + nt * 2 * P : a * 2 * N + (nt + 1) * 2 * P].bitcast(FP4X4),
+                        lhsT_scale=w4_sc[:, a * N + nt * P : a * N + (nt + 1) * P],
+                        rhs=dq[a][0][:, cols].bitcast(FP8X4),
+                        rhs_scale=dq[a][1][:, cols],
+                        start=(a == 0 and nt == 0),
+                        stop=False,
+                    )
+            for jp in range(J_PASSES):
+                for nt in range(N_TILES):
+                    nc.tensor.matmul_mx(
+                        out=acc[:, nt, :],
+                        lhsT=wq[nt][0][:, jp * P : (jp + 1) * P].bitcast(FP8X4),
+                        lhsT_scale=wq[nt][1][:, jp * P : (jp + 1) * P],
+                        rhs=hq[jp, c][0][:].bitcast(FP8X4),
+                        rhs_scale=hq[jp, c][1][:],
+                        start=False,
+                        stop=(jp == J_PASSES - 1 and nt == N_TILES - 1),
+                    )
+            result = keep.tile([P, N_TILES, P], F32, name="result%d" % c)
+            nc.scalar.copy(out=result[:], in_=acc[:])
+            nc.sync.dma_start(out=out[:, cols].rearrange("(nt p) m -> p nt m", p=P), in_=result[:])

@@ -42,44 +42,41 @@ def tile_list_operator_tangent_flow_kernel(
 
         tab_sc = keep.tile([P, T], U8, name="tab_sc", align_bytes=64)
         nc.gpsimd.memset(tab_sc[:].bitcast(I32), 0)
-        g_rows = keep.tile([P, J_PASSES * P], F32, name="g_rows")
-        nc.gpsimd.memset(g_rows[:], 0.0)
+        w4_sc = keep.tile([P, K_PASSES * N], U8, name="w4_sc", align_bytes=64)
+        nc.vector.memset(w4_sc[:].bitcast(I32), 0)
         ident = keep.tile([P, P], F32, name="ident")
         make_identity(nc, ident[:])
 
-        for q in range(4):
-            nc.scalar.dma_start(
-                out=tab_sc[32 * q : 32 * q + 8, :].bitcast(I32),
-                in_=tab_scales.bitcast(I32)[:, 4 * q : 4 * q + 4, :],
-            )
-        nc.scalar.dma_start(
-            out=g_rows[0:4, :].rearrange("t (b r) -> t b r", r=8),
-            in_=g.rearrange("(b t r) -> t b r", t=4, r=8),
-        )
+        def load_table_scales(a):
+            for q in range(4):
+                nc.sync.dma_start(
+                    out=tab_sc[32 * q + 4 * a : 32 * q + 4 * a + 4, :].bitcast(I32),
+                    in_=tab_scales.bitcast(I32)[a, 4 * q : 4 * q + 4, :],
+                )
 
-        def load_rows(src, a, name, slot):
-            raw = keep.tile([P, 4, M], F32, name=name, tag="stage%d" % slot, align_bytes=64)
+        def load_rows(src, a, name):
+            raw = keep.tile([P, 4, M], F32, name=name, align_bytes=64)
             nc.sync.dma_start(out=raw[:], in_=src[a * PASS : (a + 1) * PASS, :].rearrange("(p t) m -> p t m", t=4))
             return raw
 
         def load_table(a):
-            words = keep.tile([P, T], I32, name="tab%d" % a, tag="stage%d" % a, align_bytes=64)
+            words = keep.tile([P, T], I32, name="tab%d" % a, align_bytes=64)
             nc.sync.dma_start(out=words[:], in_=tab_words[a].rearrange("p n t -> p (n t)").bitcast(I32))
             return words
 
         def load_down(nt):
-            rows = keep.tile([P, T], F32, name="wd_raw%d" % nt, tag="stage%d" % ((nt + 2) % 4), align_bytes=64)
+            rows = keep.tile([P, T], F32, name="wd_raw%d" % nt, align_bytes=64)
             nc.sync.dma_start(out=rows[:], in_=wdT[nt * P : (nt + 1) * P, :])
             return rows
 
-        def interleave(raw, name, tag, on_vector):
-            grouped = keep.tile([P, 4 * M], BF16, name=name, tag=tag, align_bytes=64)
-            dst = grouped[:].rearrange("p (c i t) -> p c t i", i=4, t=4)
-            src = raw[:].rearrange("p t (c i) -> p c t i", i=4)
-            if on_vector:
-                nc.vector.tensor_copy(out=dst, in_=src)
-            else:
-                nc.scalar.copy(out=dst, in_=src)
+        def interleave(raw, name, scalar_cols):
+            grouped = keep.tile([P, 4 * M], BF16, name=name, align_bytes=64)
+            for engine_copy, lo, hi in ((nc.scalar.copy, 0, scalar_cols), (nc.vector.tensor_copy, scalar_cols, M)):
+                if hi > lo:
+                    engine_copy(
+                        out=grouped[:, 4 * lo : 4 * hi].rearrange("p (c i t) -> p c t i", i=4, t=4),
+                        in_=raw[:, :, lo:hi].rearrange("p t (c i) -> p c t i", i=4),
+                    )
             return grouped
 
         def quantize(grouped_ap, width, name):
@@ -88,66 +85,66 @@ def tile_list_operator_tangent_flow_kernel(
             nc.vector.quantize_mx(out=codes[:].bitcast(FP8X4), scales=scales[:], in_=grouped_ap)
             return codes, scales
 
-        tab = [load_table(a) for a in range(K_PASSES)]
-        x_raw = [load_rows(x, a, "x_raw%d" % a, 2 + a) for a in range(K_PASSES)]
-
-        v_codes = {}
-        for a in range(K_PASSES):
-            for jp in range(J_PASSES):
-                picked = keep.tile([P, PASS], U32, name="v%d_%d" % (a, jp), align_bytes=64)
-                nc.vector.tensor_copy(
-                    out=picked[:].rearrange("p (t b r) -> p b t r", t=4, r=8),
-                    in_=tab[a][:].bitcast(U32).indirect(list_pass(jp)),
-                )
-                v_codes[a, jp] = picked
-
-        v_sc_list = keep.tile([P, S], U8, name="v_sc_list", align_bytes=64)
-        nc.vector.tensor_copy(out=v_sc_list[:], in_=tab_sc[:].indirect(offsets[:]))
-        v_sc = keep.tile([P, S], U8, name="v_sc", align_bytes=64)
-        nc.vector.tensor_copy(
-            out=v_sc[:].bitcast(I32).rearrange("p (j t b w) -> p j t b w", j=J_PASSES, t=4, w=2),
-            in_=v_sc_list[:].bitcast(I32).rearrange("p (j b t w) -> p j t b w", j=J_PASSES, t=4, w=2),
-        )
-
-        xq = []
-        for a in range(K_PASSES):
-            grouped = interleave(x_raw[a], "x_grp%d" % a, "grp%d" % a, False)
-            xq.append(quantize(grouped[:], M, "xq%d" % a))
-
-        g_ps = psum.tile([P, J_PASSES, P], F32, name="g_ps", tag="x0")
-        for jp in range(J_PASSES):
-            nc.tensor.transpose(g_ps[:, jp, :], g_rows[:, jp * P : (jp + 1) * P], ident[:])
+        tab = [load_table(0)]
+        load_table_scales(0)
+        tab.append(load_table(1))
+        x_raw = [load_rows(x, 0, "x_raw0")]
+        load_table_scales(1)
+        x_raw.append(load_rows(x, 1, "x_raw1"))
         g_pos = keep.tile([P, J_PASSES, 4], F32, name="g_pos")
-        g_neg = keep.tile([P, J_PASSES, 4], F32, name="g_neg")
-        nc.scalar.copy(out=g_pos[:], in_=g_ps[:, :, 0:4])
-        nc.scalar.activation(out=g_neg[:], in_=g_ps[:, :, 0:4], func=ACT.Copy, scale=-1.0)
-
-        dx_raw = [load_rows(dx, a, "dx_raw%d" % a, a) for a in range(K_PASSES)]
-        dq = []
-        for a in range(K_PASSES):
-            grouped = interleave(dx_raw[a], "dx_grp%d" % a, "dgrp%d" % a, True)
-            dq.append(quantize(grouped[:], M, "dq%d" % a))
-
-        wd_raw = [load_down(nt) for nt in range(2)]
-        w4w = keep.tile([P, K_PASSES * 2 * N], U8, name="w4w", tag="grp0", align_bytes=64)
+        nc.sync.dma_start(out=g_pos[:], in_=g.rearrange("(j p t) -> p j t", j=J_PASSES, t=4))
+        dx_raw = [load_rows(dx, 0, "dx_raw0")]
+        wd_raw = [load_down(0)]
+        dx_raw.append(load_rows(dx, 1, "dx_raw1"))
+        wd_raw.extend(load_down(nt) for nt in range(1, N_TILES))
+        w4w = keep.tile([P, K_PASSES * 2 * N], U8, name="w4w", align_bytes=64)
         nc.sync.dma_start(
             out=w4w[:].bitcast(I32).rearrange("p (a c) -> p a c", a=K_PASSES),
             in_=w4_words.bitcast(I32).rearrange("a p c -> p a c"),
         )
-        w4_sc = keep.tile([P, K_PASSES * N], U8, name="w4_sc", tag="grp1", align_bytes=64)
-        nc.gpsimd.memset(w4_sc[:].bitcast(I32), 0)
         for q in range(4):
             nc.sync.dma_start(
                 out=w4_sc[32 * q : 32 * q + 4, :].bitcast(I32).rearrange("r (a c) -> r a c", a=K_PASSES),
                 in_=w4_scales.bitcast(I32)[:, 4 * q : 4 * q + 4, :].rearrange("a r c -> r a c"),
             )
-        wd_raw.extend(load_down(nt) for nt in range(2, N_TILES))
+
+        v_codes = []
+        for a in range(K_PASSES):
+            listed = keep.tile([P, S], U32, name="v_list%d" % a, align_bytes=64)
+            nc.vector.tensor_copy(out=listed[:], in_=tab[a][:].bitcast(U32).indirect(offsets[:]))
+            dealt = keep.tile([P, S], U32, name="v%d" % a, align_bytes=64)
+            nc.vector.tensor_copy(
+                out=dealt[:].bitcast(I32).rearrange("p (j t c i) -> p j c t i", j=J_PASSES, t=4, i=4),
+                in_=listed[:].bitcast(I32).rearrange("p (j c i t) -> p j c t i", j=J_PASSES, t=4, i=4),
+            )
+            v_codes.append(dealt)
+
+        v_sc_list = keep.tile([P, S], U8, name="v_sc_list", align_bytes=64)
+        nc.vector.tensor_copy(out=v_sc_list[:], in_=tab_sc[:].indirect(offsets[:]))
+        v_sc = keep.tile([P, S], U8, name="v_sc", align_bytes=64)
+        nc.vector.tensor_copy(
+            out=v_sc[:].rearrange("p (j t c i) -> p j c t i", j=J_PASSES, t=4, i=16),
+            in_=v_sc_list[:].rearrange("p (j c i t) -> p j c t i", j=J_PASSES, t=4, i=16),
+        )
+
+        xq = []
+        for a in range(K_PASSES):
+            grouped = interleave(x_raw[a], "x_grp%d" % a, M)
+            xq.append(quantize(grouped[:], M, "xq%d" % a))
+
+        g_neg = keep.tile([P, J_PASSES, 4], F32, name="g_neg")
+        nc.scalar.activation(out=g_neg[:], in_=g_pos[:], func=ACT.Copy, scale=-1.0)
+
+        dq = []
+        for a in range(K_PASSES):
+            grouped = interleave(dx_raw[a], "dx_grp%d" % a, (M, 0)[a])
+            dq.append(quantize(grouped[:], M, "dq%d" % a))
 
         def first_product(acc, jp, t, act, cols):
             for a in range(K_PASSES):
                 nc.tensor.matmul_mx(
                     out=acc,
-                    lhsT=v_codes[a, jp][:, t * P : (t + 1) * P].bitcast(FP8X4),
+                    lhsT=v_codes[a][:, jp * PASS + t * P : jp * PASS + (t + 1) * P].bitcast(FP8X4),
                     lhsT_scale=v_sc[4 * a :, jp * PASS + t * P : jp * PASS + (t + 1) * P],
                     rhs=act[a][0][:, cols].bitcast(FP8X4),
                     rhs_scale=act[a][1][:, cols],
@@ -159,83 +156,97 @@ def tile_list_operator_tangent_flow_kernel(
 
         def tangent(jp, c, tag):
             cols = slice(c * P, (c + 1) * P)
-            b_ps = psum.tile([P, 4, P], F32, name="b_ps", tag=("z%d" % c if jp == 0 else "x%d" % (c % 2)))
+            b_ps = psum.tile([P, 4, P], F32, name="b_ps", tag=("z%d" % c if jp == 0 else ("x0", "x1", "y0", "x0")[c]))
             for t in range(4):
                 first_product(b_ps[:, t, :], jp, t, dq, cols)
             h_grp = keep.tile([P, 4 * P], BF16, name="h_grp", tag=tag, align_bytes=64)
             nc.vector.tensor_tensor(
-                out=h_grp[:].rearrange("p (m t) -> p m t", t=4),
-                in0=b_ps[:].rearrange("p t m -> p m t"),
-                in1=slopes[jp][:, :, cols].rearrange("p t m -> p m t"),
+                out=h_grp[:].rearrange("p (c i t) -> p c t i", i=2, t=4),
+                in0=b_ps[:].rearrange("p t (c i) -> p c t i", i=2),
+                in1=slopes[jp][:, :, cols].rearrange("p t (c i) -> p c t i", i=2),
                 op=ALU.mult,
             )
             hq[jp, c] = quantize(h_grp[:], P, "hq%d_%d" % (jp, c))
 
-        for jp in range(J_PASSES):
-            slope = keep.tile([P, 4, M], F32, name="slope%d" % jp)
-            for t in range(4):
-                a_ps = psum.tile([P, M], F32, name="a_ps", tag="y%d" % (t % 2))
-                first_product(a_ps[:], jp, t, xq, slice(0, M))
-                th = ring.tile([P, M], F32, name="th")
-                nc.scalar.activation(out=th[:], in_=a_ps[:], func=ACT.Tanh)
+        def slope_tile(jp, t):
+            a_ps = psum.tile([P, M], F32, name="a_ps", tag="y%d" % (t % 2))
+            first_product(a_ps[:], jp, t, xq, slice(0, M))
+            th = ring.tile([P, M], F32, name="th")
+            nc.scalar.activation(out=th[:], in_=a_ps[:], func=ACT.Tanh)
+            if (jp, t) == (1, 3):
+                sq = keep.tile([P, M], F32, name="sq_last", tag="wd_grp2", align_bytes=64)
+            else:
                 sq = ring.tile([P, M], F32, name="sq")
-                nc.scalar.activation(out=sq[:], in_=th[:], func=ACT.Square)
-                nc.scalar.activation(
-                    out=slope[:, t, :], in_=sq[:], func=ACT.Identity,
-                    scale=g_neg[:, jp, t : t + 1], bias=g_pos[:, jp, t : t + 1],
-                )
-            slopes.append(slope)
-            if jp == 0:
-                for c in range(M_CHUNKS):
-                    tangent(0, c, "h_grp0_%d" % c)
+            nc.scalar.activation(out=sq[:], in_=th[:], func=ACT.Square)
+            nc.scalar.activation(
+                out=slopes[jp][:, t, 0:M], in_=sq[:], func=ACT.Identity,
+                scale=g_neg[:, jp, t : t + 1], bias=g_pos[:, jp, t : t + 1],
+            )
 
         wq = []
-        for nt in range(N_TILES):
-            turned = psum.tile([P, J_PASSES, 2, P], F32, name="turned", tag="y%d" % (nt % 2))
+
+        def down_tile(nt):
+            turned = psum.tile([P, J_PASSES, 2, P], F32, name="turned", tag=("y0", "y1", "y1", "y1")[nt])
             for jp in range(J_PASSES):
                 picked = keep.tile([P, PASS], BF16, name="wd_picked%d_%d" % (nt, jp), align_bytes=64)
-                nc.vector.tensor_copy(
-                    out=picked[:].rearrange("p (u b r e) -> p b u e r", u=2, r=8, e=2),
-                    in_=wd_raw[nt][:].indirect(list_pass(jp)),
-                )
+                nc.vector.tensor_copy(out=picked[:], in_=wd_raw[nt][:].indirect(list_pass(jp)))
                 words = picked[:].bitcast(F32)
                 for u in range(2):
-                    nc.tensor.transpose(turned[:, jp, u, :], words[:, u * P : (u + 1) * P], ident[:])
+                    nc.tensor.transpose(turned[:, jp, u, :], words[:, u : 2 * P : 2], ident[:])
             wd_grp = keep.tile([P, J_PASSES * 4 * P], BF16, name="wd_grp", tag="wd_grp%d" % nt, align_bytes=64)
             nc.scalar.copy(
-                out=wd_grp[:].bitcast(F32).rearrange("p (j n u) -> p j n u", j=J_PASSES, u=2),
-                in_=turned[:].rearrange("p j u n -> p j n u"),
+                out=wd_grp[:].bitcast(F32).rearrange("p (j c i u) -> p j c u i", j=J_PASSES, i=2, u=2),
+                in_=turned[:].rearrange("p j u (c i) -> p j c u i", i=2),
             )
             wq.append(quantize(wd_grp[:], J_PASSES * P, "wq%d" % nt))
 
+        slopes.extend(keep.tile([P, 4, M + 4], F32, name="slope%d" % jp) for jp in range(J_PASSES))
+        for t in range(4):
+            slope_tile(0, t)
         for c in range(M_CHUNKS):
-            tangent(1, c, "wd_grp3" if c == 1 else "h_grp1_%d" % c)
+            tangent(0, c, "h_grp0_%d" % c)
+        slope_tile(1, 0)
+        down_tile(0)
+        slope_tile(1, 1)
+        down_tile(1)
+        slope_tile(1, 2)
+        slope_tile(1, 3)
+        down_tile(2)
+        down_tile(3)
 
         for c in range(M_CHUNKS):
+            tangent(1, c, "wd_grp3" if c == 3 else "h_grp1_%d" % c)
+
+        def output_block(c, tiles, bank, late_tile, copy_out):
             cols = slice(c * P, (c + 1) * P)
-            acc = psum.tile([P, N_TILES, P], F32, name="acc", tag="z%d" % c)
-            for a in range(K_PASSES):
-                for nt in range(N_TILES):
-                    nc.tensor.matmul_mx(
-                        out=acc[:, nt, :],
-                        lhsT=w4w[:, a * 2 * N + nt * 2 * P : a * 2 * N + (nt + 1) * 2 * P].bitcast(FP4X4),
-                        lhsT_scale=w4_sc[:, a * N + nt * P : a * N + (nt + 1) * P],
-                        rhs=dq[a][0][:, cols].bitcast(FP8X4),
-                        rhs_scale=dq[a][1][:, cols],
-                        start=(a == 0 and nt == 0),
-                        stop=False,
-                    )
-            for jp in range(J_PASSES):
-                for nt in range(N_TILES):
-                    nc.tensor.matmul_mx(
-                        out=acc[:, nt, :],
-                        lhsT=wq[nt][0][:, jp * P : (jp + 1) * P].bitcast(FP8X4),
-                        lhsT_scale=wq[nt][1][:, jp * P : (jp + 1) * P],
-                        rhs=hq[jp, c][0][:].bitcast(FP8X4),
-                        rhs_scale=hq[jp, c][1][:],
-                        start=False,
-                        stop=(jp == J_PASSES - 1 and nt == N_TILES - 1),
-                    )
-            result = keep.tile([P, N_TILES, P], F32, name="result%d" % c)
-            nc.scalar.copy(out=result[:], in_=acc[:])
-            nc.sync.dma_start(out=out[:, cols].rearrange("(nt p) m -> p nt m", p=P), in_=result[:])
+            acc = psum.tile([P, len(tiles), P], F32, name="acc", tag=bank)
+            passes = [("bypass", a, nt) for a in range(K_PASSES) for nt in tiles]
+            passes.extend(("down", jp, nt) for jp in range(J_PASSES) for nt in tiles if nt != late_tile)
+            passes.extend(("down", jp, nt) for jp in range(J_PASSES) for nt in tiles if nt == late_tile)
+            for step, (kind, a, nt) in enumerate(passes):
+                if kind == "bypass":
+                    lhs = w4w[:, a * 2 * N + nt * 2 * P : a * 2 * N + (nt + 1) * 2 * P].bitcast(FP4X4)
+                    lhs_scale = w4_sc[:, a * N + nt * P : a * N + (nt + 1) * P]
+                    rhs, rhs_scale = dq[a][0][:, cols], dq[a][1][:, cols]
+                else:
+                    lhs = wq[nt][0][:, a * P : (a + 1) * P].bitcast(FP8X4)
+                    lhs_scale = wq[nt][1][:, a * P : (a + 1) * P]
+                    rhs, rhs_scale = hq[a, c][0][:], hq[a, c][1][:]
+                nc.tensor.matmul_mx(
+                    out=acc[:, nt - tiles[0], :],
+                    lhsT=lhs,
+                    lhsT_scale=lhs_scale,
+                    rhs=rhs.bitcast(FP8X4),
+                    rhs_scale=rhs_scale,
+                    start=(step == 0),
+                    stop=(step == len(passes) - 1),
+                )
+            result = keep.tile([P, len(tiles), P], F32, name="result_" + bank)
+            copy_out(out=result[:], in_=acc[:])
+            rows = out[tiles[0] * P : (tiles[-1] + 1) * P, cols]
+            nc.sync.dma_start(out=rows.rearrange("(nt p) m -> p nt m", p=P), in_=result[:])
+
+        for c in range(M_CHUNKS - 1):
+            output_block(c, [0, 1, 2, 3], "z%d" % c, N_TILES - 1, nc.scalar.copy)
+        output_block(M_CHUNKS - 1, [0, 1], "z3", None, nc.scalar.copy)
+        output_block(M_CHUNKS - 1, [2, 3], "x1", None, nc.vector.tensor_copy)

@@ -178,9 +178,9 @@ def tile_list_operator_tangent_flow_kernel(
             else:
                 sq = ring.tile([P, M], F32, name="sq")
             nc.scalar.activation(out=sq[:], in_=th[:], func=ACT.Square)
-            nc.scalar.activation(
-                out=slopes[jp][:, t, 0:M], in_=sq[:], func=ACT.Identity,
-                scale=g_neg[:, jp, t : t + 1], bias=g_pos[:, jp, t : t + 1],
+            nc.gpsimd.tensor_scalar(
+                out=slopes[jp][:, t, 0:M], in0=sq[:], scalar1=g_neg[:, jp, t : t + 1],
+                scalar2=g_pos[:, jp, t : t + 1], op0=ALU.mult, op1=ALU.add,
             )
 
         wq = []

@@ -1,3 +1,4 @@
+import math
 from contextlib import ExitStack
 
 import concourse.mybir as mybir
@@ -17,12 +18,14 @@ FP4X4 = mybir.dt.float4_e2m1fn_x4
 ACT = mybir.ActivationFunctionType
 ALU = mybir.AluOpType
 
+WIDTH = {F32: 4, I32: 4, U32: 4, BF16: 2, U8: 1}
+
 P = 128
 PASS = 512
 K_PASSES = K // PASS
 J_PASSES = S // PASS
 N_TILES = N // P
-M_CHUNKS = M // P
+HALF = M // 2
 
 
 def tile_list_operator_tangent_flow_kernel(
@@ -31,8 +34,19 @@ def tile_list_operator_tangent_flow_kernel(
     nc = tc.nc
     with ExitStack() as ctx:
         keep = ctx.enter_context(tc.tile_pool(name="keep", bufs=1))
-        ring = ctx.enter_context(tc.tile_pool(name="ring", bufs=3))
         psum = ctx.enter_context(tc.psum_pool(name="psum", bufs=1))
+
+        work = ctx.enter_context(tc.tile_pool(name="work", bufs=1))
+        home = {"end": 0}
+
+        def place(name, shape, dtype, on=None, skip=0, spare=0):
+            size = math.prod(shape[1:]) * WIDTH[dtype] + spare
+            if on is None:
+                home[name] = home["end"]
+                home["end"] = home["end"] + size
+            else:
+                home[name] = home[on] + skip
+            return work.tile(shape, dtype, name=name, align_bytes=64, offset=home[name])
 
         offsets = keep.tile([P, S // 16], U16, name="offsets")
         nc.sync.dma_start(offsets[:], offs)
@@ -40,198 +54,216 @@ def tile_list_operator_tangent_flow_kernel(
         def list_pass(jp):
             return offsets[:, jp * (PASS // 16) : (jp + 1) * (PASS // 16)]
 
-        tab_sc = keep.tile([P, T], U8, name="tab_sc", align_bytes=64)
-        nc.gpsimd.memset(tab_sc[:].bitcast(I32), 0)
+        tab_sc = place("tab_sc", [P, T], U8)
+        nc.vector.memset(tab_sc[:].bitcast(I32), 0)
         w4_sc = keep.tile([P, K_PASSES * N], U8, name="w4_sc", align_bytes=64)
-        nc.vector.memset(w4_sc[:].bitcast(I32), 0)
+        nc.gpsimd.memset(w4_sc[:].bitcast(I32), 0)
         ident = keep.tile([P, P], F32, name="ident")
         make_identity(nc, ident[:])
 
-        def load_table_scales(a):
+        def load_table_scales():
             for q in range(4):
                 nc.sync.dma_start(
-                    out=tab_sc[32 * q + 4 * a : 32 * q + 4 * a + 4, :].bitcast(I32),
-                    in_=tab_scales.bitcast(I32)[a, 4 * q : 4 * q + 4, :],
+                    out=tab_sc[32 * q : 32 * q + 8, :].bitcast(I32),
+                    in_=tab_scales.bitcast(I32)[:, 4 * q : 4 * q + 4, :],
                 )
 
-        def load_rows(src, a, name):
-            raw = keep.tile([P, 4, M], F32, name=name, align_bytes=64)
-            nc.sync.dma_start(out=raw[:], in_=src[a * PASS : (a + 1) * PASS, :].rearrange("(p t) m -> p t m", t=4))
+        def load_rows(src, h, a, name):
+            raw = place(name, [P, 4, HALF], F32, spare=3072)
+            rows = src[a * PASS : (a + 1) * PASS, h * HALF : (h + 1) * HALF]
+            nc.sync.dma_start(out=raw[:], in_=rows.rearrange("(p t) m -> p t m", t=4))
             return raw
 
+        def load_half(src, h, name):
+            return [load_rows(src, h, a, "%s%d_%d" % (name, h, a)) for a in range(K_PASSES)]
+
         def load_table(a):
-            words = keep.tile([P, T], I32, name="tab%d" % a, align_bytes=64)
+            words = place("tab%d" % a, [P, T], I32)
             nc.sync.dma_start(out=words[:], in_=tab_words[a].rearrange("p n t -> p (n t)").bitcast(I32))
             return words
 
         def load_down(nt):
-            rows = keep.tile([P, T], F32, name="wd_raw%d" % nt, align_bytes=64)
+            rows = place("wd_raw%d" % nt, [P, T], F32)
             nc.sync.dma_start(out=rows[:], in_=wdT[nt * P : (nt + 1) * P, :])
             return rows
 
-        def interleave(raw, name, scalar_cols):
-            grouped = keep.tile([P, 4 * M], BF16, name=name, align_bytes=64)
-            for engine_copy, lo, hi in ((nc.scalar.copy, 0, scalar_cols), (nc.vector.tensor_copy, scalar_cols, M)):
-                if hi > lo:
-                    engine_copy(
-                        out=grouped[:, 4 * lo : 4 * hi].rearrange("p (c i t) -> p c t i", i=4, t=4),
-                        in_=raw[:, :, lo:hi].rearrange("p t (c i) -> p c t i", i=4),
-                    )
+        def load_gains():
+            gains = keep.tile([P, J_PASSES, 4], F32, name="g_pos")
+            nc.sync.dma_start(out=gains[:], in_=g.rearrange("(j p t) -> p j t", j=J_PASSES, t=4))
+            return gains
+
+        def load_bypass():
+            words = keep.tile([P, K_PASSES * 2 * N], U8, name="w4w", align_bytes=64)
+            nc.sync.dma_start(
+                out=words[:].bitcast(I32).rearrange("p (a c) -> p a c", a=K_PASSES),
+                in_=w4_words.bitcast(I32).rearrange("a p c -> p a c"),
+            )
+            for q in range(4):
+                nc.sync.dma_start(
+                    out=w4_sc[32 * q : 32 * q + 4, :].bitcast(I32).rearrange("r (a c) -> r a c", a=K_PASSES),
+                    in_=w4_scales.bitcast(I32)[:, 4 * q : 4 * q + 4, :].rearrange("a r c -> r a c"),
+                )
+            return words
+
+        def interleave(raws, name, copies, on=None, skip=0):
+            grouped = place(name, [P, K_PASSES * 4 * HALF], BF16, on, skip)
+            for a in range(K_PASSES):
+                copies[a](
+                    out=grouped[:, a * 4 * HALF : (a + 1) * 4 * HALF].rearrange("p (c i t) -> p c t i", i=4, t=4),
+                    in_=raws[a][:].rearrange("p t (c i) -> p c t i", i=4),
+                )
             return grouped
 
-        def quantize(grouped_ap, width, name):
-            codes = keep.tile([P, width], U32, name=name + "_c", align_bytes=64)
+        def quantize(grouped_ap, width, name, on=None, skip=0):
+            codes = place(name + "_c", [P, width], U32, on, skip)
             scales = keep.tile([P, width], U8, name=name + "_s", align_bytes=64)
             nc.vector.quantize_mx(out=codes[:].bitcast(FP8X4), scales=scales[:], in_=grouped_ap)
             return codes, scales
 
-        tab = [load_table(0)]
-        load_table_scales(0)
-        tab.append(load_table(1))
-        x_raw = [load_rows(x, 0, "x_raw0")]
-        load_table_scales(1)
-        x_raw.append(load_rows(x, 1, "x_raw1"))
-        g_pos = keep.tile([P, J_PASSES, 4], F32, name="g_pos")
-        nc.sync.dma_start(out=g_pos[:], in_=g.rearrange("(j p t) -> p j t", j=J_PASSES, t=4))
-        dx_raw = [load_rows(dx, 0, "dx_raw0")]
-        wd_raw = [load_down(0)]
-        dx_raw.append(load_rows(dx, 1, "dx_raw1"))
-        wd_raw.extend(load_down(nt) for nt in range(1, N_TILES))
-        w4w = keep.tile([P, K_PASSES * 2 * N], U8, name="w4w", align_bytes=64)
-        nc.sync.dma_start(
-            out=w4w[:].bitcast(I32).rearrange("p (a c) -> p a c", a=K_PASSES),
-            in_=w4_words.bitcast(I32).rearrange("a p c -> p a c"),
-        )
-        for q in range(4):
-            nc.sync.dma_start(
-                out=w4_sc[32 * q : 32 * q + 4, :].bitcast(I32).rearrange("r (a c) -> r a c", a=K_PASSES),
-                in_=w4_scales.bitcast(I32)[:, 4 * q : 4 * q + 4, :].rearrange("a r c -> r a c"),
-            )
+        x_raw, dx_raw, tab, wd_raw = {}, {}, {}, {}
+        x_raw[0] = [load_rows(x, 0, 0, "x0_0")]
+        load_table_scales()
+        tab[0] = load_table(0)
+        x_raw[0].append(load_rows(x, 0, 1, "x0_1"))
+        tab[1] = load_table(1)
+        g_pos = load_gains()
+        dx_raw[0] = load_half(dx, 0, "dx")
+        wd_raw[0] = load_down(0)
+        x_raw[1] = load_half(x, 1, "x")
+        wd_raw[1] = load_down(1)
+        w4w = load_bypass()
+        dx_raw[1] = load_half(dx, 1, "dx")
+        wd_raw[2] = load_down(2)
+        wd_raw[3] = load_down(3)
 
-        v_codes = []
-        for a in range(K_PASSES):
-            listed = keep.tile([P, S], U32, name="v_list%d" % a, align_bytes=64)
-            nc.vector.tensor_copy(out=listed[:], in_=tab[a][:].bitcast(U32).indirect(offsets[:]))
-            dealt = keep.tile([P, S], U32, name="v%d" % a, align_bytes=64)
+        def list_cols(lo, hi):
+            return offsets[:, lo * (PASS // 16) : hi * (PASS // 16)]
+
+        def gather_scales(lo, hi, name, on=None, skip=0):
+            listed = place(name, [P, (hi - lo) * PASS], U8, on, skip)
+            nc.vector.tensor_copy(out=listed[:], in_=tab_sc[:].indirect(list_cols(lo, hi)))
+            return listed
+
+        def deal_scales(listed, lo, hi, name, on=None, skip=0):
+            dealt = place(name, [P, (hi - lo) * PASS], U8, on, skip)
             nc.vector.tensor_copy(
-                out=dealt[:].bitcast(I32).rearrange("p (j t c i) -> p j c t i", j=J_PASSES, t=4, i=4),
-                in_=listed[:].bitcast(I32).rearrange("p (j c i t) -> p j c t i", j=J_PASSES, t=4, i=4),
+                out=dealt[:].rearrange("p (j t c i) -> p j c t i", j=hi - lo, t=4, i=16),
+                in_=listed[:].rearrange("p (j c i t) -> p j c t i", j=hi - lo, t=4, i=16),
             )
-            v_codes.append(dealt)
+            for jp in range(lo, hi):
+                v_sc[jp] = dealt[:, (jp - lo) * PASS : (jp - lo + 1) * PASS]
 
-        v_sc_list = keep.tile([P, S], U8, name="v_sc_list", align_bytes=64)
-        nc.vector.tensor_copy(out=v_sc_list[:], in_=tab_sc[:].indirect(offsets[:]))
-        v_sc = keep.tile([P, S], U8, name="v_sc", align_bytes=64)
-        nc.vector.tensor_copy(
-            out=v_sc[:].rearrange("p (j t c i) -> p j c t i", j=J_PASSES, t=4, i=16),
-            in_=v_sc_list[:].rearrange("p (j c i t) -> p j c t i", j=J_PASSES, t=4, i=16),
-        )
+        def gather_words(a, lo, hi, name, on=None, skip=0):
+            listed = place(name, [P, (hi - lo) * PASS], U32, on, skip)
+            nc.vector.tensor_copy(out=listed[:], in_=tab[a][:].bitcast(U32).indirect(list_cols(lo, hi)))
+            return listed
 
-        xq = []
-        for a in range(K_PASSES):
-            grouped = interleave(x_raw[a], "x_grp%d" % a, M)
-            xq.append(quantize(grouped[:], M, "xq%d" % a))
+        def deal_words(listed, a, lo, hi, name, on=None, skip=0):
+            dealt = place(name, [P, (hi - lo) * PASS], U32, on, skip)
+            nc.vector.tensor_copy(
+                out=dealt[:].bitcast(I32).rearrange("p (j t c i) -> p j c t i", j=hi - lo, t=4, i=4),
+                in_=listed[:].bitcast(I32).rearrange("p (j c i t) -> p j c t i", j=hi - lo, t=4, i=4),
+            )
+            for jp in range(lo, hi):
+                v_codes[a, jp] = dealt[:, (jp - lo) * PASS : (jp - lo + 1) * PASS]
 
-        g_neg = keep.tile([P, J_PASSES, 4], F32, name="g_neg")
-        nc.scalar.activation(out=g_neg[:], in_=g_pos[:], func=ACT.Copy, scale=-1.0)
+        v_sc, v_codes, xq, dq, hq, wq, slopes = {}, {}, {}, {}, {}, {}, {}
+        h_rounded, turned_tiles, wd_grouped = {}, {}, {}
 
-        dq = []
-        for a in range(K_PASSES):
-            grouped = interleave(dx_raw[a], "dx_grp%d" % a, (M, 0)[a])
-            dq.append(quantize(grouped[:], M, "dq%d" % a))
-
-        def first_product(acc, jp, t, act, cols):
+        def first_product(acc, jp, t, act, lo, width):
             for a in range(K_PASSES):
+                cols = slice(a * HALF + lo, a * HALF + lo + width)
                 nc.tensor.matmul_mx(
                     out=acc,
-                    lhsT=v_codes[a][:, jp * PASS + t * P : jp * PASS + (t + 1) * P].bitcast(FP8X4),
-                    lhsT_scale=v_sc[4 * a :, jp * PASS + t * P : jp * PASS + (t + 1) * P],
-                    rhs=act[a][0][:, cols].bitcast(FP8X4),
-                    rhs_scale=act[a][1][:, cols],
+                    lhsT=v_codes[a, jp][:, t * P : (t + 1) * P].bitcast(FP8X4),
+                    lhsT_scale=v_sc[jp][4 * a :, t * P : (t + 1) * P],
+                    rhs=act[0][:, cols].bitcast(FP8X4),
+                    rhs_scale=act[1][:, cols],
                     start=(a == 0),
                     stop=(a == K_PASSES - 1),
                 )
 
-        hq, slopes = {}, []
-
-        def tangent(jp, c, tag):
-            cols = slice(c * P, (c + 1) * P)
-            b_ps = psum.tile([P, 4, P], F32, name="b_ps", tag=("z%d" % c if jp == 0 else ("x0", "x1", "y0", "x0")[c]))
+        def slope_tile(h, jp, affine, th_on=None, sq_on=None, th_skip=0, banks=None):
+            slope = place("slope%d" % (2 * h + jp), [P, 4, HALF], F32)
+            th = place("th%d" % (2 * h + jp), [P, 4, HALF], F32, th_on, th_skip)
+            for u in range(2):
+                a_ps = psum.tile([P, 2, HALF], F32, name="a_ps", tag=banks[u] if banks else "p%d" % ((4 * h + 2 * jp + u) % 3))
+                for e in range(2):
+                    first_product(a_ps[:, e, :], jp, 2 * u + e, xq[h], 0, HALF)
+                nc.scalar.activation(out=th[:, 2 * u : 2 * u + 2, :], in_=a_ps[:], func=ACT.Tanh)
+            sq = place("sq%d" % (2 * h + jp), [P, 4, HALF], F32, sq_on)
+            for u in range(2):
+                nc.scalar.activation(out=sq[:, 2 * u : 2 * u + 2, :], in_=th[:, 2 * u : 2 * u + 2, :], func=ACT.Square)
             for t in range(4):
-                first_product(b_ps[:, t, :], jp, t, dq, cols)
-            h_grp = keep.tile([P, 4 * P], BF16, name="h_grp", tag=tag, align_bytes=64)
+                affine[t](slope[:, t, :], sq[:, t, :], g_neg[:, jp, t : t + 1], g_pos[:, jp, t : t + 1])
+            slopes[h, jp] = slope
+
+        def affine_scalar(dst, src, scale, bias):
+            nc.scalar.activation(out=dst, in_=src, func=ACT.Identity, scale=scale, bias=bias)
+
+        def affine_vector(dst, src, scale, bias):
+            nc.vector.tensor_scalar(out=dst, in0=src, scalar1=scale, scalar2=bias, op0=ALU.mult, op1=ALU.add)
+
+        def affine_pool(dst, src, scale, bias):
+            nc.gpsimd.tensor_scalar(out=dst, in0=src, scalar1=scale, scalar2=bias, op0=ALU.mult, op1=ALU.add)
+
+        def tangent(h, jp, c, h_grp):
+            b_ps = psum.tile([P, 4, P], F32, name="b_ps", tag="p%d" % (4 + c))
+            for t in range(4):
+                first_product(b_ps[:, t, :], jp, t, dq[h], c * P, P)
             nc.vector.tensor_tensor(
-                out=h_grp[:].rearrange("p (c i t) -> p c t i", i=2, t=4),
+                out=h_grp.rearrange("p (c i t) -> p c t i", i=2, t=4),
                 in0=b_ps[:].rearrange("p t (c i) -> p c t i", i=2),
-                in1=slopes[jp][:, :, cols].rearrange("p t (c i) -> p c t i", i=2),
+                in1=slopes[h, jp][:, :, c * P : (c + 1) * P].rearrange("p t (c i) -> p c t i", i=2),
                 op=ALU.mult,
             )
-            hq[jp, c] = quantize(h_grp[:], P, "hq%d_%d" % (jp, c))
 
-        def slope_tile(jp, t):
-            a_ps = psum.tile([P, M], F32, name="a_ps", tag="y%d" % (t % 2))
-            first_product(a_ps[:], jp, t, xq, slice(0, M))
-            th = ring.tile([P, M], F32, name="th")
-            nc.scalar.activation(out=th[:], in_=a_ps[:], func=ACT.Tanh)
-            if (jp, t) == (1, 3):
-                sq = keep.tile([P, M], F32, name="sq_last", tag="wd_grp2", align_bytes=64)
-            else:
-                sq = ring.tile([P, M], F32, name="sq")
-            nc.scalar.activation(out=sq[:], in_=th[:], func=ACT.Square)
-            nc.gpsimd.tensor_scalar(
-                out=slopes[jp][:, t, 0:M], in0=sq[:], scalar1=g_neg[:, jp, t : t + 1],
-                scalar2=g_pos[:, jp, t : t + 1], op0=ALU.mult, op1=ALU.add,
-            )
+        def tangent_tile(h, jp, on=None, skip=0):
+            h_rounded[h, jp] = place("h%d" % (2 * h + jp), [P, 4 * HALF], BF16, on, skip)
 
-        wq = []
+        def tangent_chunk(h, jp, c):
+            tangent(h, jp, c, h_rounded[h, jp][:, c * 4 * P : (c + 1) * 4 * P])
 
-        def down_tile(nt):
-            turned = psum.tile([P, J_PASSES, 2, P], F32, name="turned", tag=("y0", "y1", "y1", "y1")[nt])
+        def quantize_tangent(h, jp, lo, hi, on=None, skip=0):
+            name = "hq%d_%d" % (2 * h + jp, lo)
+            codes, scales = quantize(h_rounded[h, jp][:, lo * 4 * P : hi * 4 * P], (hi - lo) * P, name, on, skip)
+            for c in range(lo, hi):
+                cols = slice((c - lo) * P, (c - lo + 1) * P)
+                hq[h, jp, c] = (codes[:, cols], scales[:, cols])
+
+        def down_tile(nt, bank):
+            turned = psum.tile([P, J_PASSES, 2, P], F32, name="turned", tag=bank)
             for jp in range(J_PASSES):
-                picked = keep.tile([P, PASS], BF16, name="wd_picked%d_%d" % (nt, jp), align_bytes=64)
+                picked = place("picked%d_%d" % (nt, jp), [P, PASS], BF16, spare=2048 * (1 - jp))
                 nc.vector.tensor_copy(out=picked[:], in_=wd_raw[nt][:].indirect(list_pass(jp)))
                 words = picked[:].bitcast(F32)
                 for u in range(2):
                     nc.tensor.transpose(turned[:, jp, u, :], words[:, u : 2 * P : 2], ident[:])
-            wd_grp = keep.tile([P, J_PASSES * 4 * P], BF16, name="wd_grp", tag="wd_grp%d" % nt, align_bytes=64)
+            turned_tiles[nt] = turned
+
+        def copy_down(nt, on=None, skip=0):
+            wd_grp = place("wd_grp%d" % nt, [P, J_PASSES * 4 * P], BF16, on, skip)
             nc.scalar.copy(
                 out=wd_grp[:].bitcast(F32).rearrange("p (j c i u) -> p j c u i", j=J_PASSES, i=2, u=2),
-                in_=turned[:].rearrange("p j u (c i) -> p j c u i", i=2),
+                in_=turned_tiles[nt][:].rearrange("p j u (c i) -> p j c u i", i=2),
             )
-            wq.append(quantize(wd_grp[:], J_PASSES * P, "wq%d" % nt))
+            wd_grouped[nt] = wd_grp
 
-        slopes.extend(keep.tile([P, 4, M + 4], F32, name="slope%d" % jp) for jp in range(J_PASSES))
-        for t in range(4):
-            slope_tile(0, t)
-        for c in range(M_CHUNKS):
-            tangent(0, c, "h_grp0_%d" % c)
-        slope_tile(1, 0)
-        down_tile(0)
-        slope_tile(1, 1)
-        down_tile(1)
-        slope_tile(1, 2)
-        slope_tile(1, 3)
-        down_tile(2)
-        down_tile(3)
+        def quantize_down(nt, on=None, skip=0):
+            wq[nt] = quantize(wd_grouped[nt][:], J_PASSES * P, "wq%d" % nt, on, skip)
 
-        for c in range(M_CHUNKS):
-            tangent(1, c, "wd_grp3" if c == 3 else "h_grp1_%d" % c)
-
-        def output_block(c, tiles, bank, late_tile, copy_out):
-            cols = slice(c * P, (c + 1) * P)
+        def output_block(h, c, tiles, bank, order, copy_out):
             acc = psum.tile([P, len(tiles), P], F32, name="acc", tag=bank)
-            passes = [("bypass", a, nt) for a in range(K_PASSES) for nt in tiles]
-            passes.extend(("down", jp, nt) for jp in range(J_PASSES) for nt in tiles if nt != late_tile)
-            passes.extend(("down", jp, nt) for jp in range(J_PASSES) for nt in tiles if nt == late_tile)
-            for step, (kind, a, nt) in enumerate(passes):
+            for step, (kind, a, nt) in enumerate(order):
                 if kind == "bypass":
+                    cols = slice(a * HALF + c * P, a * HALF + (c + 1) * P)
                     lhs = w4w[:, a * 2 * N + nt * 2 * P : a * 2 * N + (nt + 1) * 2 * P].bitcast(FP4X4)
                     lhs_scale = w4_sc[:, a * N + nt * P : a * N + (nt + 1) * P]
-                    rhs, rhs_scale = dq[a][0][:, cols], dq[a][1][:, cols]
+                    rhs, rhs_scale = dq[h][0][:, cols], dq[h][1][:, cols]
                 else:
                     lhs = wq[nt][0][:, a * P : (a + 1) * P].bitcast(FP8X4)
                     lhs_scale = wq[nt][1][:, a * P : (a + 1) * P]
-                    rhs, rhs_scale = hq[a, c][0][:], hq[a, c][1][:]
+                    rhs, rhs_scale = hq[h, a, c]
                 nc.tensor.matmul_mx(
                     out=acc[:, nt - tiles[0], :],
                     lhsT=lhs,
@@ -239,14 +271,80 @@ def tile_list_operator_tangent_flow_kernel(
                     rhs=rhs.bitcast(FP8X4),
                     rhs_scale=rhs_scale,
                     start=(step == 0),
-                    stop=(step == len(passes) - 1),
+                    stop=(step == len(order) - 1),
                 )
             result = keep.tile([P, len(tiles), P], F32, name="result_" + bank)
             copy_out(out=result[:], in_=acc[:])
-            rows = out[tiles[0] * P : (tiles[-1] + 1) * P, cols]
+            m0 = h * HALF + c * P
+            rows = out[tiles[0] * P : (tiles[-1] + 1) * P, m0 : m0 + P]
             nc.sync.dma_start(out=rows.rearrange("(nt p) m -> p nt m", p=P), in_=result[:])
+            return result
 
-        for c in range(M_CHUNKS - 1):
-            output_block(c, [0, 1, 2, 3], "z%d" % c, N_TILES - 1, nc.scalar.copy)
-        output_block(M_CHUNKS - 1, [0, 1], "z3", None, nc.scalar.copy)
-        output_block(M_CHUNKS - 1, [2, 3], "x1", None, nc.vector.tensor_copy)
+        def weights_last(tiles):
+            passes = [("bypass", a, nt) for a in range(K_PASSES) for nt in tiles]
+            passes.extend(("down", jp, nt) for nt in tiles for jp in range(J_PASSES))
+            return passes
+
+        def tangent_last(tiles):
+            passes = [("bypass", a, nt) for a in range(K_PASSES) for nt in tiles]
+            passes.extend(("down", jp, nt) for jp in range(J_PASSES) for nt in tiles)
+            return passes
+
+        on_scalar = (nc.scalar.copy, nc.scalar.copy)
+        on_vector = (nc.vector.tensor_copy, nc.vector.tensor_copy)
+        every = [0, 1, 2, 3]
+        sc_list = gather_scales(0, 2, "sc_list")
+        list0 = gather_words(0, 0, 2, "list0")
+        x_grp0 = interleave(x_raw[0], "x_grp0", on_scalar)
+        deal_scales(sc_list, 0, 2, "v_sc", "x0_1")
+        deal_words(list0, 0, 0, 2, "v0", "x0_1", 1024)
+        xq[0] = quantize(x_grp0[:], 2 * HALF, "xq0")
+        list1a = gather_words(1, 0, 1, "list1a")
+        deal_words(list1a, 1, 0, 1, "v1a")
+        g_neg = keep.tile([P, J_PASSES, 4], F32, name="g_neg")
+        nc.scalar.activation(out=g_neg[:], in_=g_pos[:], func=ACT.Copy, scale=-1.0)
+        dx_grp0 = interleave(dx_raw[0], "dx_grp0", on_scalar)
+        list1b = gather_words(1, 1, 2, "list1b", "dx0_0")
+        dq[0] = quantize(dx_grp0[:], 2 * HALF, "dq0")
+        deal_words(list1b, 1, 1, 2, "v1b", "dx0_1")
+        slope_tile(0, 0, [affine_scalar] * 4, "dx0_1", None, 2048)
+        down_tile(0, "p6")
+        x_grp1 = interleave(x_raw[1], "x_grp1", on_vector)
+        slope_tile(0, 1, [affine_scalar] * 4, "th0")
+        copy_down(0, "sq0")
+        tangent_tile(0, 0, "picked0_0")
+        tangent_chunk(0, 0, 0)
+        xq[1] = quantize(x_grp1[:], 2 * HALF, "xq1")
+        tangent_chunk(0, 0, 1)
+        quantize_down(0)
+        quantize_tangent(0, 0, 0, 2)
+        down_tile(1, "p6")
+        tangent_tile(0, 1, "picked1_0")
+        tangent_chunk(0, 1, 0)
+        tangent_chunk(0, 1, 1)
+        dx_grp1 = interleave(dx_raw[1], "dx_grp1", on_scalar, "th1")
+        dq[1] = quantize(dx_grp1[:], 2 * HALF, "dq1")
+        quantize_tangent(0, 1, 0, 2, "dx1_1")
+        slope_tile(1, 0, [affine_scalar] * 4, "dx1_1", None, 3072)
+        copy_down(1, "dx1_1", 1024)
+        down_tile(2, "p6")
+        quantize_down(1, "picked2_0")
+        slope_tile(1, 1, [affine_scalar] * 4, "th2")
+        copy_down(2, "sq2")
+        down_tile(3, "p2")
+        quantize_down(2, "wd_raw2")
+        tangent_tile(1, 0, "picked3_0")
+        tangent_chunk(1, 0, 0)
+        tangent_chunk(1, 0, 1)
+        copy_down(3, "th3")
+        quantize_down(3)
+        quantize_tangent(1, 0, 0, 2)
+        output_block(0, 0, every, "p3", weights_last(every), nc.scalar.copy)
+        output_block(0, 1, every, "p7", weights_last(every), nc.scalar.copy)
+        tangent_tile(1, 1)
+        tangent_chunk(1, 1, 0)
+        tangent_chunk(1, 1, 1)
+        quantize_tangent(1, 1, 0, 1)
+        quantize_tangent(1, 1, 1, 2)
+        output_block(1, 0, every, "p1", tangent_last(every), nc.scalar.copy)
+        output_block(1, 1, every, "p0", tangent_last(every), nc.vector.tensor_copy)

@@ -39,11 +39,11 @@ def tile_list_operator_tangent_flow_kernel(
         work = ctx.enter_context(tc.tile_pool(name="work", bufs=1))
         home = {"end": 0}
 
-        def place(name, shape, dtype, on=None, skip=0, spare=0):
+        def place(name, shape, dtype, on=None, skip=0, spare=0, lead=0):
             size = math.prod(shape[1:]) * WIDTH[dtype] + spare
             if on is None:
-                home[name] = home["end"]
-                home["end"] = home["end"] + size
+                home[name] = home["end"] + lead
+                home["end"] = home[name] + size
             else:
                 home[name] = home[on] + skip
             return work.tile(shape, dtype, name=name, align_bytes=64, offset=home[name])
@@ -68,14 +68,10 @@ def tile_list_operator_tangent_flow_kernel(
                     in_=tab_scales.bitcast(I32)[:, 4 * q : 4 * q + 4, :],
                 )
 
-        def load_rows(src, h, a, name):
-            raw = place(name, [P, 4, HALF], F32, spare=3072)
-            rows = src[a * PASS : (a + 1) * PASS, h * HALF : (h + 1) * HALF]
-            nc.sync.dma_start(out=raw[:], in_=rows.rearrange("(p t) m -> p t m", t=4))
+        def load_rows(src, a, name):
+            raw = place(name, [P, 4, M], F32)
+            nc.sync.dma_start(out=raw[:], in_=src[a * PASS : (a + 1) * PASS, :].rearrange("(p t) m -> p t m", t=4))
             return raw
-
-        def load_half(src, h, name):
-            return [load_rows(src, h, a, "%s%d_%d" % (name, h, a)) for a in range(K_PASSES)]
 
         def load_table(a):
             words = place("tab%d" % a, [P, T], I32)
@@ -105,35 +101,34 @@ def tile_list_operator_tangent_flow_kernel(
                 )
             return words
 
-        def interleave(raws, name, copies, on=None, skip=0):
-            grouped = place(name, [P, K_PASSES * 4 * HALF], BF16, on, skip)
-            for a in range(K_PASSES):
-                copies[a](
-                    out=grouped[:, a * 4 * HALF : (a + 1) * 4 * HALF].rearrange("p (c i t) -> p c t i", i=4, t=4),
-                    in_=raws[a][:].rearrange("p t (c i) -> p c t i", i=4),
-                )
-            return grouped
+        def interleave(grouped, raw, a, h, copy):
+            copy(
+                out=grouped[:, a * 4 * HALF : (a + 1) * 4 * HALF].rearrange("p (c i t) -> p c t i", i=4, t=4),
+                in_=raw[:, :, h * HALF : (h + 1) * HALF].rearrange("p t (c i) -> p c t i", i=4),
+            )
+
+        def grouped_tile(name, on=None, skip=0):
+            return place(name, [P, K_PASSES * 4 * HALF], BF16, on, skip)
 
         def quantize(grouped_ap, width, name, on=None, skip=0):
-            codes = place(name + "_c", [P, width], U32, on, skip)
-            scales = keep.tile([P, width], U8, name=name + "_s", align_bytes=64)
+            codes = place(name + "_c", [P, width], U32)
+            scales = place(name + "_s", [P, width], U8, on, skip)
             nc.vector.quantize_mx(out=codes[:].bitcast(FP8X4), scales=scales[:], in_=grouped_ap)
             return codes, scales
 
         x_raw, dx_raw, tab, wd_raw = {}, {}, {}, {}
-        x_raw[0] = [load_rows(x, 0, 0, "x0_0")]
-        load_table_scales()
         tab[0] = load_table(0)
-        x_raw[0].append(load_rows(x, 0, 1, "x0_1"))
+        load_table_scales()
         tab[1] = load_table(1)
+        x_raw[0] = load_rows(x, 0, "x0")
+        x_raw[1] = load_rows(x, 1, "x1")
         g_pos = load_gains()
-        dx_raw[0] = load_half(dx, 0, "dx")
+        dx_raw[0] = load_rows(dx, 0, "dx0")
         wd_raw[0] = load_down(0)
-        x_raw[1] = load_half(x, 1, "x")
+        dx_raw[1] = load_rows(dx, 1, "dx1")
         wd_raw[1] = load_down(1)
-        w4w = load_bypass()
-        dx_raw[1] = load_half(dx, 1, "dx")
         wd_raw[2] = load_down(2)
+        w4w = load_bypass()
         wd_raw[3] = load_down(3)
 
         def list_cols(lo, hi):
@@ -168,7 +163,7 @@ def tile_list_operator_tangent_flow_kernel(
                 v_codes[a, jp] = dealt[:, (jp - lo) * PASS : (jp - lo + 1) * PASS]
 
         v_sc, v_codes, xq, dq, hq, wq, slopes = {}, {}, {}, {}, {}, {}, {}
-        h_rounded, turned_tiles, wd_grouped = {}, {}, {}
+        h_rounded, turned_tiles, wd_grouped, tanhs = {}, {}, {}, {}
 
         def first_product(acc, jp, t, act, lo, width):
             for a in range(K_PASSES):
@@ -183,19 +178,23 @@ def tile_list_operator_tangent_flow_kernel(
                     stop=(a == K_PASSES - 1),
                 )
 
-        def slope_tile(h, jp, affine, th_on=None, sq_on=None, th_skip=0, banks=None):
-            slope = place("slope%d" % (2 * h + jp), [P, 4, HALF], F32)
-            th = place("th%d" % (2 * h + jp), [P, 4, HALF], F32, th_on, th_skip)
+        def tanh_tile(h, jp, on=None, skip=0):
+            th = place("th%d" % (2 * h + jp), [P, 4, HALF], F32, on, skip, 2048 * (on is None))
             for u in range(2):
-                a_ps = psum.tile([P, 2, HALF], F32, name="a_ps", tag=banks[u] if banks else "p%d" % ((4 * h + 2 * jp + u) % 3))
+                a_ps = psum.tile([P, 2, HALF], F32, name="a_ps", tag="p%d" % (4 * h + 2 * jp + u))
                 for e in range(2):
                     first_product(a_ps[:, e, :], jp, 2 * u + e, xq[h], 0, HALF)
                 nc.scalar.activation(out=th[:, 2 * u : 2 * u + 2, :], in_=a_ps[:], func=ACT.Tanh)
-            sq = place("sq%d" % (2 * h + jp), [P, 4, HALF], F32, sq_on)
+            tanhs[h, jp] = th
+
+        def slope_tile(h, jp, affine, on=None, skip=0):
+            slope = place("slope%d" % (2 * h + jp), [P, 4, HALF + 4], F32)
+            sq = place("sq%d" % (2 * h + jp), [P, 4, HALF], F32, on, skip, 4096 * (on is None))
             for u in range(2):
-                nc.scalar.activation(out=sq[:, 2 * u : 2 * u + 2, :], in_=th[:, 2 * u : 2 * u + 2, :], func=ACT.Square)
+                pair = slice(2 * u, 2 * u + 2)
+                nc.scalar.activation(out=sq[:, pair, :], in_=tanhs[h, jp][:, pair, :], func=ACT.Square)
             for t in range(4):
-                affine[t](slope[:, t, :], sq[:, t, :], g_neg[:, jp, t : t + 1], g_pos[:, jp, t : t + 1])
+                affine[t](slope[:, t, 0:HALF], sq[:, t, :], g_neg[:, jp, t : t + 1], g_pos[:, jp, t : t + 1])
             slopes[h, jp] = slope
 
         def affine_scalar(dst, src, scale, bias):
@@ -207,8 +206,8 @@ def tile_list_operator_tangent_flow_kernel(
         def affine_pool(dst, src, scale, bias):
             nc.gpsimd.tensor_scalar(out=dst, in0=src, scalar1=scale, scalar2=bias, op0=ALU.mult, op1=ALU.add)
 
-        def tangent(h, jp, c, h_grp):
-            b_ps = psum.tile([P, 4, P], F32, name="b_ps", tag="p%d" % (4 + c))
+        def tangent(h, jp, c, h_grp, bank):
+            b_ps = psum.tile([P, 4, P], F32, name="b_ps", tag=bank)
             for t in range(4):
                 first_product(b_ps[:, t, :], jp, t, dq[h], c * P, P)
             nc.vector.tensor_tensor(
@@ -221,12 +220,13 @@ def tile_list_operator_tangent_flow_kernel(
         def tangent_tile(h, jp, on=None, skip=0):
             h_rounded[h, jp] = place("h%d" % (2 * h + jp), [P, 4 * HALF], BF16, on, skip)
 
-        def tangent_chunk(h, jp, c):
-            tangent(h, jp, c, h_rounded[h, jp][:, c * 4 * P : (c + 1) * 4 * P])
+        def tangent_chunk(h, jp, c, bank):
+            tangent(h, jp, c, h_rounded[h, jp][:, c * 4 * P : (c + 1) * 4 * P], bank)
 
         def quantize_tangent(h, jp, lo, hi, on=None, skip=0):
             name = "hq%d_%d" % (2 * h + jp, lo)
             codes, scales = quantize(h_rounded[h, jp][:, lo * 4 * P : hi * 4 * P], (hi - lo) * P, name, on, skip)
+            hq[h, jp] = (codes[:], scales[:])
             for c in range(lo, hi):
                 cols = slice((c - lo) * P, (c - lo + 1) * P)
                 hq[h, jp, c] = (codes[:, cols], scales[:, cols])
@@ -234,7 +234,7 @@ def tile_list_operator_tangent_flow_kernel(
         def down_tile(nt, bank):
             turned = psum.tile([P, J_PASSES, 2, P], F32, name="turned", tag=bank)
             for jp in range(J_PASSES):
-                picked = place("picked%d_%d" % (nt, jp), [P, PASS], BF16, spare=2048 * (1 - jp))
+                picked = place("picked%d_%d" % (nt, jp), [P, PASS], BF16, spare=3584, lead=2048 * (nt == 3 and jp == 0))
                 nc.vector.tensor_copy(out=picked[:], in_=wd_raw[nt][:].indirect(list_pass(jp)))
                 words = picked[:].bitcast(F32)
                 for u in range(2):
@@ -280,6 +280,32 @@ def tile_list_operator_tangent_flow_kernel(
             nc.sync.dma_start(out=rows.rearrange("(nt p) m -> p nt m", p=P), in_=result[:])
             return result
 
+        def output_half(h, tiles, bank, order, copy_out):
+            acc = psum.tile([P, len(tiles), HALF], F32, name="acc", tag=bank)
+            for step, (kind, a, nt) in enumerate(order):
+                if kind == "bypass":
+                    cols = slice(a * HALF, (a + 1) * HALF)
+                    lhs = w4w[:, a * 2 * N + nt * 2 * P : a * 2 * N + (nt + 1) * 2 * P].bitcast(FP4X4)
+                    lhs_scale = w4_sc[:, a * N + nt * P : a * N + (nt + 1) * P]
+                    rhs, rhs_scale = dq[h][0][:, cols], dq[h][1][:, cols]
+                else:
+                    lhs = wq[nt][0][:, a * P : (a + 1) * P].bitcast(FP8X4)
+                    lhs_scale = wq[nt][1][:, a * P : (a + 1) * P]
+                    rhs, rhs_scale = hq[h, a]
+                nc.tensor.matmul_mx(
+                    out=acc[:, nt - tiles[0], :],
+                    lhsT=lhs,
+                    lhsT_scale=lhs_scale,
+                    rhs=rhs.bitcast(FP8X4),
+                    rhs_scale=rhs_scale,
+                    start=(step == 0),
+                    stop=(step == len(order) - 1),
+                )
+            result = keep.tile([P, len(tiles), HALF], F32, name="result_" + bank)
+            copy_out(out=result[:], in_=acc[:])
+            rows = out[tiles[0] * P : (tiles[-1] + 1) * P, h * HALF : (h + 1) * HALF]
+            nc.sync.dma_start(out=rows.rearrange("(nt p) m -> p nt m", p=P), in_=result[:])
+
         def weights_last(tiles):
             passes = [("bypass", a, nt) for a in range(K_PASSES) for nt in tiles]
             passes.extend(("down", jp, nt) for nt in tiles for jp in range(J_PASSES))
@@ -293,58 +319,64 @@ def tile_list_operator_tangent_flow_kernel(
         on_scalar = (nc.scalar.copy, nc.scalar.copy)
         on_vector = (nc.vector.tensor_copy, nc.vector.tensor_copy)
         every = [0, 1, 2, 3]
-        sc_list = gather_scales(0, 2, "sc_list")
         list0 = gather_words(0, 0, 2, "list0")
-        x_grp0 = interleave(x_raw[0], "x_grp0", on_scalar)
-        deal_scales(sc_list, 0, 2, "v_sc", "x0_1")
-        deal_words(list0, 0, 0, 2, "v0", "x0_1", 1024)
-        xq[0] = quantize(x_grp0[:], 2 * HALF, "xq0")
-        list1a = gather_words(1, 0, 1, "list1a")
-        deal_words(list1a, 1, 0, 1, "v1a")
+        list1 = gather_words(1, 0, 2, "list1")
+        deal_words(list0, 0, 0, 2, "v0", "tab1")
+        sc_list = gather_scales(0, 2, "sc_list", "tab1", 4096)
+        deal_words(list1, 1, 0, 2, "v1", "list0")
+        x_grp = [grouped_tile("x_grp%d" % h) for h in range(2)]
+        for a in range(K_PASSES):
+            for h in range(2):
+                interleave(x_grp[h], x_raw[a], a, h, nc.scalar.copy)
+        deal_scales(sc_list, 0, 2, "v_sc")
+        for h in range(2):
+            xq[h] = quantize(x_grp[h][:], 2 * HALF, "xq%d" % h)
         g_neg = keep.tile([P, J_PASSES, 4], F32, name="g_neg")
         nc.scalar.activation(out=g_neg[:], in_=g_pos[:], func=ACT.Copy, scale=-1.0)
-        dx_grp0 = interleave(dx_raw[0], "dx_grp0", on_scalar)
-        list1b = gather_words(1, 1, 2, "list1b", "dx0_0")
-        dq[0] = quantize(dx_grp0[:], 2 * HALF, "dq0")
-        deal_words(list1b, 1, 1, 2, "v1b", "dx0_1")
-        slope_tile(0, 0, [affine_scalar] * 4, "dx0_1", None, 2048)
-        down_tile(0, "p6")
-        x_grp1 = interleave(x_raw[1], "x_grp1", on_vector)
-        slope_tile(0, 1, [affine_scalar] * 4, "th0")
-        copy_down(0, "sq0")
-        tangent_tile(0, 0, "picked0_0")
-        tangent_chunk(0, 0, 0)
-        xq[1] = quantize(x_grp1[:], 2 * HALF, "xq1")
-        tangent_chunk(0, 0, 1)
-        quantize_down(0)
+        dx_grp = [grouped_tile("dx_grp%d" % h) for h in range(2)]
+        interleave(dx_grp[0], dx_raw[0], 0, 0, nc.vector.tensor_copy)
+        interleave(dx_grp[1], dx_raw[0], 0, 1, nc.vector.tensor_copy)
+        tanh_tile(0, 0)
+        tanh_tile(0, 1)
+        down_tile(0, "p0")
+        interleave(dx_grp[0], dx_raw[1], 1, 0, nc.vector.tensor_copy)
+        interleave(dx_grp[1], dx_raw[1], 1, 1, nc.vector.tensor_copy)
+        dq[0] = quantize(dx_grp[0][:], 2 * HALF, "dq0")
+        dq[1] = quantize(dx_grp[1][:], 2 * HALF, "dq1")
+        slope_tile(0, 0, [affine_scalar] * 4)
+        copy_down(0, "th0")
+        tanh_tile(1, 0, "sq0")
+        tanh_tile(1, 1, "th0", 2048)
+        down_tile(1, "p3")
+        copy_down(1)
+        slope_tile(0, 1, [affine_scalar] * 4, "picked1_1")
+        down_tile(2, "p0")
+        copy_down(2)
+        slope_tile(1, 0, [affine_scalar] * 4, "picked2_1", 256)
+        down_tile(3, "p0")
+        copy_down(3)
+        slope_tile(1, 1, [affine_scalar] * 4, "picked3_1")
+        quantize_down(0, "wd_raw3")
+        tangent_tile(0, 0, "wd_raw3", 1024)
+        tangent_tile(0, 1, "wd_raw3", 3072)
+        tangent_chunk(0, 0, 0, "p1")
+        tangent_chunk(0, 0, 1, "p2")
+        quantize_down(1, "wd_raw3", 256)
         quantize_tangent(0, 0, 0, 2)
-        down_tile(1, "p6")
-        tangent_tile(0, 1, "picked1_0")
-        tangent_chunk(0, 1, 0)
-        tangent_chunk(0, 1, 1)
-        dx_grp1 = interleave(dx_raw[1], "dx_grp1", on_scalar, "th1")
-        dq[1] = quantize(dx_grp1[:], 2 * HALF, "dq1")
-        quantize_tangent(0, 1, 0, 2, "dx1_1")
-        slope_tile(1, 0, [affine_scalar] * 4, "dx1_1", None, 3072)
-        copy_down(1, "dx1_1", 1024)
-        down_tile(2, "p6")
-        quantize_down(1, "picked2_0")
-        slope_tile(1, 1, [affine_scalar] * 4, "th2")
-        copy_down(2, "sq2")
-        down_tile(3, "p2")
-        quantize_down(2, "wd_raw2")
-        tangent_tile(1, 0, "picked3_0")
-        tangent_chunk(1, 0, 0)
-        tangent_chunk(1, 0, 1)
-        copy_down(3, "th3")
+        tangent_chunk(0, 1, 0, "p6")
+        tangent_chunk(0, 1, 1, "p7")
+        quantize_down(2, "wd_raw3", 512)
+        quantize_tangent(0, 1, 0, 2)
+        tangent_tile(1, 0, "slope1")
+        tangent_chunk(1, 0, 0, "p1")
+        tangent_chunk(1, 0, 1, "p2")
         quantize_down(3)
         quantize_tangent(1, 0, 0, 2)
-        output_block(0, 0, every, "p3", weights_last(every), nc.scalar.copy)
-        output_block(0, 1, every, "p7", weights_last(every), nc.scalar.copy)
-        tangent_tile(1, 1)
-        tangent_chunk(1, 1, 0)
-        tangent_chunk(1, 1, 1)
-        quantize_tangent(1, 1, 0, 1)
-        quantize_tangent(1, 1, 1, 2)
-        output_block(1, 0, every, "p1", tangent_last(every), nc.scalar.copy)
-        output_block(1, 1, every, "p0", tangent_last(every), nc.vector.tensor_copy)
+        output_half(0, [0, 1], "p4", tangent_last([0, 1]), nc.scalar.copy)
+        output_half(0, [2, 3], "p5", weights_last([2, 3]), nc.scalar.copy)
+        tangent_tile(1, 1, "slope2")
+        tangent_chunk(1, 1, 0, "p6")
+        tangent_chunk(1, 1, 1, "p7")
+        quantize_tangent(1, 1, 0, 2)
+        output_half(1, [0, 1], "p3", tangent_last([0, 1]), nc.scalar.copy)
+        output_half(1, [2, 3], "p0", tangent_last([2, 3]), nc.vector.tensor_copy)

@@ -61,11 +61,11 @@ def tile_list_operator_tangent_flow_kernel(
         ident = keep.tile([P, P], F32, name="ident")
         make_identity(nc, ident[:])
 
-        def load_table_scales():
+        def load_table_scales(a):
             for q in range(4):
                 nc.sync.dma_start(
-                    out=tab_sc[32 * q : 32 * q + 8, :].bitcast(I32),
-                    in_=tab_scales.bitcast(I32)[:, 4 * q : 4 * q + 4, :],
+                    out=tab_sc[32 * q + 4 * a : 32 * q + 4 * a + 4, :].bitcast(I32),
+                    in_=tab_scales.bitcast(I32)[a, 4 * q : 4 * q + 4, :],
                 )
 
         def load_rows(src, a, name):
@@ -118,17 +118,18 @@ def tile_list_operator_tangent_flow_kernel(
 
         x_raw, dx_raw, tab, wd_raw = {}, {}, {}, {}
         tab[0] = load_table(0)
-        load_table_scales()
+        load_table_scales(0)
         tab[1] = load_table(1)
         x_raw[0] = load_rows(x, 0, "x0")
+        load_table_scales(1)
         x_raw[1] = load_rows(x, 1, "x1")
         g_pos = load_gains()
         dx_raw[0] = load_rows(dx, 0, "dx0")
-        wd_raw[0] = load_down(0)
         dx_raw[1] = load_rows(dx, 1, "dx1")
+        wd_raw[0] = load_down(0)
         wd_raw[1] = load_down(1)
-        wd_raw[2] = load_down(2)
         w4w = load_bypass()
+        wd_raw[2] = load_down(2)
         wd_raw[3] = load_down(3)
 
         def list_cols(lo, hi):
@@ -338,45 +339,46 @@ def tile_list_operator_tangent_flow_kernel(
         interleave(dx_grp[1], dx_raw[0], 0, 1, nc.vector.tensor_copy)
         tanh_tile(0, 0)
         tanh_tile(0, 1)
-        down_tile(0, "p0")
+        tanh_tile(1, 0)
+        tanh_tile(1, 1)
         interleave(dx_grp[0], dx_raw[1], 1, 0, nc.vector.tensor_copy)
         interleave(dx_grp[1], dx_raw[1], 1, 1, nc.vector.tensor_copy)
         dq[0] = quantize(dx_grp[0][:], 2 * HALF, "dq0")
         dq[1] = quantize(dx_grp[1][:], 2 * HALF, "dq1")
         slope_tile(0, 0, [affine_scalar] * 4)
-        copy_down(0, "th0")
-        tanh_tile(1, 0, "sq0")
-        tanh_tile(1, 1, "th0", 2048)
+        down_tile(0, "p0")
+        copy_down(0)
+        slope_tile(0, 1, [affine_scalar] * 4, "picked0_1")
         down_tile(1, "p3")
         copy_down(1)
-        slope_tile(0, 1, [affine_scalar] * 4, "picked1_1")
-        down_tile(2, "p0")
-        copy_down(2)
-        slope_tile(1, 0, [affine_scalar] * 4, "picked2_1", 256)
-        down_tile(3, "p0")
-        copy_down(3)
-        slope_tile(1, 1, [affine_scalar] * 4, "picked3_1")
-        quantize_down(0, "wd_raw3")
-        tangent_tile(0, 0, "wd_raw3", 1024)
-        tangent_tile(0, 1, "wd_raw3", 3072)
+        quantize_down(0, "wd_raw1")
+        tangent_tile(0, 0, "wd_raw1", 1024)
         tangent_chunk(0, 0, 0, "p1")
         tangent_chunk(0, 0, 1, "p2")
-        quantize_down(1, "wd_raw3", 256)
-        quantize_tangent(0, 0, 0, 2)
+        slope_tile(1, 0, [affine_scalar] * 4, "picked1_1")
+        down_tile(2, "p0")
+        copy_down(2)
+        slope_tile(1, 1, [affine_scalar] * 4, "picked2_1")
+        down_tile(3, "p3")
+        copy_down(3)
+        quantize_tangent(0, 0, 0, 2, "wd_raw3")
+        tangent_tile(0, 1, "wd_raw3", 1024)
         tangent_chunk(0, 1, 0, "p6")
         tangent_chunk(0, 1, 1, "p7")
-        quantize_down(2, "wd_raw3", 512)
+        quantize_down(1, "wd_raw3", 256)
         quantize_tangent(0, 1, 0, 2)
+        quantize_down(2, "wd_raw3", 512)
         tangent_tile(1, 0, "slope1")
         tangent_chunk(1, 0, 0, "p1")
         tangent_chunk(1, 0, 1, "p2")
-        quantize_down(3)
+        quantize_down(3, "wd_grp2")
         quantize_tangent(1, 0, 0, 2)
         output_half(0, [0, 1], "p4", tangent_last([0, 1]), nc.scalar.copy)
         output_half(0, [2, 3], "p5", weights_last([2, 3]), nc.scalar.copy)
         tangent_tile(1, 1, "slope2")
         tangent_chunk(1, 1, 0, "p6")
         tangent_chunk(1, 1, 1, "p7")
-        quantize_tangent(1, 1, 0, 2)
-        output_half(1, [0, 1], "p3", tangent_last([0, 1]), nc.scalar.copy)
-        output_half(1, [2, 3], "p0", tangent_last([2, 3]), nc.vector.tensor_copy)
+        quantize_tangent(1, 1, 0, 1)
+        quantize_tangent(1, 1, 1, 2)
+        output_block(1, 0, every, "p0", tangent_last(every), nc.scalar.copy)
+        output_block(1, 1, every, "p3", tangent_last(every), nc.vector.tensor_copy)

@@ -35,26 +35,21 @@ def tile_list_operator_tangent_flow_kernel(
     with ExitStack() as ctx:
         keep = ctx.enter_context(tc.tile_pool(name="keep", bufs=1))
         psum = ctx.enter_context(tc.psum_pool(name="psum", bufs=1))
-
         work = ctx.enter_context(tc.tile_pool(name="work", bufs=1))
         home = {"end": 0}
 
-        def place(name, shape, dtype, on=None, skip=0, spare=0, lead=0):
-            size = math.prod(shape[1:]) * WIDTH[dtype] + spare
+        def place(name, shape, dtype, on=None, spare=0, lead=0):
             if on is None:
                 home[name] = home["end"] + lead
-                home["end"] = home[name] + size
+                home["end"] = home[name] + math.prod(shape[1:]) * WIDTH[dtype] + spare
             else:
-                home[name] = home[on] + skip
+                home[name] = home[on[0]] + on[1]
             return work.tile(shape, dtype, name=name, align_bytes=64, offset=home[name])
 
         offsets = keep.tile([P, S // 16], U16, name="offsets")
         nc.sync.dma_start(offsets[:], offs)
 
-        def list_pass(jp):
-            return offsets[:, jp * (PASS // 16) : (jp + 1) * (PASS // 16)]
-
-        tab_sc = place("tab_sc", [P, T], U8)
+        tab_sc = place("tab_sc", [P, T], U8, spare=6144)
         nc.vector.memset(tab_sc[:].bitcast(I32), 0)
         w4_sc = keep.tile([P, K_PASSES * N], U8, name="w4_sc", align_bytes=64)
         nc.gpsimd.memset(w4_sc[:].bitcast(I32), 0)
@@ -69,7 +64,7 @@ def tile_list_operator_tangent_flow_kernel(
                 )
 
         def load_rows(src, a, name):
-            raw = place(name, [P, 4, M], F32)
+            raw = place(name, [P, 4, M], F32, spare=8192, lead=64)
             nc.sync.dma_start(out=raw[:], in_=src[a * PASS : (a + 1) * PASS, :].rearrange("(p t) m -> p t m", t=4))
             return raw
 
@@ -101,20 +96,32 @@ def tile_list_operator_tangent_flow_kernel(
                 )
             return words
 
-        def interleave(grouped, raw, a, h, copy):
+        def interleave(grouped, raw, lo, hi, copy):
             copy(
-                out=grouped[:, a * 4 * HALF : (a + 1) * 4 * HALF].rearrange("p (c i t) -> p c t i", i=4, t=4),
-                in_=raw[:, :, h * HALF : (h + 1) * HALF].rearrange("p t (c i) -> p c t i", i=4),
+                out=grouped[:, 4 * lo : 4 * hi].rearrange("p (c i t) -> p c t i", i=4, t=4),
+                in_=raw[:, :, lo:hi].rearrange("p t (c i) -> p c t i", i=4),
             )
 
-        def grouped_tile(name, on=None, skip=0):
-            return place(name, [P, K_PASSES * 4 * HALF], BF16, on, skip)
-
-        def quantize(grouped_ap, width, name, on=None, skip=0):
+        def quantize(grouped, name, on=None):
+            width = grouped.shape[1] // 4
             codes = place(name + "_c", [P, width], U32)
-            scales = place(name + "_s", [P, width], U8, on, skip)
-            nc.vector.quantize_mx(out=codes[:].bitcast(FP8X4), scales=scales[:], in_=grouped_ap)
+            scales = place(name + "_s", [P, width], U8, on)
+            nc.vector.quantize_mx(out=codes[:].bitcast(FP8X4), scales=scales[:], in_=grouped)
             return codes, scales
+
+        def columns(pair, lo, hi):
+            return pair[0][:, lo:hi], pair[1][:, lo:hi]
+
+        def mx(acc, lhs, rhs, step, steps, fmt=FP8X4):
+            nc.tensor.matmul_mx(
+                out=acc,
+                lhsT=lhs[0].bitcast(fmt),
+                lhsT_scale=lhs[1],
+                rhs=rhs[0].bitcast(FP8X4),
+                rhs_scale=rhs[1],
+                start=(step == 0),
+                stop=(step == steps - 1),
+            )
 
         x_raw, dx_raw, tab, wd_raw = {}, {}, {}, {}
         tab[0] = load_table(0)
@@ -125,78 +132,52 @@ def tile_list_operator_tangent_flow_kernel(
         x_raw[1] = load_rows(x, 1, "x1")
         g_pos = load_gains()
         dx_raw[0] = load_rows(dx, 0, "dx0")
-        dx_raw[1] = load_rows(dx, 1, "dx1")
         wd_raw[0] = load_down(0)
+        dx_raw[1] = load_rows(dx, 1, "dx1")
         wd_raw[1] = load_down(1)
         w4w = load_bypass()
         wd_raw[2] = load_down(2)
         wd_raw[3] = load_down(3)
 
-        def list_cols(lo, hi):
-            return offsets[:, lo * (PASS // 16) : hi * (PASS // 16)]
+        xq, dq, hq, wq, tanhs, slopes, turned, wd_grp, h_grp, v = {}, {}, {}, {}, {}, {}, {}, {}, {}, {}
 
-        def gather_scales(lo, hi, name, on=None, skip=0):
-            listed = place(name, [P, (hi - lo) * PASS], U8, on, skip)
-            nc.vector.tensor_copy(out=listed[:], in_=tab_sc[:].indirect(list_cols(lo, hi)))
+        def gather_words(listed, a):
+            nc.vector.tensor_copy(out=listed[:, a * S : (a + 1) * S], in_=tab[a][:].bitcast(U32).indirect(offsets[:]))
+
+        def deal_words(listed, lo, hi, on=None):
+            dealt = place("v%d" % lo, [P, (hi - lo) * S], U32, on)
+            nc.vector.tensor_copy(
+                out=dealt[:].bitcast(I32).rearrange("p (j t c i) -> p j c t i", t=4, c=32, i=4),
+                in_=listed[:, lo * S : hi * S].bitcast(I32).rearrange("p (j c i t) -> p j c t i", t=4, c=32, i=4),
+            )
+            for a in range(lo, hi):
+                v[a] = dealt[:, (a - lo) * S : (a - lo + 1) * S]
+
+        def gather_scales(on=None):
+            listed = place("sc_list", [P, S], U8, on)
+            nc.vector.tensor_copy(out=listed[:], in_=tab_sc[:].indirect(offsets[:]))
             return listed
 
-        def deal_scales(listed, lo, hi, name, on=None, skip=0):
-            dealt = place(name, [P, (hi - lo) * PASS], U8, on, skip)
+        def deal_scales(listed, on=None):
+            dealt = place("v_sc", [P, S], U8, on)
             nc.vector.tensor_copy(
-                out=dealt[:].rearrange("p (j t c i) -> p j c t i", j=hi - lo, t=4, i=16),
-                in_=listed[:].rearrange("p (j c i t) -> p j c t i", j=hi - lo, t=4, i=16),
+                out=dealt[:].rearrange("p (j t c i) -> p j c t i", j=J_PASSES, t=4, i=16),
+                in_=listed[:].rearrange("p (j c i t) -> p j c t i", j=J_PASSES, t=4, i=16),
             )
-            for jp in range(lo, hi):
-                v_sc[jp] = dealt[:, (jp - lo) * PASS : (jp - lo + 1) * PASS]
+            return dealt
 
-        def gather_words(a, lo, hi, name, on=None, skip=0):
-            listed = place(name, [P, (hi - lo) * PASS], U32, on, skip)
-            nc.vector.tensor_copy(out=listed[:], in_=tab[a][:].bitcast(U32).indirect(list_cols(lo, hi)))
-            return listed
+        def slot(a, jp, t):
+            cols = slice(jp * PASS + t * P, jp * PASS + (t + 1) * P)
+            return v[a][:, cols], v_sc[4 * a :, cols]
 
-        def deal_words(listed, a, lo, hi, name, on=None, skip=0):
-            dealt = place(name, [P, (hi - lo) * PASS], U32, on, skip)
-            nc.vector.tensor_copy(
-                out=dealt[:].bitcast(I32).rearrange("p (j t c i) -> p j c t i", j=hi - lo, t=4, i=4),
-                in_=listed[:].bitcast(I32).rearrange("p (j c i t) -> p j c t i", j=hi - lo, t=4, i=4),
-            )
-            for jp in range(lo, hi):
-                v_codes[a, jp] = dealt[:, (jp - lo) * PASS : (jp - lo + 1) * PASS]
-
-        v_sc, v_codes, xq, dq, hq, wq, slopes = {}, {}, {}, {}, {}, {}, {}
-        h_rounded, turned_tiles, wd_grouped, tanhs = {}, {}, {}, {}
-
-        def first_product(acc, jp, t, act, lo, width):
-            for a in range(K_PASSES):
-                cols = slice(a * HALF + lo, a * HALF + lo + width)
-                nc.tensor.matmul_mx(
-                    out=acc,
-                    lhsT=v_codes[a, jp][:, t * P : (t + 1) * P].bitcast(FP8X4),
-                    lhsT_scale=v_sc[jp][4 * a :, t * P : (t + 1) * P],
-                    rhs=act[0][:, cols].bitcast(FP8X4),
-                    rhs_scale=act[1][:, cols],
-                    start=(a == 0),
-                    stop=(a == K_PASSES - 1),
-                )
-
-        def tanh_tile(h, jp, on=None, skip=0):
-            th = place("th%d" % (2 * h + jp), [P, 4, HALF], F32, on, skip, 2048 * (on is None))
-            for u in range(2):
-                a_ps = psum.tile([P, 2, HALF], F32, name="a_ps", tag="p%d" % (4 * h + 2 * jp + u))
-                for e in range(2):
-                    first_product(a_ps[:, e, :], jp, 2 * u + e, xq[h], 0, HALF)
-                nc.scalar.activation(out=th[:, 2 * u : 2 * u + 2, :], in_=a_ps[:], func=ACT.Tanh)
-            tanhs[h, jp] = th
-
-        def slope_tile(h, jp, affine, on=None, skip=0):
-            slope = place("slope%d" % (2 * h + jp), [P, 4, HALF + 4], F32)
-            sq = place("sq%d" % (2 * h + jp), [P, 4, HALF], F32, on, skip, 4096 * (on is None))
-            for u in range(2):
-                pair = slice(2 * u, 2 * u + 2)
-                nc.scalar.activation(out=sq[:, pair, :], in_=tanhs[h, jp][:, pair, :], func=ACT.Square)
+        def tanh_tile(jp, on=None):
+            th = place("th%d" % jp, [P, 4, M], F32, on)
             for t in range(4):
-                affine[t](slope[:, t, 0:HALF], sq[:, t, :], g_neg[:, jp, t : t + 1], g_pos[:, jp, t : t + 1])
-            slopes[h, jp] = slope
+                a_ps = psum.tile([P, M], F32, name="a_ps", tag="p%d" % (4 * jp + t))
+                for a in range(K_PASSES):
+                    mx(a_ps[:], slot(a, jp, t), xq[a], a, K_PASSES)
+                nc.scalar.activation(out=th[:, t, :], in_=a_ps[:], func=ACT.Tanh)
+            tanhs[jp] = th
 
         def affine_scalar(dst, src, scale, bias):
             nc.scalar.activation(out=dst, in_=src, func=ACT.Identity, scale=scale, bias=bias)
@@ -204,181 +185,142 @@ def tile_list_operator_tangent_flow_kernel(
         def affine_vector(dst, src, scale, bias):
             nc.vector.tensor_scalar(out=dst, in0=src, scalar1=scale, scalar2=bias, op0=ALU.mult, op1=ALU.add)
 
-        def affine_pool(dst, src, scale, bias):
-            nc.gpsimd.tensor_scalar(out=dst, in0=src, scalar1=scale, scalar2=bias, op0=ALU.mult, op1=ALU.add)
+        def slope_tile(jp, lo, hi, on=None, slope_on=None, affine=affine_scalar):
+            slope = place("slope%d_%d" % (jp, lo), [P, 4, hi - lo + 4], F32, slope_on)
+            sq = place("sq%d_%d" % (jp, lo), [P, 4, hi - lo], F32, on)
+            for u in range(2):
+                pair = slice(2 * u, 2 * u + 2)
+                nc.scalar.activation(out=sq[:, pair, :], in_=tanhs[jp][:, pair, lo:hi], func=ACT.Square)
+            for t in range(4):
+                affine(slope[:, t, 0 : hi - lo], sq[:, t, :], g_neg[:, jp, t : t + 1], g_pos[:, jp, t : t + 1])
+            for c in range(lo // P, hi // P):
+                slopes[jp, c] = slope[:, :, c * P - lo : (c + 1) * P - lo]
 
-        def tangent(h, jp, c, h_grp, bank):
+        def tangent_tile(jp, lo, hi, on=None):
+            rounded = place("h%d_%d" % (jp, lo), [P, (hi - lo) * 4 * P], BF16, on)
+            for c in range(lo, hi):
+                h_grp[jp, c] = (rounded, lo)
+
+        def tangent(jp, c, bank):
             b_ps = psum.tile([P, 4, P], F32, name="b_ps", tag=bank)
             for t in range(4):
-                first_product(b_ps[:, t, :], jp, t, dq[h], c * P, P)
+                for a in range(K_PASSES):
+                    mx(b_ps[:, t, :], slot(a, jp, t), columns(dq[a], c * P, (c + 1) * P), a, K_PASSES)
+            rounded, lo = h_grp[jp, c]
             nc.vector.tensor_tensor(
-                out=h_grp.rearrange("p (c i t) -> p c t i", i=2, t=4),
+                out=rounded[:, (c - lo) * 4 * P : (c - lo + 1) * 4 * P].rearrange("p (c i t) -> p c t i", i=2, t=4),
                 in0=b_ps[:].rearrange("p t (c i) -> p c t i", i=2),
-                in1=slopes[h, jp][:, :, c * P : (c + 1) * P].rearrange("p t (c i) -> p c t i", i=2),
+                in1=slopes[jp, c].rearrange("p t (c i) -> p c t i", i=2),
                 op=ALU.mult,
             )
 
-        def tangent_tile(h, jp, on=None, skip=0):
-            h_rounded[h, jp] = place("h%d" % (2 * h + jp), [P, 4 * HALF], BF16, on, skip)
-
-        def tangent_chunk(h, jp, c, bank):
-            tangent(h, jp, c, h_rounded[h, jp][:, c * 4 * P : (c + 1) * 4 * P], bank)
-
-        def quantize_tangent(h, jp, lo, hi, on=None, skip=0):
-            name = "hq%d_%d" % (2 * h + jp, lo)
-            codes, scales = quantize(h_rounded[h, jp][:, lo * 4 * P : hi * 4 * P], (hi - lo) * P, name, on, skip)
-            hq[h, jp] = (codes[:], scales[:])
+        def quantize_tangent(jp, lo, hi, on=None):
+            rounded, first = h_grp[jp, lo]
+            pair = quantize(rounded[:, (lo - first) * 4 * P : (hi - first) * 4 * P], "hq%d_%d" % (jp, lo), on)
             for c in range(lo, hi):
-                cols = slice((c - lo) * P, (c - lo + 1) * P)
-                hq[h, jp, c] = (codes[:, cols], scales[:, cols])
+                hq[jp, c] = (pair, lo)
 
-        def down_tile(nt, bank):
-            turned = psum.tile([P, J_PASSES, 2, P], F32, name="turned", tag=bank)
+        def tangent_columns(jp, lo, hi):
+            pair, first = hq[jp, lo]
+            return columns(pair, (lo - first) * P, (hi - first) * P)
+
+        def down_tile(nt, bank, on=None):
+            turned[nt] = psum.tile([P, J_PASSES, 2, P], F32, name="turned", tag=bank)
+            picked = place("picked%d" % nt, [P, S], BF16, on, spare=8192)
+            nc.vector.tensor_copy(out=picked[:], in_=wd_raw[nt][:].indirect(offsets[:]))
+            words = picked[:].bitcast(F32)
             for jp in range(J_PASSES):
-                picked = place("picked%d_%d" % (nt, jp), [P, PASS], BF16, spare=3584, lead=2048 * (nt == 3 and jp == 0))
-                nc.vector.tensor_copy(out=picked[:], in_=wd_raw[nt][:].indirect(list_pass(jp)))
-                words = picked[:].bitcast(F32)
                 for u in range(2):
-                    nc.tensor.transpose(turned[:, jp, u, :], words[:, u : 2 * P : 2], ident[:])
-            turned_tiles[nt] = turned
+                    nc.tensor.transpose(turned[nt][:, jp, u, :], words[:, jp * 2 * P + u : (jp + 1) * 2 * P : 2], ident[:])
 
-        def copy_down(nt, on=None, skip=0):
-            wd_grp = place("wd_grp%d" % nt, [P, J_PASSES * 4 * P], BF16, on, skip)
+        def down_group(lo, hi, on=None):
+            grouped = place("wd_grp%d" % lo, [P, (hi - lo) * S], BF16, on)
+            for nt in range(lo, hi):
+                wd_grp[nt] = (grouped, lo)
+
+        def copy_down(nt):
+            grouped, lo = wd_grp[nt]
             nc.scalar.copy(
-                out=wd_grp[:].bitcast(F32).rearrange("p (j c i u) -> p j c u i", j=J_PASSES, i=2, u=2),
-                in_=turned_tiles[nt][:].rearrange("p j u (c i) -> p j c u i", i=2),
+                out=grouped[:, (nt - lo) * S : (nt - lo + 1) * S].bitcast(F32).rearrange("p (j c i u) -> p j c u i", j=J_PASSES, i=2, u=2),
+                in_=turned[nt][:].rearrange("p j u (c i) -> p j c u i", i=2),
             )
-            wd_grouped[nt] = wd_grp
 
-        def quantize_down(nt, on=None, skip=0):
-            wq[nt] = quantize(wd_grouped[nt][:], J_PASSES * P, "wq%d" % nt, on, skip)
+        def quantize_down(lo, hi, on=None):
+            grouped, first = wd_grp[lo]
+            pair = quantize(grouped[:, (lo - first) * S : (hi - first) * S], "wq%d" % lo, on)
+            for nt in range(lo, hi):
+                wq[nt] = columns(pair, (nt - lo) * 2 * P, (nt - lo + 1) * 2 * P)
 
-        def output_block(h, c, tiles, bank, order, copy_out):
-            acc = psum.tile([P, len(tiles), P], F32, name="acc", tag=bank)
+        def output_block(lo, hi, tiles, bank, order, copy_out):
+            acc = psum.tile([P, len(tiles), (hi - lo) * P], F32, name="acc", tag=bank)
             for step, (kind, a, nt) in enumerate(order):
+                dst = acc[:, nt - tiles[0], :]
                 if kind == "bypass":
-                    cols = slice(a * HALF + c * P, a * HALF + (c + 1) * P)
-                    lhs = w4w[:, a * 2 * N + nt * 2 * P : a * 2 * N + (nt + 1) * 2 * P].bitcast(FP4X4)
-                    lhs_scale = w4_sc[:, a * N + nt * P : a * N + (nt + 1) * P]
-                    rhs, rhs_scale = dq[h][0][:, cols], dq[h][1][:, cols]
+                    lhs = (w4w[:, a * 2 * N + nt * 2 * P : a * 2 * N + (nt + 1) * 2 * P], w4_sc[:, a * N + nt * P : a * N + (nt + 1) * P])
+                    mx(dst, lhs, columns(dq[a], lo * P, hi * P), step, len(order), FP4X4)
                 else:
-                    lhs = wq[nt][0][:, a * P : (a + 1) * P].bitcast(FP8X4)
-                    lhs_scale = wq[nt][1][:, a * P : (a + 1) * P]
-                    rhs, rhs_scale = hq[h, a, c]
-                nc.tensor.matmul_mx(
-                    out=acc[:, nt - tiles[0], :],
-                    lhsT=lhs,
-                    lhsT_scale=lhs_scale,
-                    rhs=rhs.bitcast(FP8X4),
-                    rhs_scale=rhs_scale,
-                    start=(step == 0),
-                    stop=(step == len(order) - 1),
-                )
-            result = keep.tile([P, len(tiles), P], F32, name="result_" + bank)
+                    mx(dst, columns(wq[nt], a * P, (a + 1) * P), tangent_columns(a, lo, hi), step, len(order))
+            result = keep.tile([P, len(tiles), (hi - lo) * P], F32, name="result_" + bank)
             copy_out(out=result[:], in_=acc[:])
-            m0 = h * HALF + c * P
-            rows = out[tiles[0] * P : (tiles[-1] + 1) * P, m0 : m0 + P]
+            rows = out[tiles[0] * P : (tiles[-1] + 1) * P, lo * P : hi * P]
             nc.sync.dma_start(out=rows.rearrange("(nt p) m -> p nt m", p=P), in_=result[:])
-            return result
-
-        def output_half(h, tiles, bank, order, copy_out):
-            acc = psum.tile([P, len(tiles), HALF], F32, name="acc", tag=bank)
-            for step, (kind, a, nt) in enumerate(order):
-                if kind == "bypass":
-                    cols = slice(a * HALF, (a + 1) * HALF)
-                    lhs = w4w[:, a * 2 * N + nt * 2 * P : a * 2 * N + (nt + 1) * 2 * P].bitcast(FP4X4)
-                    lhs_scale = w4_sc[:, a * N + nt * P : a * N + (nt + 1) * P]
-                    rhs, rhs_scale = dq[h][0][:, cols], dq[h][1][:, cols]
-                else:
-                    lhs = wq[nt][0][:, a * P : (a + 1) * P].bitcast(FP8X4)
-                    lhs_scale = wq[nt][1][:, a * P : (a + 1) * P]
-                    rhs, rhs_scale = hq[h, a]
-                nc.tensor.matmul_mx(
-                    out=acc[:, nt - tiles[0], :],
-                    lhsT=lhs,
-                    lhsT_scale=lhs_scale,
-                    rhs=rhs.bitcast(FP8X4),
-                    rhs_scale=rhs_scale,
-                    start=(step == 0),
-                    stop=(step == len(order) - 1),
-                )
-            result = keep.tile([P, len(tiles), HALF], F32, name="result_" + bank)
-            copy_out(out=result[:], in_=acc[:])
-            rows = out[tiles[0] * P : (tiles[-1] + 1) * P, h * HALF : (h + 1) * HALF]
-            nc.sync.dma_start(out=rows.rearrange("(nt p) m -> p nt m", p=P), in_=result[:])
-
-        def weights_last(tiles):
-            passes = [("bypass", a, nt) for a in range(K_PASSES) for nt in tiles]
-            passes.extend(("down", jp, nt) for nt in tiles for jp in range(J_PASSES))
-            return passes
 
         def tangent_last(tiles):
             passes = [("bypass", a, nt) for a in range(K_PASSES) for nt in tiles]
             passes.extend(("down", jp, nt) for jp in range(J_PASSES) for nt in tiles)
             return passes
 
-        on_scalar = (nc.scalar.copy, nc.scalar.copy)
-        on_vector = (nc.vector.tensor_copy, nc.vector.tensor_copy)
         every = [0, 1, 2, 3]
-        list0 = gather_words(0, 0, 2, "list0")
-        list1 = gather_words(1, 0, 2, "list1")
-        deal_words(list0, 0, 0, 2, "v0", "tab1")
-        sc_list = gather_scales(0, 2, "sc_list", "tab1", 4096)
-        deal_words(list1, 1, 0, 2, "v1", "list0")
-        x_grp = [grouped_tile("x_grp%d" % h) for h in range(2)]
+        listed = place("listed", [P, K_PASSES * S], U32)
+        gather_words(listed, 0)
+        gather_words(listed, 1)
+        x_grp = place("x_grp", [P, K_PASSES * 4 * M], BF16)
         for a in range(K_PASSES):
-            for h in range(2):
-                interleave(x_grp[h], x_raw[a], a, h, nc.scalar.copy)
-        deal_scales(sc_list, 0, 2, "v_sc")
-        for h in range(2):
-            xq[h] = quantize(x_grp[h][:], 2 * HALF, "xq%d" % h)
+            interleave(x_grp[:, a * 4 * M : (a + 1) * 4 * M], x_raw[a], 0, M, nc.scalar.copy)
+        sc_list = gather_scales()
+        deal_words(listed, 0, 2, ("x0", 1024))
+        v_sc = deal_scales(sc_list, ("x0", 0))
+        x_pair = quantize(x_grp[:], "xq")
+        for a in range(K_PASSES):
+            xq[a] = columns(x_pair, a * M, (a + 1) * M)
         g_neg = keep.tile([P, J_PASSES, 4], F32, name="g_neg")
         nc.scalar.activation(out=g_neg[:], in_=g_pos[:], func=ACT.Copy, scale=-1.0)
-        dx_grp = [grouped_tile("dx_grp%d" % h) for h in range(2)]
-        interleave(dx_grp[0], dx_raw[0], 0, 0, nc.vector.tensor_copy)
-        interleave(dx_grp[1], dx_raw[0], 0, 1, nc.vector.tensor_copy)
-        tanh_tile(0, 0)
-        tanh_tile(0, 1)
-        tanh_tile(1, 0)
-        tanh_tile(1, 1)
-        interleave(dx_grp[0], dx_raw[1], 1, 0, nc.vector.tensor_copy)
-        interleave(dx_grp[1], dx_raw[1], 1, 1, nc.vector.tensor_copy)
-        dq[0] = quantize(dx_grp[0][:], 2 * HALF, "dq0")
-        dq[1] = quantize(dx_grp[1][:], 2 * HALF, "dq1")
-        slope_tile(0, 0, [affine_scalar] * 4)
+        dx_grp = [place("dx_grp%d" % a, [P, 4 * M], BF16) for a in range(K_PASSES)]
+        interleave(dx_grp[0], dx_raw[0], 0, M, nc.scalar.copy)
+        tanh_tile(0, ("dx0", -64))
         down_tile(0, "p0")
+        dq[0] = quantize(dx_grp[0][:], "dq0", ("wd_raw0", 0))
+        interleave(dx_grp[1], dx_raw[1], 0, M, nc.vector.tensor_copy)
+        dq[1] = quantize(dx_grp[1][:], "dq1")
+        tanh_tile(1, ("dx0", 8192 - 64))
+        down_group(0, 2)
         copy_down(0)
-        slope_tile(0, 1, [affine_scalar] * 4, "picked0_1")
-        down_tile(1, "p3")
+        down_tile(1, "p1")
         copy_down(1)
-        quantize_down(0, "wd_raw1")
-        tangent_tile(0, 0, "wd_raw1", 1024)
-        tangent_chunk(0, 0, 0, "p1")
-        tangent_chunk(0, 0, 1, "p2")
-        slope_tile(1, 0, [affine_scalar] * 4, "picked1_1")
-        down_tile(2, "p0")
+        slope_tile(0, 0, M, ("picked0", 0), ("picked1", 0))
+        down_tile(2, "p2")
+        down_group(2, 4, ("th0", 0))
         copy_down(2)
-        slope_tile(1, 1, [affine_scalar] * 4, "picked2_1")
+        slope_tile(1, 0, HALF, ("picked2", 0))
         down_tile(3, "p3")
         copy_down(3)
-        quantize_tangent(0, 0, 0, 2, "wd_raw3")
-        tangent_tile(0, 1, "wd_raw3", 1024)
-        tangent_chunk(0, 1, 0, "p6")
-        tangent_chunk(0, 1, 1, "p7")
-        quantize_down(1, "wd_raw3", 256)
-        quantize_tangent(0, 1, 0, 2)
-        quantize_down(2, "wd_raw3", 512)
-        tangent_tile(1, 0, "slope1")
-        tangent_chunk(1, 0, 0, "p1")
-        tangent_chunk(1, 0, 1, "p2")
-        quantize_down(3, "wd_grp2")
-        quantize_tangent(1, 0, 0, 2)
-        output_half(0, [0, 1], "p4", tangent_last([0, 1]), nc.scalar.copy)
-        output_half(0, [2, 3], "p5", weights_last([2, 3]), nc.scalar.copy)
-        tangent_tile(1, 1, "slope2")
-        tangent_chunk(1, 1, 0, "p6")
-        tangent_chunk(1, 1, 1, "p7")
-        quantize_tangent(1, 1, 0, 1)
-        quantize_tangent(1, 1, 1, 2)
-        output_block(1, 0, every, "p0", tangent_last(every), nc.scalar.copy)
-        output_block(1, 1, every, "p3", tangent_last(every), nc.vector.tensor_copy)
+        slope_tile(1, HALF, M, ("picked3", 0))
+        tangent_tile(0, 0, 4, ("wd_raw3", 1024))
+        for c in range(4):
+            tangent(0, c, "p%d" % (4 + c))
+        quantize_down(0, 2, ("wd_raw3", 0))
+        quantize_tangent(0, 0, 4)
+        tangent_tile(1, 0, 2, ("wd_grp0", 0))
+        tangent(1, 0, "p4")
+        tangent(1, 1, "p5")
+        quantize_down(2, 4, ("h0_0", 0))
+        quantize_tangent(1, 0, 2)
+        tangent_tile(1, 2, 4, ("wd_grp2", 0))
+        tangent(1, 2, "p6")
+        tangent(1, 3, "p7")
+        quantize_tangent(1, 2, 3)
+        quantize_tangent(1, 3, 4)
+        output_block(0, 2, [0, 1], "p0", tangent_last([0, 1]), nc.scalar.copy)
+        output_block(0, 2, [2, 3], "p1", tangent_last([2, 3]), nc.scalar.copy)
+        output_block(2, 3, every, "p2", tangent_last(every), nc.scalar.copy)
+        output_block(3, 4, every, "p3", tangent_last(every), nc.vector.tensor_copy)

@@ -50,9 +50,9 @@ def tile_list_operator_tangent_flow_kernel(
         nc.sync.dma_start(offsets[:], offs)
 
         tab_sc = place("tab_sc", [P, T], U8, spare=6144)
-        nc.vector.memset(tab_sc[:].bitcast(I32), 0)
+        nc.gpsimd.memset(tab_sc[:].bitcast(I32), 0)
         w4_sc = keep.tile([P, K_PASSES * N], U8, name="w4_sc", align_bytes=64)
-        nc.gpsimd.memset(w4_sc[:].bitcast(I32), 0)
+        nc.vector.memset(w4_sc[:].bitcast(I32), 0)
         ident = keep.tile([P, P], F32, name="ident")
         make_identity(nc, ident[:])
 
@@ -135,8 +135,8 @@ def tile_list_operator_tangent_flow_kernel(
         wd_raw[0] = load_down(0)
         dx_raw[1] = load_rows(dx, 1, "dx1")
         wd_raw[1] = load_down(1)
-        w4w = load_bypass()
         wd_raw[2] = load_down(2)
+        w4w = load_bypass()
         wd_raw[3] = load_down(3)
 
         xq, dq, hq, wq, tanhs, slopes, turned, wd_grp, h_grp, v = {}, {}, {}, {}, {}, {}, {}, {}, {}, {}
@@ -285,13 +285,14 @@ def tile_list_operator_tangent_flow_kernel(
             xq[a] = columns(x_pair, a * M, (a + 1) * M)
         g_neg = keep.tile([P, J_PASSES, 4], F32, name="g_neg")
         nc.scalar.activation(out=g_neg[:], in_=g_pos[:], func=ACT.Copy, scale=-1.0)
-        dx_grp = [place("dx_grp%d" % a, [P, 4 * M], BF16) for a in range(K_PASSES)]
-        interleave(dx_grp[0], dx_raw[0], 0, M, nc.scalar.copy)
+        dx_grp = place("dx_grp", [P, K_PASSES * 4 * M], BF16)
+        interleave(dx_grp[:, 0 : 4 * M], dx_raw[0], 0, M, nc.scalar.copy)
         tanh_tile(0, ("dx0", -64))
         down_tile(0, "p0")
-        dq[0] = quantize(dx_grp[0][:], "dq0", ("wd_raw0", 0))
-        interleave(dx_grp[1], dx_raw[1], 0, M, nc.vector.tensor_copy)
-        dq[1] = quantize(dx_grp[1][:], "dq1")
+        interleave(dx_grp[:, 4 * M : 8 * M], dx_raw[1], 0, M, nc.vector.tensor_copy)
+        dx_pair = quantize(dx_grp[:], "dq")
+        for a in range(K_PASSES):
+            dq[a] = columns(dx_pair, a * M, (a + 1) * M)
         tanh_tile(1, ("dx0", 8192 - 64))
         down_group(0, 2)
         copy_down(0)
@@ -305,22 +306,27 @@ def tile_list_operator_tangent_flow_kernel(
         down_tile(3, "p3")
         copy_down(3)
         slope_tile(1, HALF, M, ("picked3", 0))
-        tangent_tile(0, 0, 4, ("wd_raw3", 1024))
-        for c in range(4):
-            tangent(0, c, "p%d" % (4 + c))
+        tangent_tile(0, 0, 2, ("wd_raw3", 1024))
+        tangent(0, 0, "p4")
+        tangent(0, 1, "p5")
         quantize_down(0, 2, ("wd_raw3", 0))
-        quantize_tangent(0, 0, 4)
-        tangent_tile(1, 0, 2, ("wd_grp0", 0))
-        tangent(1, 0, "p4")
-        tangent(1, 1, "p5")
-        quantize_down(2, 4, ("h0_0", 0))
+        quantize_tangent(0, 0, 2)
+        tangent_tile(1, 0, 2, ("wd_raw3", 3072))
+        tangent(1, 0, "p6")
+        tangent(1, 1, "p7")
+        quantize_down(2, 4, ("wd_raw3", 512))
         quantize_tangent(1, 0, 2)
-        tangent_tile(1, 2, 4, ("wd_grp2", 0))
-        tangent(1, 2, "p6")
-        tangent(1, 3, "p7")
-        quantize_tangent(1, 2, 3)
-        quantize_tangent(1, 3, 4)
         output_block(0, 2, [0, 1], "p0", tangent_last([0, 1]), nc.scalar.copy)
         output_block(0, 2, [2, 3], "p1", tangent_last([2, 3]), nc.scalar.copy)
+        tangent_tile(0, 2, 4, ("wd_grp2", 0))
+        tangent(0, 2, "p4")
+        tangent(0, 3, "p5")
+        tangent_tile(1, 2, 4, ("wd_grp2", 2048))
+        tangent(1, 2, "p6")
+        quantize_tangent(0, 2, 4)
+        quantize_tangent(1, 2, 3)
+        tangent(1, 3, "p7")
+        quantize_tangent(1, 3, 4)
         output_block(2, 3, every, "p2", tangent_last(every), nc.scalar.copy)
-        output_block(3, 4, every, "p3", tangent_last(every), nc.vector.tensor_copy)
+        output_block(3, 4, [0, 1], "p3", tangent_last([0, 1]), nc.scalar.copy)
+        output_block(3, 4, [2, 3], "p4", tangent_last([2, 3]), nc.vector.tensor_copy)

@@ -49,7 +49,7 @@ def tile_list_operator_tangent_flow_kernel(
         offsets = keep.tile([P, S // 16], U16, name="offsets")
         nc.sync.dma_start(offsets[:], offs)
 
-        tab_sc = place("tab_sc", [P, T], U8, spare=6144)
+        tab_sc = place("tab_sc", [P, T], U8)
         nc.gpsimd.memset(tab_sc[:].bitcast(I32), 0)
         w4_sc = keep.tile([P, K_PASSES * N], U8, name="w4_sc", align_bytes=64)
         nc.vector.memset(w4_sc[:].bitcast(I32), 0)
@@ -64,7 +64,7 @@ def tile_list_operator_tangent_flow_kernel(
                 )
 
         def load_rows(src, a, name):
-            raw = place(name, [P, 4, M], F32, spare=8192, lead=64)
+            raw = place(name, [P, 4, M], F32, spare=1024, lead=64)
             nc.sync.dma_start(out=raw[:], in_=src[a * PASS : (a + 1) * PASS, :].rearrange("(p t) m -> p t m", t=4))
             return raw
 
@@ -185,6 +185,9 @@ def tile_list_operator_tangent_flow_kernel(
         def affine_vector(dst, src, scale, bias):
             nc.vector.tensor_scalar(out=dst, in0=src, scalar1=scale, scalar2=bias, op0=ALU.mult, op1=ALU.add)
 
+        def affine_pool(dst, src, scale, bias):
+            nc.gpsimd.tensor_scalar(out=dst, in0=src, scalar1=scale, scalar2=bias, op0=ALU.mult, op1=ALU.add)
+
         def slope_tile(jp, lo, hi, on=None, slope_on=None, affine=affine_scalar):
             slope = place("slope%d_%d" % (jp, lo), [P, 4, hi - lo + 4], F32, slope_on)
             sq = place("sq%d_%d" % (jp, lo), [P, 4, hi - lo], F32, on)
@@ -226,7 +229,7 @@ def tile_list_operator_tangent_flow_kernel(
 
         def down_tile(nt, bank, on=None):
             turned[nt] = psum.tile([P, J_PASSES, 2, P], F32, name="turned", tag=bank)
-            picked = place("picked%d" % nt, [P, S], BF16, on, spare=8192)
+            picked = place("picked%d" % nt, [P, S], BF16, on, spare=2176)
             nc.vector.tensor_copy(out=picked[:], in_=wd_raw[nt][:].indirect(offsets[:]))
             words = picked[:].bitcast(F32)
             for jp in range(J_PASSES):
@@ -285,7 +288,7 @@ def tile_list_operator_tangent_flow_kernel(
             xq[a] = columns(x_pair, a * M, (a + 1) * M)
         g_neg = keep.tile([P, J_PASSES, 4], F32, name="g_neg")
         nc.scalar.activation(out=g_neg[:], in_=g_pos[:], func=ACT.Copy, scale=-1.0)
-        dx_grp = place("dx_grp", [P, K_PASSES * 4 * M], BF16)
+        dx_grp = place("dx_grp", [P, K_PASSES * 4 * M], BF16, spare=64)
         interleave(dx_grp[:, 0 : 4 * M], dx_raw[0], 0, M, nc.scalar.copy)
         tanh_tile(0, ("dx0", -64))
         down_tile(0, "p0")
@@ -293,19 +296,19 @@ def tile_list_operator_tangent_flow_kernel(
         dx_pair = quantize(dx_grp[:], "dq")
         for a in range(K_PASSES):
             dq[a] = columns(dx_pair, a * M, (a + 1) * M)
-        tanh_tile(1, ("dx0", 8192 - 64))
-        down_group(0, 2)
+        slope_tile(0, 0, M, None, ("dx_grp", 0), affine_pool)
+        tanh_tile(1, ("th0", 0))
+        down_group(0, 2, None)
         copy_down(0)
         down_tile(1, "p1")
         copy_down(1)
-        slope_tile(0, 0, M, ("picked0", 0), ("picked1", 0))
+        slope_tile(1, 0, HALF)
         down_tile(2, "p2")
-        down_group(2, 4, ("th0", 0))
+        down_group(2, 4)
         copy_down(2)
-        slope_tile(1, 0, HALF, ("picked2", 0))
         down_tile(3, "p3")
         copy_down(3)
-        slope_tile(1, HALF, M, ("picked3", 0))
+        slope_tile(1, HALF, M, ("picked2", 0), ("picked3", 0))
         tangent_tile(0, 0, 2, ("wd_raw3", 1024))
         tangent(0, 0, "p4")
         tangent(0, 1, "p5")

@@ -47,7 +47,6 @@ def tile_list_operator_tangent_flow_kernel(
             return work.tile(shape, dtype, name=name, align_bytes=64, offset=home[name])
 
         offsets = keep.tile([P, S // 16], U16, name="offsets")
-        nc.sync.dma_start(offsets[:], offs)
 
         tab_sc = place("tab_sc", [P, T], U8)
         nc.gpsimd.memset(tab_sc[:].bitcast(I32), 0)
@@ -63,8 +62,8 @@ def tile_list_operator_tangent_flow_kernel(
                     in_=tab_scales.bitcast(I32)[a, 4 * q : 4 * q + 4, :],
                 )
 
-        def load_rows(src, a, name):
-            raw = place(name, [P, 4, M], F32, spare=1024, lead=64)
+        def load_rows(src, a, name, spare=0, lead=0):
+            raw = place(name, [P, 4, M], F32, spare=spare, lead=lead)
             nc.sync.dma_start(out=raw[:], in_=src[a * PASS : (a + 1) * PASS, :].rearrange("(p t) m -> p t m", t=4))
             return raw
 
@@ -125,15 +124,16 @@ def tile_list_operator_tangent_flow_kernel(
 
         x_raw, dx_raw, tab, wd_raw = {}, {}, {}, {}
         tab[0] = load_table(0)
+        nc.sync.dma_start(offsets[:], offs)
         load_table_scales(0)
         tab[1] = load_table(1)
-        x_raw[0] = load_rows(x, 0, "x0")
+        x_raw[0] = load_rows(x, 0, "x0", spare=1024)
         load_table_scales(1)
         x_raw[1] = load_rows(x, 1, "x1")
-        g_pos = load_gains()
         dx_raw[0] = load_rows(dx, 0, "dx0")
         wd_raw[0] = load_down(0)
-        dx_raw[1] = load_rows(dx, 1, "dx1")
+        dx_raw[1] = load_rows(dx, 1, "dx1", spare=64, lead=4096)
+        g_pos = load_gains()
         wd_raw[1] = load_down(1)
         wd_raw[2] = load_down(2)
         w4w = load_bypass()
@@ -170,14 +170,15 @@ def tile_list_operator_tangent_flow_kernel(
             cols = slice(jp * PASS + t * P, jp * PASS + (t + 1) * P)
             return v[a][:, cols], v_sc[4 * a :, cols]
 
-        def tanh_tile(jp, on=None):
-            th = place("th%d" % jp, [P, 4, M], F32, on)
-            for t in range(4):
+        def tanh_pair(jp, u, on=None):
+            th = place("th%d_%d" % (jp, u), [P, 2, M], F32, on)
+            for e in range(2):
+                t = 2 * u + e
                 a_ps = psum.tile([P, M], F32, name="a_ps", tag="p%d" % (4 * jp + t))
                 for a in range(K_PASSES):
                     mx(a_ps[:], slot(a, jp, t), xq[a], a, K_PASSES)
-                nc.scalar.activation(out=th[:, t, :], in_=a_ps[:], func=ACT.Tanh)
-            tanhs[jp] = th
+                nc.scalar.activation(out=th[:, e, :], in_=a_ps[:], func=ACT.Tanh)
+            tanhs[jp, u] = th
 
         def affine_scalar(dst, src, scale, bias):
             nc.scalar.activation(out=dst, in_=src, func=ACT.Identity, scale=scale, bias=bias)
@@ -193,7 +194,7 @@ def tile_list_operator_tangent_flow_kernel(
             sq = place("sq%d_%d" % (jp, lo), [P, 4, hi - lo], F32, on)
             for u in range(2):
                 pair = slice(2 * u, 2 * u + 2)
-                nc.scalar.activation(out=sq[:, pair, :], in_=tanhs[jp][:, pair, lo:hi], func=ACT.Square)
+                nc.scalar.activation(out=sq[:, pair, :], in_=tanhs[jp, u][:, :, lo:hi], func=ACT.Square)
             for t in range(4):
                 affine(slope[:, t, 0 : hi - lo], sq[:, t, :], g_neg[:, jp, t : t + 1], g_pos[:, jp, t : t + 1])
             for c in range(lo // P, hi // P):
@@ -286,19 +287,22 @@ def tile_list_operator_tangent_flow_kernel(
         x_pair = quantize(x_grp[:], "xq")
         for a in range(K_PASSES):
             xq[a] = columns(x_pair, a * M, (a + 1) * M)
+        dx_grp = place("dx_grp", [P, K_PASSES * 4 * M], BF16, spare=4160, lead=4096)
+        interleave(dx_grp[:, 0 : 4 * M], dx_raw[0], 0, M, nc.scalar.copy)
+        tanh_pair(0, 0, ("dx0", 0))
+        down_tile(0, "p0")
+        interleave(dx_grp[:, 4 * M : 8 * M], dx_raw[1], 0, HALF, nc.vector.tensor_copy)
+        interleave(dx_grp[:, 4 * M : 8 * M], dx_raw[1], HALF, M, nc.scalar.copy)
+        tanh_pair(0, 1, ("dx1", 64))
+        tanh_pair(1, 0, ("dx1", 64 + 4096))
+        tanh_pair(1, 1, ("dx1", 64 - 4096))
         g_neg = keep.tile([P, J_PASSES, 4], F32, name="g_neg")
         nc.scalar.activation(out=g_neg[:], in_=g_pos[:], func=ACT.Copy, scale=-1.0)
-        dx_grp = place("dx_grp", [P, K_PASSES * 4 * M], BF16, spare=64)
-        interleave(dx_grp[:, 0 : 4 * M], dx_raw[0], 0, M, nc.scalar.copy)
-        tanh_tile(0, ("dx0", -64))
-        down_tile(0, "p0")
-        interleave(dx_grp[:, 4 * M : 8 * M], dx_raw[1], 0, M, nc.vector.tensor_copy)
         dx_pair = quantize(dx_grp[:], "dq")
         for a in range(K_PASSES):
             dq[a] = columns(dx_pair, a * M, (a + 1) * M)
-        slope_tile(0, 0, M, None, ("dx_grp", 0), affine_pool)
-        tanh_tile(1, ("th0", 0))
-        down_group(0, 2, None)
+        slope_tile(0, 0, M, ("dx_grp", -4096), ("dx_grp", 4096), affine_pool)
+        down_group(0, 2, ("th0_0", 0))
         copy_down(0)
         down_tile(1, "p1")
         copy_down(1)
@@ -331,5 +335,5 @@ def tile_list_operator_tangent_flow_kernel(
         tangent(1, 3, "p7")
         quantize_tangent(1, 3, 4)
         output_block(2, 3, every, "p2", tangent_last(every), nc.scalar.copy)
-        output_block(3, 4, [0, 1], "p3", tangent_last([0, 1]), nc.scalar.copy)
+        output_block(3, 4, [0, 1], "p5", tangent_last([0, 1]), nc.scalar.copy)
         output_block(3, 4, [2, 3], "p4", tangent_last([2, 3]), nc.vector.tensor_copy)

@@ -132,7 +132,7 @@ def tile_list_operator_tangent_flow_kernel(
         x_raw[1] = load_rows(x, 1, "x1")
         dx_raw[0] = load_rows(dx, 0, "dx0")
         wd_raw[0] = load_down(0)
-        dx_raw[1] = load_rows(dx, 1, "dx1", spare=64, lead=4096)
+        dx_raw[1] = load_rows(dx, 1, "dx1")
         g_pos = load_gains()
         wd_raw[1] = load_down(1)
         wd_raw[2] = load_down(2)
@@ -293,20 +293,20 @@ def tile_list_operator_tangent_flow_kernel(
         down_tile(0, "p0")
         interleave(dx_grp[:, 4 * M : 8 * M], dx_raw[1], 0, HALF, nc.vector.tensor_copy)
         interleave(dx_grp[:, 4 * M : 8 * M], dx_raw[1], HALF, M, nc.scalar.copy)
-        tanh_pair(0, 1, ("dx1", 64))
-        tanh_pair(1, 0, ("dx1", 64 + 4096))
-        tanh_pair(1, 1, ("dx1", 64 - 4096))
+        tanh_pair(0, 1, ("dx1", 0))
+        tanh_pair(1, 0, ("dx1", 4096))
         g_neg = keep.tile([P, J_PASSES, 4], F32, name="g_neg")
         nc.scalar.activation(out=g_neg[:], in_=g_pos[:], func=ACT.Copy, scale=-1.0)
         dx_pair = quantize(dx_grp[:], "dq")
         for a in range(K_PASSES):
             dq[a] = columns(dx_pair, a * M, (a + 1) * M)
         slope_tile(0, 0, M, ("dx_grp", -4096), ("dx_grp", 4096), affine_pool)
+        tanh_pair(1, 1, ("th0_1", 0))
+        slope_tile(1, 0, HALF, None, None, affine_pool)
         down_group(0, 2, ("th0_0", 0))
         copy_down(0)
         down_tile(1, "p1")
         copy_down(1)
-        slope_tile(1, 0, HALF)
         down_tile(2, "p2")
         down_group(2, 4)
         copy_down(2)

@@ -302,15 +302,15 @@ def tile_list_operator_tangent_flow_kernel(
             dq[a] = columns(dx_pair, a * M, (a + 1) * M)
         slope_tile(0, 0, M, ("dx_grp", -4096), ("dx_grp", 4096), affine_pool)
         tanh_pair(1, 1, ("th0_1", 0))
-        slope_tile(1, 0, HALF, None, None, affine_pool)
         down_group(0, 2, ("th0_0", 0))
         copy_down(0)
         down_tile(1, "p1")
         copy_down(1)
-        down_tile(2, "p2")
+        slope_tile(1, 0, HALF)
+        down_tile(2, "p6")
         down_group(2, 4)
         copy_down(2)
-        down_tile(3, "p3")
+        down_tile(3, "p7")
         copy_down(3)
         slope_tile(1, HALF, M, ("picked2", 0), ("picked3", 0))
         tangent_tile(0, 0, 2, ("wd_raw3", 1024))
@@ -319,8 +319,8 @@ def tile_list_operator_tangent_flow_kernel(
         quantize_down(0, 2, ("wd_raw3", 0))
         quantize_tangent(0, 0, 2)
         tangent_tile(1, 0, 2, ("wd_raw3", 3072))
-        tangent(1, 0, "p6")
-        tangent(1, 1, "p7")
+        tangent(1, 0, "p2")
+        tangent(1, 1, "p3")
         quantize_down(2, 4, ("wd_raw3", 512))
         quantize_tangent(1, 0, 2)
         output_block(0, 2, [0, 1], "p0", tangent_last([0, 1]), nc.scalar.copy)
@@ -329,11 +329,11 @@ def tile_list_operator_tangent_flow_kernel(
         tangent(0, 2, "p4")
         tangent(0, 3, "p5")
         tangent_tile(1, 2, 4, ("wd_grp2", 2048))
-        tangent(1, 2, "p6")
+        tangent(1, 2, "p2")
         quantize_tangent(0, 2, 4)
         quantize_tangent(1, 2, 3)
-        tangent(1, 3, "p7")
+        tangent(1, 3, "p3")
         quantize_tangent(1, 3, 4)
-        output_block(2, 3, every, "p2", tangent_last(every), nc.scalar.copy)
+        output_block(2, 3, every, "p6", tangent_last(every), nc.scalar.copy)
         output_block(3, 4, [0, 1], "p5", tangent_last([0, 1]), nc.scalar.copy)
         output_block(3, 4, [2, 3], "p4", tangent_last([2, 3]), nc.vector.tensor_copy)

@@ -24,8 +24,9 @@ P = 128
 PASS = 512
 K_PASSES = K // PASS
 J_PASSES = S // PASS
-N_TILES = N // P
 HALF = M // 2
+FIRST_SPLIT = 192
+DX_SPLIT = 320
 
 
 def tile_list_operator_tangent_flow_kernel(
@@ -38,9 +39,9 @@ def tile_list_operator_tangent_flow_kernel(
         work = ctx.enter_context(tc.tile_pool(name="work", bufs=1))
         home = {"end": 0}
 
-        def place(name, shape, dtype, on=None, spare=0, lead=0):
+        def place(name, shape, dtype, on=None, spare=0):
             if on is None:
-                home[name] = home["end"] + lead
+                home[name] = home["end"]
                 home["end"] = home[name] + math.prod(shape[1:]) * WIDTH[dtype] + spare
             else:
                 home[name] = home[on[0]] + on[1]
@@ -51,19 +52,19 @@ def tile_list_operator_tangent_flow_kernel(
         tab_sc = place("tab_sc", [P, T], U8)
         nc.gpsimd.memset(tab_sc[:].bitcast(I32), 0)
         w4_sc = keep.tile([P, K_PASSES * N], U8, name="w4_sc", align_bytes=64)
-        nc.vector.memset(w4_sc[:].bitcast(I32), 0)
+        nc.gpsimd.memset(w4_sc[:].bitcast(I32), 0)
         ident = keep.tile([P, P], F32, name="ident")
         make_identity(nc, ident[:])
 
-        def load_table_scales(a):
-            for q in range(4):
+        def load_table_scales():
+            for q in (0, 2, 1, 3):
                 nc.sync.dma_start(
-                    out=tab_sc[32 * q + 4 * a : 32 * q + 4 * a + 4, :].bitcast(I32),
-                    in_=tab_scales.bitcast(I32)[a, 4 * q : 4 * q + 4, :],
+                    out=tab_sc[32 * q : 32 * q + 4 * K_PASSES, :].bitcast(I32),
+                    in_=tab_scales.bitcast(I32)[:, 4 * q : 4 * q + 4, :],
                 )
 
-        def load_rows(src, a, name, spare=0, lead=0):
-            raw = place(name, [P, 4, M], F32, spare=spare, lead=lead)
+        def load_rows(src, a, name, spare=0):
+            raw = place(name, [P, 4, M], F32, spare=spare)
             nc.sync.dma_start(out=raw[:], in_=src[a * PASS : (a + 1) * PASS, :].rearrange("(p t) m -> p t m", t=4))
             return raw
 
@@ -88,7 +89,7 @@ def tile_list_operator_tangent_flow_kernel(
                 out=words[:].bitcast(I32).rearrange("p (a c) -> p a c", a=K_PASSES),
                 in_=w4_words.bitcast(I32).rearrange("a p c -> p a c"),
             )
-            for q in range(4):
+            for q in (0, 2, 1, 3):
                 nc.sync.dma_start(
                     out=w4_sc[32 * q : 32 * q + 4, :].bitcast(I32).rearrange("r (a c) -> r a c", a=K_PASSES),
                     in_=w4_scales.bitcast(I32)[:, 4 * q : 4 * q + 4, :].rearrange("a r c -> r a c"),
@@ -103,63 +104,62 @@ def tile_list_operator_tangent_flow_kernel(
 
         def quantize(grouped, name, on=None):
             width = grouped.shape[1] // 4
-            codes = place(name + "_c", [P, width], U32)
-            scales = place(name + "_s", [P, width], U8, on)
+            codes = place(name + "_c", [P, width], U32, on)
+            scales = place(name + "_s", [P, width], U8)
             nc.vector.quantize_mx(out=codes[:].bitcast(FP8X4), scales=scales[:], in_=grouped)
             return codes, scales
 
         def columns(pair, lo, hi):
             return pair[0][:, lo:hi], pair[1][:, lo:hi]
 
-        def mx(acc, lhs, rhs, step, steps, fmt=FP8X4):
+        def mx(acc, lhs, rhs, first, last, fmt=FP8X4):
             nc.tensor.matmul_mx(
                 out=acc,
                 lhsT=lhs[0].bitcast(fmt),
                 lhsT_scale=lhs[1],
                 rhs=rhs[0].bitcast(FP8X4),
                 rhs_scale=rhs[1],
-                start=(step == 0),
-                stop=(step == steps - 1),
+                start=first,
+                stop=last,
             )
 
         x_raw, dx_raw, tab, wd_raw = {}, {}, {}, {}
         tab[0] = load_table(0)
         nc.sync.dma_start(offsets[:], offs)
-        load_table_scales(0)
+        load_table_scales()
+        x_raw[0] = load_rows(x, 0, "x0")
         tab[1] = load_table(1)
-        x_raw[0] = load_rows(x, 0, "x0", spare=1024)
-        load_table_scales(1)
         x_raw[1] = load_rows(x, 1, "x1")
-        dx_raw[0] = load_rows(dx, 0, "dx0")
         wd_raw[0] = load_down(0)
-        dx_raw[1] = load_rows(dx, 1, "dx1")
         g_pos = load_gains()
         wd_raw[1] = load_down(1)
+        dx_raw[0] = load_rows(dx, 0, "dx0", spare=4096)
+        dx_raw[1] = load_rows(dx, 1, "dx1", spare=7168)
         wd_raw[2] = load_down(2)
         w4w = load_bypass()
         wd_raw[3] = load_down(3)
 
-        xq, dq, hq, wq, tanhs, slopes, turned, wd_grp, h_grp, v = {}, {}, {}, {}, {}, {}, {}, {}, {}, {}
+        xq, dq, hq, wq, th, slopes, a_ps, v, h, sums, projected = {}, {}, {}, {}, {}, {}, {}, {}, {}, {}, {}
 
-        def gather_words(listed, a):
-            nc.vector.tensor_copy(out=listed[:, a * S : (a + 1) * S], in_=tab[a][:].bitcast(U32).indirect(offsets[:]))
+        def gather_words(a, on=None):
+            listed = place("listed%d" % a, [P, S], U32, on)
+            nc.vector.tensor_copy(out=listed[:], in_=tab[a][:].bitcast(U32).indirect(offsets[:]))
+            return listed
 
-        def deal_words(listed, lo, hi, on=None):
-            dealt = place("v%d" % lo, [P, (hi - lo) * S], U32, on)
+        def deal_words(listed, a):
+            v[a] = place("v%d" % a, [P, S], U32)
             nc.vector.tensor_copy(
-                out=dealt[:].bitcast(I32).rearrange("p (j t c i) -> p j c t i", t=4, c=32, i=4),
-                in_=listed[:, lo * S : hi * S].bitcast(I32).rearrange("p (j c i t) -> p j c t i", t=4, c=32, i=4),
+                out=v[a][:].bitcast(I32).rearrange("p (j t c i) -> p j c t i", t=4, c=32, i=4),
+                in_=listed[:].bitcast(I32).rearrange("p (j c i t) -> p j c t i", t=4, c=32, i=4),
             )
-            for a in range(lo, hi):
-                v[a] = dealt[:, (a - lo) * S : (a - lo + 1) * S]
 
-        def gather_scales(on=None):
-            listed = place("sc_list", [P, S], U8, on)
+        def gather_scales():
+            listed = place("sc_list", [P, S], U8)
             nc.vector.tensor_copy(out=listed[:], in_=tab_sc[:].indirect(offsets[:]))
             return listed
 
-        def deal_scales(listed, on=None):
-            dealt = place("v_sc", [P, S], U8, on)
+        def deal_scales(listed):
+            dealt = place("v_sc", [P, S], U8)
             nc.vector.tensor_copy(
                 out=dealt[:].rearrange("p (j t c i) -> p j c t i", j=J_PASSES, t=4, i=16),
                 in_=listed[:].rearrange("p (j c i t) -> p j c t i", j=J_PASSES, t=4, i=16),
@@ -170,57 +170,60 @@ def tile_list_operator_tangent_flow_kernel(
             cols = slice(jp * PASS + t * P, jp * PASS + (t + 1) * P)
             return v[a][:, cols], v_sc[4 * a :, cols]
 
-        def tanh_pair(jp, u, on=None):
-            th = place("th%d_%d" % (jp, u), [P, 2, M], F32, on)
-            for e in range(2):
-                t = 2 * u + e
-                a_ps = psum.tile([P, M], F32, name="a_ps", tag="p%d" % (4 * jp + t))
-                for a in range(K_PASSES):
-                    mx(a_ps[:], slot(a, jp, t), xq[a], a, K_PASSES)
-                nc.scalar.activation(out=th[:, e, :], in_=a_ps[:], func=ACT.Tanh)
-            tanhs[jp, u] = th
+        def state_pass(a, jp, t):
+            if a == 0:
+                a_ps[jp, t] = psum.tile([P, M], F32, name="a_ps", tag="p%d" % (4 * jp + t))
+            mx(a_ps[jp, t][:], slot(a, jp, t), xq[a], a == 0, a == K_PASSES - 1)
+
+        def tanh_pass(jp, on=None):
+            th[jp] = place("th%d" % jp, [P, 4, M], F32, on)
+            for t in range(4):
+                nc.scalar.activation(out=th[jp][:, t, :], in_=a_ps[jp, t][:], func=ACT.Tanh)
+
+        def square(name, src, on=None):
+            squares = place(name, list(src.shape), F32, on)
+            nc.scalar.activation(out=squares[:], in_=src, func=ACT.Square)
+            return squares
 
         def affine_scalar(dst, src, scale, bias):
             nc.scalar.activation(out=dst, in_=src, func=ACT.Identity, scale=scale, bias=bias)
 
-        def affine_vector(dst, src, scale, bias):
-            nc.vector.tensor_scalar(out=dst, in0=src, scalar1=scale, scalar2=bias, op0=ALU.mult, op1=ALU.add)
-
         def affine_pool(dst, src, scale, bias):
             nc.gpsimd.tensor_scalar(out=dst, in0=src, scalar1=scale, scalar2=bias, op0=ALU.mult, op1=ALU.add)
 
-        def slope_tile(jp, lo, hi, on=None, slope_on=None, affine=affine_scalar):
-            slope = place("slope%d_%d" % (jp, lo), [P, 4, hi - lo + 4], F32, slope_on)
-            sq = place("sq%d_%d" % (jp, lo), [P, 4, hi - lo], F32, on)
-            for u in range(2):
-                pair = slice(2 * u, 2 * u + 2)
-                nc.scalar.activation(out=sq[:, pair, :], in_=tanhs[jp, u][:, :, lo:hi], func=ACT.Square)
-            for t in range(4):
-                affine(slope[:, t, 0 : hi - lo], sq[:, t, :], g_neg[:, jp, t : t + 1], g_pos[:, jp, t : t + 1])
-            for c in range(lo // P, hi // P):
-                slopes[jp, c] = slope[:, :, c * P - lo : (c + 1) * P - lo]
-
-        def tangent_tile(jp, lo, hi, on=None):
-            rounded = place("h%d_%d" % (jp, lo), [P, (hi - lo) * 4 * P], BF16, on)
+        def slope_tile(jp, lo, hi, on=None):
+            slope = place("slope%d_%d" % (jp, lo), [P, 4, (hi - lo) * P], F32, on)
             for c in range(lo, hi):
-                h_grp[jp, c] = (rounded, lo)
+                slopes[jp, c] = slope[:, :, (c - lo) * P : (c - lo + 1) * P]
+            return slope
 
-        def tangent(jp, c, bank):
+        def slope_rows(slope, jp, first, squares, affine):
+            for e in range(squares.shape[1]):
+                t = first + e
+                affine(slope[:, t, :], squares[:, e, :], g_neg[:, jp, t : t + 1], g_pos[:, jp, t : t + 1])
+
+        def project(jp, c, bank, passes=(0, 1)):
             b_ps = psum.tile([P, 4, P], F32, name="b_ps", tag=bank)
+            projected[jp, c] = b_ps
+            for a in passes:
+                project_pass(jp, c, a)
+
+        def project_pass(jp, c, a):
             for t in range(4):
-                for a in range(K_PASSES):
-                    mx(b_ps[:, t, :], slot(a, jp, t), columns(dq[a], c * P, (c + 1) * P), a, K_PASSES)
-            rounded, lo = h_grp[jp, c]
+                first, last = a == 0 and t == 0, a == K_PASSES - 1 and t == 3
+                mx(projected[jp, c][:, t, :], slot(a, jp, t), columns(dq[a], c * P, (c + 1) * P), first, last)
+
+        def tangent(jp, c):
+            b_ps = projected[jp, c]
             nc.vector.tensor_tensor(
-                out=rounded[:, (c - lo) * 4 * P : (c - lo + 1) * 4 * P].rearrange("p (c i t) -> p c t i", i=2, t=4),
+                out=h[jp, c // 2][:, (c % 2) * 4 * P : (c % 2 + 1) * 4 * P].rearrange("p (c i t) -> p c t i", i=2, t=4),
                 in0=b_ps[:].rearrange("p t (c i) -> p c t i", i=2),
                 in1=slopes[jp, c].rearrange("p t (c i) -> p c t i", i=2),
                 op=ALU.mult,
             )
 
-        def quantize_tangent(jp, lo, hi, on=None):
-            rounded, first = h_grp[jp, lo]
-            pair = quantize(rounded[:, (lo - first) * 4 * P : (hi - first) * 4 * P], "hq%d_%d" % (jp, lo), on)
+        def quantize_tangent(jp, lo, hi):
+            pair = quantize(h[jp, lo // 2][:, (lo % 2) * 4 * P : (lo % 2 + hi - lo) * 4 * P], "hq%d_%d" % (jp, lo))
             for c in range(lo, hi):
                 hq[jp, c] = (pair, lo)
 
@@ -229,111 +232,142 @@ def tile_list_operator_tangent_flow_kernel(
             return columns(pair, (lo - first) * P, (hi - first) * P)
 
         def down_tile(nt, bank, on=None):
-            turned[nt] = psum.tile([P, J_PASSES, 2, P], F32, name="turned", tag=bank)
-            picked = place("picked%d" % nt, [P, S], BF16, on, spare=2176)
+            turned = psum.tile([P, J_PASSES, 2, P], F32, name="turned", tag=bank)
+            picked = place("picked%d" % nt, [P, S], BF16, on, spare=2048 * (nt == 3))
             nc.vector.tensor_copy(out=picked[:], in_=wd_raw[nt][:].indirect(offsets[:]))
             words = picked[:].bitcast(F32)
             for jp in range(J_PASSES):
                 for u in range(2):
-                    nc.tensor.transpose(turned[nt][:, jp, u, :], words[:, jp * 2 * P + u : (jp + 1) * 2 * P : 2], ident[:])
+                    nc.tensor.transpose(turned[:, jp, u, :], words[:, jp * 2 * P + u : (jp + 1) * 2 * P : 2], ident[:])
+            return turned
 
-        def down_group(lo, hi, on=None):
-            grouped = place("wd_grp%d" % lo, [P, (hi - lo) * S], BF16, on)
-            for nt in range(lo, hi):
-                wd_grp[nt] = (grouped, lo)
-
-        def copy_down(nt):
-            grouped, lo = wd_grp[nt]
+        def copy_down(turned, nt, on=None):
+            grouped = place("wd_grp%d" % nt, [P, S], BF16, on)
             nc.scalar.copy(
-                out=grouped[:, (nt - lo) * S : (nt - lo + 1) * S].bitcast(F32).rearrange("p (j c i u) -> p j c u i", j=J_PASSES, i=2, u=2),
-                in_=turned[nt][:].rearrange("p j u (c i) -> p j c u i", i=2),
+                out=grouped[:].bitcast(F32).rearrange("p (j c i u) -> p j c u i", j=J_PASSES, i=2, u=2),
+                in_=turned[:].rearrange("p j u (c i) -> p j c u i", i=2),
             )
+            return grouped
 
-        def quantize_down(lo, hi, on=None):
-            grouped, first = wd_grp[lo]
-            pair = quantize(grouped[:, (lo - first) * S : (hi - first) * S], "wq%d" % lo, on)
-            for nt in range(lo, hi):
-                wq[nt] = columns(pair, (nt - lo) * 2 * P, (nt - lo + 1) * 2 * P)
+        def quantize_down(grouped, nt, on=None):
+            pair = quantize(grouped[:], "wq%d" % nt, on)
+            for jp in range(J_PASSES):
+                wq[nt, jp] = columns(pair, jp * P, (jp + 1) * P)
 
-        def output_block(lo, hi, tiles, bank, order, copy_out):
+        def open_sum(bank, lo, hi, tiles):
             acc = psum.tile([P, len(tiles), (hi - lo) * P], F32, name="acc", tag=bank)
-            for step, (kind, a, nt) in enumerate(order):
-                dst = acc[:, nt - tiles[0], :]
-                if kind == "bypass":
+            sums[bank] = (acc, lo, hi, tiles)
+            for a in range(K_PASSES):
+                for nt in tiles:
                     lhs = (w4w[:, a * 2 * N + nt * 2 * P : a * 2 * N + (nt + 1) * 2 * P], w4_sc[:, a * N + nt * P : a * N + (nt + 1) * P])
-                    mx(dst, lhs, columns(dq[a], lo * P, hi * P), step, len(order), FP4X4)
-                else:
-                    mx(dst, columns(wq[nt], a * P, (a + 1) * P), tangent_columns(a, lo, hi), step, len(order))
-            result = keep.tile([P, len(tiles), (hi - lo) * P], F32, name="result_" + bank)
+                    mx(acc[:, nt - tiles[0], :], lhs, columns(dq[a], lo * P, hi * P), a == 0 and nt == tiles[0], False, FP4X4)
+
+        def add_down(bank, jp, some):
+            acc, lo, hi, tiles = sums[bank]
+            for nt in some:
+                mx(acc[:, nt - tiles[0], :], wq[nt, jp], tangent_columns(jp, lo, hi), False, jp == J_PASSES - 1 and nt == tiles[-1])
+
+        def store(bank, copy_out):
+            acc, lo, hi, tiles = sums[bank]
+            result = place("result_" + bank, [P, len(tiles), (hi - lo) * P], F32)
             copy_out(out=result[:], in_=acc[:])
             rows = out[tiles[0] * P : (tiles[-1] + 1) * P, lo * P : hi * P]
             nc.sync.dma_start(out=rows.rearrange("(nt p) m -> p nt m", p=P), in_=result[:])
 
-        def tangent_last(tiles):
-            passes = [("bypass", a, nt) for a in range(K_PASSES) for nt in tiles]
-            passes.extend(("down", jp, nt) for jp in range(J_PASSES) for nt in tiles)
-            return passes
-
-        every = [0, 1, 2, 3]
-        listed = place("listed", [P, K_PASSES * S], U32)
-        gather_words(listed, 0)
-        gather_words(listed, 1)
-        x_grp = place("x_grp", [P, K_PASSES * 4 * M], BF16)
-        for a in range(K_PASSES):
-            interleave(x_grp[:, a * 4 * M : (a + 1) * 4 * M], x_raw[a], 0, M, nc.scalar.copy)
-        sc_list = gather_scales()
-        deal_words(listed, 0, 2, ("x0", 1024))
-        v_sc = deal_scales(sc_list, ("x0", 0))
-        x_pair = quantize(x_grp[:], "xq")
-        for a in range(K_PASSES):
-            xq[a] = columns(x_pair, a * M, (a + 1) * M)
-        dx_grp = place("dx_grp", [P, K_PASSES * 4 * M], BF16, spare=4160, lead=4096)
-        interleave(dx_grp[:, 0 : 4 * M], dx_raw[0], 0, M, nc.scalar.copy)
-        tanh_pair(0, 0, ("dx0", 0))
-        down_tile(0, "p0")
-        interleave(dx_grp[:, 4 * M : 8 * M], dx_raw[1], 0, HALF, nc.vector.tensor_copy)
-        interleave(dx_grp[:, 4 * M : 8 * M], dx_raw[1], HALF, M, nc.scalar.copy)
-        tanh_pair(0, 1, ("dx1", 0))
-        tanh_pair(1, 0, ("dx1", 4096))
+        slots = [(jp, t) for jp in range(J_PASSES) for t in range(4)]
+        x_grp = place("x_grp", [P, K_PASSES, 4 * M], BF16)
         g_neg = keep.tile([P, J_PASSES, 4], F32, name="g_neg")
+
+        listed = gather_words(0)
+        sc_list = gather_scales()
+        deal_words(listed, 0)
+        v_sc = deal_scales(sc_list)
+        interleave(x_grp[:, 0, :], x_raw[0], 0, M, nc.scalar.copy)
+        xq[0] = quantize(x_grp[:, 0, :], "xq0")
+        for jp, t in slots:
+            state_pass(0, jp, t)
+        listed = gather_words(1, ("x0", 0))
+        deal_words(listed, 1)
+        interleave(x_grp[:, 1, :], x_raw[1], 0, M, nc.scalar.copy)
+        xq[1] = quantize(x_grp[:, 1, :], "xq1")
+        for jp, t in slots:
+            state_pass(1, jp, t)
+        tanh_pass(0)
         nc.scalar.activation(out=g_neg[:], in_=g_pos[:], func=ACT.Copy, scale=-1.0)
-        dx_pair = quantize(dx_grp[:], "dq")
-        for a in range(K_PASSES):
-            dq[a] = columns(dx_pair, a * M, (a + 1) * M)
-        slope_tile(0, 0, M, ("dx_grp", -4096), ("dx_grp", 4096), affine_pool)
-        tanh_pair(1, 1, ("th0_1", 0))
-        down_group(0, 2, ("th0_0", 0))
-        copy_down(0)
-        down_tile(1, "p1")
-        copy_down(1)
-        slope_tile(1, 0, HALF)
-        down_tile(2, "p6")
-        down_group(2, 4)
-        copy_down(2)
-        down_tile(3, "p7")
-        copy_down(3)
-        slope_tile(1, HALF, M, ("picked2", 0), ("picked3", 0))
-        tangent_tile(0, 0, 2, ("wd_raw3", 1024))
-        tangent(0, 0, "p4")
-        tangent(0, 1, "p5")
-        quantize_down(0, 2, ("wd_raw3", 0))
+        low = square("sq0_low", th[0][:, 0:2, :])
+        turned = {0: down_tile(0, "p0", ("x1", 0))}
+        turned[1] = down_tile(1, "p1")
+        dx_grp = place("dx_grp0", [P, 4 * M], BF16)
+        interleave(dx_grp, dx_raw[0], 0, FIRST_SPLIT, nc.vector.tensor_copy)
+        interleave(dx_grp, dx_raw[0], FIRST_SPLIT, M, nc.scalar.copy)
+        grouped = {0: copy_down(turned[0], 0, ("dx0", 0))}
+        dq[0] = quantize(dx_grp[:], "dq0")
+        project(0, 0, "p2", [0])
+        project(0, 1, "p3", [0])
+        project(1, 0, "p0", [0])
+        dx_grp = place("dx_grp1", [P, 4 * M], BF16, ("dx0", 4096))
+        interleave(dx_grp, dx_raw[1], 0, DX_SPLIT, nc.vector.tensor_copy)
+        interleave(dx_grp, dx_raw[1], DX_SPLIT, M, nc.scalar.copy)
+        quantize_down(grouped[0], 0, ("dx1", 0))
+        dq[1] = quantize(dx_grp[:], "dq1")
+        grouped[1] = copy_down(turned[1], 1, ("dx1", 1024))
+        quantize_down(grouped[1], 1)
+        high = square("sq0_high", th[0][:, 2:4, :], ("dx1", 3072))
+        tanh_pass(1, ("dx1", 7168))
+        slope = slope_tile(0, 0, 4, ("dx_grp1", 0))
+        slope_rows(slope, 0, 0, low, affine_pool)
+        slope_rows(slope, 0, 2, high, affine_pool)
+        project_pass(0, 0, 1)
+        project_pass(0, 1, 1)
+        project_pass(1, 0, 1)
+        project(1, 1, "p1")
+        project(0, 2, "p4")
+        project(0, 3, "p5")
+        turned[2] = down_tile(2, "p7")
+        slope_rows(slope_tile(1, 0, 2), 1, 0, square("sq1_0", th[1][:, :, 0:HALF]), affine_pool)
+        grouped[2] = copy_down(turned[2], 2)
+        late_squares = square("sq1_1", th[1][:, :, HALF:M])
+        open_sum("p6", 0, 2, [0, 1])
+        turned[3] = down_tile(3, "p7")
+        grouped[3] = copy_down(turned[3], 3)
+        slope_rows(slope_tile(1, 2, 4, ("picked3", 0)), 1, 0, late_squares, affine_scalar)
+        h[0, 0] = place("h0_0", [P, 4 * HALF], BF16, ("wd_raw3", 0))
+        h[1, 0] = place("h1_0", [P, 4 * HALF], BF16, ("wd_raw3", 2048))
+        tangent(0, 0)
+        open_sum("p2", 0, 2, [2, 3])
+        tangent(0, 1)
+        project(1, 2, "p3")
+        quantize_down(grouped[2], 2, ("wd_raw3", 4096))
         quantize_tangent(0, 0, 2)
-        tangent_tile(1, 0, 2, ("wd_raw3", 3072))
-        tangent(1, 0, "p2")
-        tangent(1, 1, "p3")
-        quantize_down(2, 4, ("wd_raw3", 512))
+        add_down("p6", 0, [0, 1])
+        open_sum("p7", 3, 4, [0, 1])
+        tangent(1, 0)
+        project(1, 3, "p0")
+        tangent(1, 1)
+        open_sum("p1", 2, 3, [0, 1, 2, 3])
+        quantize_down(grouped[3], 3, ("sq1_0", 0))
         quantize_tangent(1, 0, 2)
-        output_block(0, 2, [0, 1], "p0", tangent_last([0, 1]), nc.scalar.copy)
-        output_block(0, 2, [2, 3], "p1", tangent_last([2, 3]), nc.scalar.copy)
-        tangent_tile(0, 2, 4, ("wd_grp2", 0))
-        tangent(0, 2, "p4")
-        tangent(0, 3, "p5")
-        tangent_tile(1, 2, 4, ("wd_grp2", 2048))
-        tangent(1, 2, "p2")
+        add_down("p6", 1, [0, 1])
+        store("p6", nc.scalar.copy)
+        add_down("p2", 0, [2, 3])
+        add_down("p2", 1, [2, 3])
+        store("p2", nc.scalar.copy)
+        h[0, 1] = place("h0_1", [P, 4 * HALF], BF16, ("slope1_0", 0))
+        h[1, 1] = place("h1_1", [P, 4 * HALF], BF16, ("slope1_0", 2048))
+        tangent(0, 2)
+        open_sum("p4", 3, 4, [2, 3])
+        tangent(0, 3)
+        tangent(1, 2)
         quantize_tangent(0, 2, 4)
         quantize_tangent(1, 2, 3)
-        tangent(1, 3, "p3")
+        add_down("p1", 0, [0, 1, 2, 3])
+        add_down("p1", 1, [0, 1, 2, 3])
+        store("p1", nc.scalar.copy)
+        add_down("p7", 0, [0, 1])
+        add_down("p4", 0, [2, 3])
+        tangent(1, 3)
         quantize_tangent(1, 3, 4)
-        output_block(2, 3, every, "p6", tangent_last(every), nc.scalar.copy)
-        output_block(3, 4, [0, 1], "p5", tangent_last([0, 1]), nc.scalar.copy)
-        output_block(3, 4, [2, 3], "p4", tangent_last([2, 3]), nc.vector.tensor_copy)
+        add_down("p7", 1, [0, 1])
+        add_down("p4", 1, [2, 3])
+        store("p7", nc.scalar.copy)
+        store("p4", nc.vector.tensor_copy)

@@ -322,13 +322,13 @@ def tile_list_operator_tangent_flow_kernel(
         project_pass(1, 0, 1)
         project(1, 1, "p1")
         project(0, 2, "p4")
-        project(0, 3, "p5")
+        open_sum("p6", 0, 2, [0, 1])
         turned[2] = down_tile(2, "p7")
         slope_rows(slope_tile(1, 0, 2), 1, 0, square("sq1_0", th[1][:, :, 0:HALF]), affine_pool)
         grouped[2] = copy_down(turned[2], 2)
+        project(0, 3, "p7")
         late_squares = square("sq1_1", th[1][:, :, HALF:M])
-        open_sum("p6", 0, 2, [0, 1])
-        turned[3] = down_tile(3, "p7")
+        turned[3] = down_tile(3, "p5")
         grouped[3] = copy_down(turned[3], 3)
         slope_rows(slope_tile(1, 2, 4, ("picked3", 0)), 1, 0, late_squares, affine_scalar)
         h[0, 0] = place("h0_0", [P, 4 * HALF], BF16, ("wd_raw3", 0))
@@ -340,7 +340,7 @@ def tile_list_operator_tangent_flow_kernel(
         quantize_down(grouped[2], 2, ("wd_raw3", 4096))
         quantize_tangent(0, 0, 2)
         add_down("p6", 0, [0, 1])
-        open_sum("p7", 3, 4, [0, 1])
+        open_sum("p5", 3, 4, [0, 1])
         tangent(1, 0)
         project(1, 3, "p0")
         tangent(1, 1)
@@ -356,18 +356,19 @@ def tile_list_operator_tangent_flow_kernel(
         h[1, 1] = place("h1_1", [P, 4 * HALF], BF16, ("slope1_0", 2048))
         tangent(0, 2)
         open_sum("p4", 3, 4, [2, 3])
-        tangent(0, 3)
         tangent(1, 2)
-        quantize_tangent(0, 2, 4)
+        quantize_tangent(0, 2, 3)
         quantize_tangent(1, 2, 3)
         add_down("p1", 0, [0, 1, 2, 3])
         add_down("p1", 1, [0, 1, 2, 3])
         store("p1", nc.scalar.copy)
-        add_down("p7", 0, [0, 1])
-        add_down("p4", 0, [2, 3])
+        tangent(0, 3)
         tangent(1, 3)
+        quantize_tangent(0, 3, 4)
         quantize_tangent(1, 3, 4)
-        add_down("p7", 1, [0, 1])
+        add_down("p5", 0, [0, 1])
+        add_down("p4", 0, [2, 3])
+        add_down("p5", 1, [0, 1])
         add_down("p4", 1, [2, 3])
-        store("p7", nc.scalar.copy)
+        store("p5", nc.scalar.copy)
         store("p4", nc.vector.tensor_copy)

@@ -98,8 +98,8 @@ def tile_list_operator_tangent_flow_kernel(
 
         def interleave(grouped, raw, lo, hi, copy):
             copy(
-                out=grouped[:, 4 * lo : 4 * hi].rearrange("p (c i t) -> p c t i", i=4, t=4),
-                in_=raw[:, :, lo:hi].rearrange("p t (c i) -> p c t i", i=4),
+                out=grouped[:, 4 * lo : 4 * hi].rearrange("p (c i t) -> p c t i", i=2, t=4),
+                in_=raw[:, :, lo:hi].rearrange("p t (c i) -> p c t i", i=2),
             )
 
         def quantize(grouped, name, on=None):
@@ -149,8 +149,8 @@ def tile_list_operator_tangent_flow_kernel(
         def deal_words(listed, a):
             v[a] = place("v%d" % a, [P, S], U32)
             nc.vector.tensor_copy(
-                out=v[a][:].bitcast(I32).rearrange("p (j t c i) -> p j c t i", t=4, c=32, i=4),
-                in_=listed[:].bitcast(I32).rearrange("p (j c i t) -> p j c t i", t=4, c=32, i=4),
+                out=v[a][:].bitcast(I32).rearrange("p (u e c i) -> p c u i e", u=2, e=2, i=4),
+                in_=listed[:].bitcast(I32).rearrange("p (c i u e) -> p c u i e", u=2, e=2, i=4),
             )
 
         def gather_scales():
@@ -161,13 +161,13 @@ def tile_list_operator_tangent_flow_kernel(
         def deal_scales(listed):
             dealt = place("v_sc", [P, S], U8)
             nc.vector.tensor_copy(
-                out=dealt[:].rearrange("p (j t c i) -> p j c t i", j=J_PASSES, t=4, i=16),
-                in_=listed[:].rearrange("p (j c i t) -> p j c t i", j=J_PASSES, t=4, i=16),
+                out=dealt[:].rearrange("p (t c i) -> p c t i", t=4, i=16),
+                in_=listed[:].rearrange("p (c i t) -> p c t i", t=4, i=16),
             )
             return dealt
 
         def slot(a, jp, t):
-            cols = slice(jp * PASS + t * P, jp * PASS + (t + 1) * P)
+            cols = slice((J_PASSES * t + jp) * P, (J_PASSES * t + jp + 1) * P)
             return v[a][:, cols], v_sc[4 * a :, cols]
 
         def state_pass(a, jp, t):

@@ -216,9 +216,9 @@ def tile_list_operator_tangent_flow_kernel(
         def tangent(jp, c):
             b_ps = projected[jp, c]
             nc.vector.tensor_tensor(
-                out=h[jp, c // 2][:, (c % 2) * 4 * P : (c % 2 + 1) * 4 * P].rearrange("p (c i t) -> p c t i", i=2, t=4),
-                in0=b_ps[:].rearrange("p t (c i) -> p c t i", i=2),
-                in1=slopes[jp, c].rearrange("p t (c i) -> p c t i", i=2),
+                out=h[jp, c // 2][:, (c % 2) * 4 * P : (c % 2 + 1) * 4 * P].rearrange("p (c i t) -> p c t i", i=4, t=4),
+                in0=b_ps[:].rearrange("p t (c i) -> p c t i", i=4),
+                in1=slopes[jp, c].rearrange("p t (c i) -> p c t i", i=4),
                 op=ALU.mult,
             )
 

@@ -25,8 +25,9 @@ PASS = 512
 K_PASSES = K // PASS
 J_PASSES = S // PASS
 HALF = M // 2
-FIRST_SPLIT = 192
-DX_SPLIT = 320
+FIRST_SHARE = 64
+SECOND_SHARE = 320
+QUADRANTS = (0, 2, 1, 3)
 
 
 def tile_list_operator_tangent_flow_kernel(
@@ -57,7 +58,7 @@ def tile_list_operator_tangent_flow_kernel(
         make_identity(nc, ident[:])
 
         def load_table_scales():
-            for q in (0, 2, 1, 3):
+            for q in QUADRANTS:
                 nc.sync.dma_start(
                     out=tab_sc[32 * q : 32 * q + 4 * K_PASSES, :].bitcast(I32),
                     in_=tab_scales.bitcast(I32)[:, 4 * q : 4 * q + 4, :],
@@ -89,7 +90,7 @@ def tile_list_operator_tangent_flow_kernel(
                 out=words[:].bitcast(I32).rearrange("p (a c) -> p a c", a=K_PASSES),
                 in_=w4_words.bitcast(I32).rearrange("a p c -> p a c"),
             )
-            for q in (0, 2, 1, 3):
+            for q in QUADRANTS:
                 nc.sync.dma_start(
                     out=w4_sc[32 * q : 32 * q + 4, :].bitcast(I32).rearrange("r (a c) -> r a c", a=K_PASSES),
                     in_=w4_scales.bitcast(I32)[:, 4 * q : 4 * q + 4, :].rearrange("a r c -> r a c"),
@@ -133,13 +134,14 @@ def tile_list_operator_tangent_flow_kernel(
         wd_raw[0] = load_down(0)
         g_pos = load_gains()
         wd_raw[1] = load_down(1)
-        dx_raw[0] = load_rows(dx, 0, "dx0", spare=4096)
-        dx_raw[1] = load_rows(dx, 1, "dx1", spare=7168)
+        dx_raw[0] = load_rows(dx, 0, "dx0", spare=8192)
+        dx_raw[1] = load_rows(dx, 1, "dx1", spare=7232)
         wd_raw[2] = load_down(2)
         w4w = load_bypass()
         wd_raw[3] = load_down(3)
 
-        xq, dq, hq, wq, th, slopes, a_ps, v, h, sums, projected = {}, {}, {}, {}, {}, {}, {}, {}, {}, {}, {}
+        xq, dq, hq, wq, v, th, slopes, h = {}, {}, {}, {}, {}, {}, {}, {}
+        a_ps, projected, sums = {}, {}, {}
 
         def gather_words(a, on=None):
             listed = place("listed%d" % a, [P, S], U32, on)
@@ -175,9 +177,8 @@ def tile_list_operator_tangent_flow_kernel(
                 a_ps[jp, t] = psum.tile([P, M], F32, name="a_ps", tag="p%d" % (4 * jp + t))
             mx(a_ps[jp, t][:], slot(a, jp, t), xq[a], a == 0, a == K_PASSES - 1)
 
-        def tanh_pass(jp, on=None):
-            th[jp] = place("th%d" % jp, [P, 4, M], F32, on)
-            for t in range(4):
+        def tanh_slots(jp, lo, hi):
+            for t in range(lo, hi):
                 nc.scalar.activation(out=th[jp][:, t, :], in_=a_ps[jp, t][:], func=ACT.Tanh)
 
         def square(name, src, on=None):
@@ -259,8 +260,10 @@ def tile_list_operator_tangent_flow_kernel(
             sums[bank] = (acc, lo, hi, tiles)
             for a in range(K_PASSES):
                 for nt in tiles:
-                    lhs = (w4w[:, a * 2 * N + nt * 2 * P : a * 2 * N + (nt + 1) * 2 * P], w4_sc[:, a * N + nt * P : a * N + (nt + 1) * P])
-                    mx(acc[:, nt - tiles[0], :], lhs, columns(dq[a], lo * P, hi * P), a == 0 and nt == tiles[0], False, FP4X4)
+                    first = a * N + nt * P
+                    lhs = (w4w[:, 2 * first : 2 * (first + P)], w4_sc[:, first : first + P])
+                    rhs = columns(dq[a], lo * P, hi * P)
+                    mx(acc[:, nt - tiles[0], :], lhs, rhs, a == 0 and nt == tiles[0], False, FP4X4)
 
         def add_down(bank, jp, some):
             acc, lo, hi, tiles = sums[bank]
@@ -292,28 +295,32 @@ def tile_list_operator_tangent_flow_kernel(
         xq[1] = quantize(x_grp[:, 1, :], "xq1")
         for jp, t in slots:
             state_pass(1, jp, t)
-        tanh_pass(0)
+        th[0] = place("th0", [P, 4, M], F32)
+        tanh_slots(0, 0, 4)
         nc.scalar.activation(out=g_neg[:], in_=g_pos[:], func=ACT.Copy, scale=-1.0)
-        low = square("sq0_low", th[0][:, 0:2, :])
         turned = {0: down_tile(0, "p0", ("x1", 0))}
         turned[1] = down_tile(1, "p1")
         dx_grp = place("dx_grp0", [P, 4 * M], BF16)
-        interleave(dx_grp, dx_raw[0], 0, FIRST_SPLIT, nc.vector.tensor_copy)
-        interleave(dx_grp, dx_raw[0], FIRST_SPLIT, M, nc.scalar.copy)
+        interleave(dx_grp, dx_raw[0], 0, FIRST_SHARE, nc.vector.tensor_copy)
+        interleave(dx_grp, dx_raw[0], FIRST_SHARE, M, nc.scalar.copy)
         grouped = {0: copy_down(turned[0], 0, ("dx0", 0))}
         dq[0] = quantize(dx_grp[:], "dq0")
         project(0, 0, "p2", [0])
         project(0, 1, "p3", [0])
         project(1, 0, "p0", [0])
         dx_grp = place("dx_grp1", [P, 4 * M], BF16, ("dx0", 4096))
-        interleave(dx_grp, dx_raw[1], 0, DX_SPLIT, nc.vector.tensor_copy)
-        interleave(dx_grp, dx_raw[1], DX_SPLIT, M, nc.scalar.copy)
-        quantize_down(grouped[0], 0, ("dx1", 0))
+        interleave(dx_grp, dx_raw[1], 0, SECOND_SHARE, nc.vector.tensor_copy)
+        interleave(dx_grp, dx_raw[1], SECOND_SHARE, M, nc.scalar.copy)
+        quantize_down(grouped[0], 0, ("dx1", 64))
         dq[1] = quantize(dx_grp[:], "dq1")
-        grouped[1] = copy_down(turned[1], 1, ("dx1", 1024))
+        grouped[1] = copy_down(turned[1], 1, ("dx1", 1088))
         quantize_down(grouped[1], 1)
-        high = square("sq0_high", th[0][:, 2:4, :], ("dx1", 3072))
-        tanh_pass(1, ("dx1", 7168))
+        low = square("sq0_low", th[0][:, 0:2, :], ("dx1", 64 - 4096))
+        high = square("sq0_high", th[0][:, 2:4, :], ("dx1", 3136))
+        th[1] = place("th1", [P, 4, M], F32, ("dx1", 7232))
+        tanh_slots(1, 0, 2)
+        early_squares = [square("sq1_0_0", th[1][:, 0:2, 0:HALF])]
+        tanh_slots(1, 2, 3)
         slope = slope_tile(0, 0, 4, ("dx_grp1", 0))
         slope_rows(slope, 0, 0, low, affine_pool)
         slope_rows(slope, 0, 2, high, affine_pool)
@@ -322,10 +329,14 @@ def tile_list_operator_tangent_flow_kernel(
         project_pass(1, 0, 1)
         project(1, 1, "p1")
         project(0, 2, "p4")
+        turned[2] = down_tile(2, "p5")
         open_sum("p6", 0, 2, [0, 1])
-        turned[2] = down_tile(2, "p7")
-        slope_rows(slope_tile(1, 0, 2), 1, 0, square("sq1_0", th[1][:, :, 0:HALF]), affine_pool)
         grouped[2] = copy_down(turned[2], 2)
+        tanh_slots(1, 3, 4)
+        early_squares.append(square("sq1_0_1", th[1][:, 2:4, 0:HALF]))
+        slope = slope_tile(1, 0, 2)
+        for u in range(2):
+            slope_rows(slope, 1, 2 * u, early_squares[u], affine_pool)
         project(0, 3, "p7")
         late_squares = square("sq1_1", th[1][:, :, HALF:M])
         turned[3] = down_tile(3, "p5")
@@ -345,7 +356,7 @@ def tile_list_operator_tangent_flow_kernel(
         project(1, 3, "p0")
         tangent(1, 1)
         open_sum("p1", 2, 3, [0, 1, 2, 3])
-        quantize_down(grouped[3], 3, ("sq1_0", 0))
+        quantize_down(grouped[3], 3, ("sq1_0_1", 0))
         quantize_tangent(1, 0, 2)
         add_down("p6", 1, [0, 1])
         store("p6", nc.scalar.copy)

@@ -25,7 +25,7 @@ PASS = 512
 K_PASSES = K // PASS
 J_PASSES = S // PASS
 HALF = M // 2
-FIRST_SHARE = 64
+FIRST_SHARE = 192
 SECOND_SHARE = 320
 QUADRANTS = (0, 2, 1, 3)
 
@@ -80,8 +80,8 @@ def tile_list_operator_tangent_flow_kernel(
             return rows
 
         def load_gains():
-            gains = keep.tile([P, J_PASSES, 4], F32, name="g_pos")
-            nc.sync.dma_start(out=gains[:], in_=g.rearrange("(j p t) -> p j t", j=J_PASSES, t=4))
+            gains = keep.tile([P, J_PASSES, 8], F32, name="g_pos")[:, :, 0:4]
+            nc.sync.dma_start(out=gains, in_=g.rearrange("(j p t) -> p j t", j=J_PASSES, t=4))
             return gains
 
         def load_bypass():
@@ -137,8 +137,8 @@ def tile_list_operator_tangent_flow_kernel(
         dx_raw[0] = load_rows(dx, 0, "dx0", spare=8192)
         dx_raw[1] = load_rows(dx, 1, "dx1", spare=7232)
         wd_raw[2] = load_down(2)
-        w4w = load_bypass()
         wd_raw[3] = load_down(3)
+        w4w = load_bypass()
 
         xq, dq, hq, wq, v, th, slopes, h = {}, {}, {}, {}, {}, {}, {}, {}
         a_ps, projected, sums = {}, {}, {}
@@ -297,7 +297,8 @@ def tile_list_operator_tangent_flow_kernel(
             state_pass(1, jp, t)
         th[0] = place("th0", [P, 4, M], F32)
         tanh_slots(0, 0, 4)
-        nc.scalar.activation(out=g_neg[:], in_=g_pos[:], func=ACT.Copy, scale=-1.0)
+        nc.scalar.activation(out=g_neg[:], in_=g_pos, func=ACT.Copy, scale=-1.0)
+        low = square("sq0_low", th[0][:, 0:2, :])
         turned = {0: down_tile(0, "p0", ("x1", 0))}
         turned[1] = down_tile(1, "p1")
         dx_grp = place("dx_grp0", [P, 4 * M], BF16)
@@ -315,12 +316,11 @@ def tile_list_operator_tangent_flow_kernel(
         dq[1] = quantize(dx_grp[:], "dq1")
         grouped[1] = copy_down(turned[1], 1, ("dx1", 1088))
         quantize_down(grouped[1], 1)
-        low = square("sq0_low", th[0][:, 0:2, :], ("dx1", 64 - 4096))
         high = square("sq0_high", th[0][:, 2:4, :], ("dx1", 3136))
         th[1] = place("th1", [P, 4, M], F32, ("dx1", 7232))
         tanh_slots(1, 0, 2)
         early_squares = [square("sq1_0_0", th[1][:, 0:2, 0:HALF])]
-        tanh_slots(1, 2, 3)
+        tanh_slots(1, 2, 4)
         slope = slope_tile(0, 0, 4, ("dx_grp1", 0))
         slope_rows(slope, 0, 0, low, affine_pool)
         slope_rows(slope, 0, 2, high, affine_pool)
@@ -330,10 +330,9 @@ def tile_list_operator_tangent_flow_kernel(
         project(1, 1, "p1")
         project(0, 2, "p4")
         turned[2] = down_tile(2, "p5")
-        open_sum("p6", 0, 2, [0, 1])
-        grouped[2] = copy_down(turned[2], 2)
-        tanh_slots(1, 3, 4)
+        project(1, 2, "p6")
         early_squares.append(square("sq1_0_1", th[1][:, 2:4, 0:HALF]))
+        grouped[2] = copy_down(turned[2], 2)
         slope = slope_tile(1, 0, 2)
         for u in range(2):
             slope_rows(slope, 1, 2 * u, early_squares[u], affine_pool)
@@ -345,12 +344,12 @@ def tile_list_operator_tangent_flow_kernel(
         h[0, 0] = place("h0_0", [P, 4 * HALF], BF16, ("wd_raw3", 0))
         h[1, 0] = place("h1_0", [P, 4 * HALF], BF16, ("wd_raw3", 2048))
         tangent(0, 0)
-        open_sum("p2", 0, 2, [2, 3])
+        open_sum("p2", 0, 2, [0, 1])
         tangent(0, 1)
-        project(1, 2, "p3")
+        open_sum("p3", 0, 2, [2, 3])
         quantize_down(grouped[2], 2, ("wd_raw3", 4096))
         quantize_tangent(0, 0, 2)
-        add_down("p6", 0, [0, 1])
+        add_down("p2", 0, [0, 1])
         open_sum("p5", 3, 4, [0, 1])
         tangent(1, 0)
         project(1, 3, "p0")
@@ -358,11 +357,11 @@ def tile_list_operator_tangent_flow_kernel(
         open_sum("p1", 2, 3, [0, 1, 2, 3])
         quantize_down(grouped[3], 3, ("sq1_0_1", 0))
         quantize_tangent(1, 0, 2)
-        add_down("p6", 1, [0, 1])
-        store("p6", nc.scalar.copy)
-        add_down("p2", 0, [2, 3])
-        add_down("p2", 1, [2, 3])
+        add_down("p2", 1, [0, 1])
         store("p2", nc.scalar.copy)
+        add_down("p3", 0, [2, 3])
+        add_down("p3", 1, [2, 3])
+        store("p3", nc.scalar.copy)
         h[0, 1] = place("h0_1", [P, 4 * HALF], BF16, ("slope1_0", 0))
         h[1, 1] = place("h1_1", [P, 4 * HALF], BF16, ("slope1_0", 2048))
         tangent(0, 2)

@@ -57,11 +57,11 @@ def tile_list_operator_tangent_flow_kernel(
         ident = keep.tile([P, P], F32, name="ident")
         make_identity(nc, ident[:])
 
-        def load_table_scales():
+        def load_table_scales(a):
             for q in QUADRANTS:
                 nc.sync.dma_start(
-                    out=tab_sc[32 * q : 32 * q + 4 * K_PASSES, :].bitcast(I32),
-                    in_=tab_scales.bitcast(I32)[:, 4 * q : 4 * q + 4, :],
+                    out=tab_sc[32 * q + 4 * a : 32 * q + 4 * a + 4, :].bitcast(I32),
+                    in_=tab_scales.bitcast(I32)[a, 4 * q : 4 * q + 4, :],
                 )
 
         def load_rows(src, a, name, spare=0):
@@ -127,16 +127,17 @@ def tile_list_operator_tangent_flow_kernel(
         x_raw, dx_raw, tab, wd_raw = {}, {}, {}, {}
         tab[0] = load_table(0)
         nc.sync.dma_start(offsets[:], offs)
-        load_table_scales()
+        load_table_scales(0)
         x_raw[0] = load_rows(x, 0, "x0")
+        load_table_scales(1)
         tab[1] = load_table(1)
         x_raw[1] = load_rows(x, 1, "x1")
         wd_raw[0] = load_down(0)
-        g_pos = load_gains()
         wd_raw[1] = load_down(1)
         dx_raw[0] = load_rows(dx, 0, "dx0", spare=8192)
         dx_raw[1] = load_rows(dx, 1, "dx1", spare=7232)
         wd_raw[2] = load_down(2)
+        g_pos = load_gains()
         wd_raw[3] = load_down(3)
         w4w = load_bypass()
 
@@ -161,7 +162,7 @@ def tile_list_operator_tangent_flow_kernel(
             return listed
 
         def deal_scales(listed):
-            dealt = place("v_sc", [P, S], U8)
+            dealt = place("v_sc", [P, S], U8, ("x0", 4096))
             nc.vector.tensor_copy(
                 out=dealt[:].rearrange("p (t c i) -> p c t i", t=4, i=16),
                 in_=listed[:].rearrange("p (c i t) -> p c t i", t=4, i=16),
@@ -282,11 +283,11 @@ def tile_list_operator_tangent_flow_kernel(
         g_neg = keep.tile([P, J_PASSES, 4], F32, name="g_neg")
 
         listed = gather_words(0)
-        sc_list = gather_scales()
         deal_words(listed, 0)
-        v_sc = deal_scales(sc_list)
+        sc_list = gather_scales()
         interleave(x_grp[:, 0, :], x_raw[0], 0, M, nc.scalar.copy)
         xq[0] = quantize(x_grp[:, 0, :], "xq0")
+        v_sc = deal_scales(sc_list)
         for jp, t in slots:
             state_pass(0, jp, t)
         listed = gather_words(1, ("x0", 0))
@@ -297,7 +298,6 @@ def tile_list_operator_tangent_flow_kernel(
             state_pass(1, jp, t)
         th[0] = place("th0", [P, 4, M], F32)
         tanh_slots(0, 0, 4)
-        nc.scalar.activation(out=g_neg[:], in_=g_pos, func=ACT.Copy, scale=-1.0)
         low = square("sq0_low", th[0][:, 0:2, :])
         turned = {0: down_tile(0, "p0", ("x1", 0))}
         turned[1] = down_tile(1, "p1")
@@ -321,6 +321,7 @@ def tile_list_operator_tangent_flow_kernel(
         tanh_slots(1, 0, 2)
         early_squares = [square("sq1_0_0", th[1][:, 0:2, 0:HALF])]
         tanh_slots(1, 2, 4)
+        affine_pool(g_neg[:], g_pos, -1.0, 0.0)
         slope = slope_tile(0, 0, 4, ("dx_grp1", 0))
         slope_rows(slope, 0, 0, low, affine_pool)
         slope_rows(slope, 0, 2, high, affine_pool)

@@ -57,12 +57,13 @@ def tile_list_operator_tangent_flow_kernel(
         ident = keep.tile([P, P], F32, name="ident")
         make_identity(nc, ident[:])
 
-        def load_table_scales(a):
-            for q in QUADRANTS:
-                nc.sync.dma_start(
-                    out=tab_sc[32 * q + 4 * a : 32 * q + 4 * a + 4, :].bitcast(I32),
-                    in_=tab_scales.bitcast(I32)[a, 4 * q : 4 * q + 4, :],
-                )
+        def load_table_scales(quadrants):
+            for q in quadrants:
+                for a in range(K_PASSES):
+                    nc.sync.dma_start(
+                        out=tab_sc[32 * q + 4 * a : 32 * q + 4 * a + 4, :].bitcast(I32),
+                        in_=tab_scales.bitcast(I32)[a, 4 * q : 4 * q + 4, :],
+                    )
 
         def load_rows(src, a, name, spare=0):
             raw = place(name, [P, 4, M], F32, spare=spare)
@@ -127,9 +128,9 @@ def tile_list_operator_tangent_flow_kernel(
         x_raw, dx_raw, tab, wd_raw = {}, {}, {}, {}
         tab[0] = load_table(0)
         nc.sync.dma_start(offsets[:], offs)
-        load_table_scales(0)
+        load_table_scales(QUADRANTS[:2])
         x_raw[0] = load_rows(x, 0, "x0")
-        load_table_scales(1)
+        load_table_scales(QUADRANTS[2:])
         tab[1] = load_table(1)
         x_raw[1] = load_rows(x, 1, "x1")
         wd_raw[0] = load_down(0)

import math
from contextlib import ExitStack

import concourse.mybir as mybir
from concourse.masks import make_identity

K, T, S, M, N = 1024, 2048, 1024, 512, 512
FLOPS = 2 * (2 * K * S * M + S * N * M + K * N * M)

F32 = mybir.dt.float32
BF16 = mybir.dt.bfloat16
I32 = mybir.dt.int32
U32 = mybir.dt.uint32
U16 = mybir.dt.uint16
U8 = mybir.dt.uint8
FP8X4 = mybir.dt.float8_e4m3fn_x4
FP4X4 = mybir.dt.float4_e2m1fn_x4
ACT = mybir.ActivationFunctionType
ALU = mybir.AluOpType

WIDTH = {F32: 4, I32: 4, U32: 4, BF16: 2, U8: 1}

P = 128
PASS = 512
K_PASSES = K // PASS
J_PASSES = S // PASS
HALF = M // 2
FIRST_SHARE = 192
SECOND_SHARE = 320
QUADRANTS = (0, 2, 1, 3)


def tile_list_operator_tangent_flow_kernel(
    tc, tab_words, tab_scales, offs, x, dx, g, wdT, w4_words, w4_scales, out
):
    nc = tc.nc
    with ExitStack() as ctx:
        keep = ctx.enter_context(tc.tile_pool(name="keep", bufs=1))
        psum = ctx.enter_context(tc.psum_pool(name="psum", bufs=1))
        work = ctx.enter_context(tc.tile_pool(name="work", bufs=1))
        home = {"end": 0}

        def place(name, shape, dtype, on=None, spare=0):
            if on is None:
                home[name] = home["end"]
                home["end"] = home[name] + math.prod(shape[1:]) * WIDTH[dtype] + spare
            else:
                home[name] = home[on[0]] + on[1]
            return work.tile(shape, dtype, name=name, align_bytes=64, offset=home[name])

        offsets = keep.tile([P, S // 16], U16, name="offsets")

        tab_sc = place("tab_sc", [P, T], U8)
        nc.gpsimd.memset(tab_sc[:].bitcast(I32), 0)
        w4_sc = keep.tile([P, K_PASSES * N], U8, name="w4_sc", align_bytes=64)
        nc.gpsimd.memset(w4_sc[:].bitcast(I32), 0)
        ident = keep.tile([P, P], F32, name="ident")
        make_identity(nc, ident[:])

        def load_table_scales(quadrants):
            for q in quadrants:
                for a in range(K_PASSES):
                    nc.sync.dma_start(
                        out=tab_sc[32 * q + 4 * a : 32 * q + 4 * a + 4, :].bitcast(I32),
                        in_=tab_scales.bitcast(I32)[a, 4 * q : 4 * q + 4, :],
                    )

        def load_rows(src, a, name, spare=0):
            raw = place(name, [P, 4, M], F32, spare=spare)
            nc.sync.dma_start(out=raw[:], in_=src[a * PASS : (a + 1) * PASS, :].rearrange("(p t) m -> p t m", t=4))
            return raw

        def load_table(a):
            words = place("tab%d" % a, [P, T], I32)
            nc.sync.dma_start(out=words[:], in_=tab_words[a].rearrange("p n t -> p (n t)").bitcast(I32))
            return words

        def load_down(nt):
            rows = place("wd_raw%d" % nt, [P, T], F32)
            nc.sync.dma_start(out=rows[:], in_=wdT[nt * P : (nt + 1) * P, :])
            return rows

        def load_gains():
            gains = keep.tile([P, J_PASSES, 8], F32, name="g_pos")[:, :, 0:4]
            nc.sync.dma_start(out=gains, in_=g.rearrange("(j p t) -> p j t", j=J_PASSES, t=4))
            return gains

        def load_bypass():
            words = keep.tile([P, K_PASSES * 2 * N], U8, name="w4w", align_bytes=64)
            nc.sync.dma_start(
                out=words[:].bitcast(I32).rearrange("p (a c) -> p a c", a=K_PASSES),
                in_=w4_words.bitcast(I32).rearrange("a p c -> p a c"),
            )
            for q in QUADRANTS:
                nc.sync.dma_start(
                    out=w4_sc[32 * q : 32 * q + 4, :].bitcast(I32).rearrange("r (a c) -> r a c", a=K_PASSES),
                    in_=w4_scales.bitcast(I32)[:, 4 * q : 4 * q + 4, :].rearrange("a r c -> r a c"),
                )
            return words

        def interleave(grouped, raw, lo, hi, copy):
            copy(
                out=grouped[:, 4 * lo : 4 * hi].rearrange("p (c i t) -> p c t i", i=2, t=4),
                in_=raw[:, :, lo:hi].rearrange("p t (c i) -> p c t i", i=2),
            )

        def quantize(grouped, name, on=None):
            width = grouped.shape[1] // 4
            codes = place(name + "_c", [P, width], U32, on)
            scales = place(name + "_s", [P, width], U8)
            nc.vector.quantize_mx(out=codes[:].bitcast(FP8X4), scales=scales[:], in_=grouped)
            return codes, scales

        def columns(pair, lo, hi):
            return pair[0][:, lo:hi], pair[1][:, lo:hi]

        def mx(acc, lhs, rhs, first, last, fmt=FP8X4):
            nc.tensor.matmul_mx(
                out=acc,
                lhsT=lhs[0].bitcast(fmt),
                lhsT_scale=lhs[1],
                rhs=rhs[0].bitcast(FP8X4),
                rhs_scale=rhs[1],
                start=first,
                stop=last,
            )

        x_raw, dx_raw, tab, wd_raw = {}, {}, {}, {}
        tab[0] = load_table(0)
        nc.sync.dma_start(offsets[:], offs)
        load_table_scales(QUADRANTS[:2])
        x_raw[0] = load_rows(x, 0, "x0")
        load_table_scales(QUADRANTS[2:])
        tab[1] = load_table(1)
        x_raw[1] = load_rows(x, 1, "x1")
        wd_raw[0] = load_down(0)
        wd_raw[1] = load_down(1)
        dx_raw[0] = load_rows(dx, 0, "dx0", spare=8192)
        dx_raw[1] = load_rows(dx, 1, "dx1", spare=7232)
        wd_raw[2] = load_down(2)
        g_pos = load_gains()
        wd_raw[3] = load_down(3)
        w4w = load_bypass()

        xq, dq, hq, wq, v, th, slopes, h = {}, {}, {}, {}, {}, {}, {}, {}
        a_ps, projected, sums = {}, {}, {}

        def gather_words(a, on=None):
            listed = place("listed%d" % a, [P, S], U32, on)
            nc.vector.tensor_copy(out=listed[:], in_=tab[a][:].bitcast(U32).indirect(offsets[:]))
            return listed

        def deal_words(listed, a):
            v[a] = place("v%d" % a, [P, S], U32)
            nc.vector.tensor_copy(
                out=v[a][:].bitcast(I32).rearrange("p (u e c i) -> p c u i e", u=2, e=2, i=4),
                in_=listed[:].bitcast(I32).rearrange("p (c i u e) -> p c u i e", u=2, e=2, i=4),
            )

        def gather_scales():
            listed = place("sc_list", [P, S], U8)
            nc.vector.tensor_copy(out=listed[:], in_=tab_sc[:].indirect(offsets[:]))
            return listed

        def deal_scales(listed):
            dealt = place("v_sc", [P, S], U8, ("x0", 4096))
            nc.vector.tensor_copy(
                out=dealt[:].rearrange("p (t c i) -> p c t i", t=4, i=16),
                in_=listed[:].rearrange("p (c i t) -> p c t i", t=4, i=16),
            )
            return dealt

        def slot(a, jp, t):
            cols = slice((J_PASSES * t + jp) * P, (J_PASSES * t + jp + 1) * P)
            return v[a][:, cols], v_sc[4 * a :, cols]

        def state_pass(a, jp, t):
            if a == 0:
                a_ps[jp, t] = psum.tile([P, M], F32, name="a_ps", tag="p%d" % (4 * jp + t))
            mx(a_ps[jp, t][:], slot(a, jp, t), xq[a], a == 0, a == K_PASSES - 1)

        def tanh_slots(jp, lo, hi):
            for t in range(lo, hi):
                nc.scalar.activation(out=th[jp][:, t, :], in_=a_ps[jp, t][:], func=ACT.Tanh)

        def square(name, src, on=None):
            squares = place(name, list(src.shape), F32, on)
            nc.scalar.activation(out=squares[:], in_=src, func=ACT.Square)
            return squares

        def affine_scalar(dst, src, scale, bias):
            nc.scalar.activation(out=dst, in_=src, func=ACT.Identity, scale=scale, bias=bias)

        def affine_pool(dst, src, scale, bias):
            nc.gpsimd.tensor_scalar(out=dst, in0=src, scalar1=scale, scalar2=bias, op0=ALU.mult, op1=ALU.add)

        def slope_tile(jp, lo, hi, on=None):
            slope = place("slope%d_%d" % (jp, lo), [P, 4, (hi - lo) * P], F32, on)
            for c in range(lo, hi):
                slopes[jp, c] = slope[:, :, (c - lo) * P : (c - lo + 1) * P]
            return slope

        def slope_rows(slope, jp, first, squares, affine):
            for e in range(squares.shape[1]):
                t = first + e
                affine(slope[:, t, :], squares[:, e, :], g_neg[:, jp, t : t + 1], g_pos[:, jp, t : t + 1])

        def project(jp, c, bank, passes=(0, 1)):
            b_ps = psum.tile([P, 4, P], F32, name="b_ps", tag=bank)
            projected[jp, c] = b_ps
            for a in passes:
                project_pass(jp, c, a)

        def project_pass(jp, c, a):
            for t in range(4):
                first, last = a == 0 and t == 0, a == K_PASSES - 1 and t == 3
                mx(projected[jp, c][:, t, :], slot(a, jp, t), columns(dq[a], c * P, (c + 1) * P), first, last)

        def tangent(jp, c):
            b_ps = projected[jp, c]
            nc.vector.tensor_tensor(
                out=h[jp, c // 2][:, (c % 2) * 4 * P : (c % 2 + 1) * 4 * P].rearrange("p (c i t) -> p c t i", i=4, t=4),
                in0=b_ps[:].rearrange("p t (c i) -> p c t i", i=4),
                in1=slopes[jp, c].rearrange("p t (c i) -> p c t i", i=4),
                op=ALU.mult,
            )

        def quantize_tangent(jp, lo, hi):
            pair = quantize(h[jp, lo // 2][:, (lo % 2) * 4 * P : (lo % 2 + hi - lo) * 4 * P], "hq%d_%d" % (jp, lo))
            for c in range(lo, hi):
                hq[jp, c] = (pair, lo)

        def tangent_columns(jp, lo, hi):
            pair, first = hq[jp, lo]
            return columns(pair, (lo - first) * P, (hi - first) * P)

        def down_tile(nt, bank, on=None):
            turned = psum.tile([P, J_PASSES, 2, P], F32, name="turned", tag=bank)
            picked = place("picked%d" % nt, [P, S], BF16, on, spare=2048 * (nt == 3))
            nc.vector.tensor_copy(out=picked[:], in_=wd_raw[nt][:].indirect(offsets[:]))
            words = picked[:].bitcast(F32)
            for jp in range(J_PASSES):
                for u in range(2):
                    nc.tensor.transpose(turned[:, jp, u, :], words[:, jp * 2 * P + u : (jp + 1) * 2 * P : 2], ident[:])
            return turned

        def copy_down(turned, nt, on=None):
            grouped = place("wd_grp%d" % nt, [P, S], BF16, on)
            nc.scalar.copy(
                out=grouped[:].bitcast(F32).rearrange("p (j c i u) -> p j c u i", j=J_PASSES, i=2, u=2),
                in_=turned[:].rearrange("p j u (c i) -> p j c u i", i=2),
            )
            return grouped

        def quantize_down(grouped, nt, on=None):
            pair = quantize(grouped[:], "wq%d" % nt, on)
            for jp in range(J_PASSES):
                wq[nt, jp] = columns(pair, jp * P, (jp + 1) * P)

        def open_sum(bank, lo, hi, tiles):
            acc = psum.tile([P, len(tiles), (hi - lo) * P], F32, name="acc", tag=bank)
            sums[bank] = (acc, lo, hi, tiles)
            for a in range(K_PASSES):
                for nt in tiles:
                    first = a * N + nt * P
                    lhs = (w4w[:, 2 * first : 2 * (first + P)], w4_sc[:, first : first + P])
                    rhs = columns(dq[a], lo * P, hi * P)
                    mx(acc[:, nt - tiles[0], :], lhs, rhs, a == 0 and nt == tiles[0], False, FP4X4)

        def add_down(bank, jp, some):
            acc, lo, hi, tiles = sums[bank]
            for nt in some:
                mx(acc[:, nt - tiles[0], :], wq[nt, jp], tangent_columns(jp, lo, hi), False, jp == J_PASSES - 1 and nt == tiles[-1])

        def store(bank, copy_out):
            acc, lo, hi, tiles = sums[bank]
            result = place("result_" + bank, [P, len(tiles), (hi - lo) * P], F32)
            copy_out(out=result[:], in_=acc[:])
            rows = out[tiles[0] * P : (tiles[-1] + 1) * P, lo * P : hi * P]
            nc.sync.dma_start(out=rows.rearrange("(nt p) m -> p nt m", p=P), in_=result[:])

        slots = [(jp, t) for jp in range(J_PASSES) for t in range(4)]
        x_grp = place("x_grp", [P, K_PASSES, 4 * M], BF16)
        g_neg = keep.tile([P, J_PASSES, 4], F32, name="g_neg")

        listed = gather_words(0)
        deal_words(listed, 0)
        sc_list = gather_scales()
        interleave(x_grp[:, 0, :], x_raw[0], 0, M, nc.scalar.copy)
        xq[0] = quantize(x_grp[:, 0, :], "xq0")
        v_sc = deal_scales(sc_list)
        for jp, t in slots:
            state_pass(0, jp, t)
        listed = gather_words(1, ("x0", 0))
        deal_words(listed, 1)
        interleave(x_grp[:, 1, :], x_raw[1], 0, M, nc.scalar.copy)
        xq[1] = quantize(x_grp[:, 1, :], "xq1")
        for jp, t in slots:
            state_pass(1, jp, t)
        th[0] = place("th0", [P, 4, M], F32)
        tanh_slots(0, 0, 4)
        low = square("sq0_low", th[0][:, 0:2, :])
        turned = {0: down_tile(0, "p0", ("x1", 0))}
        turned[1] = down_tile(1, "p1")
        dx_grp = place("dx_grp0", [P, 4 * M], BF16)
        interleave(dx_grp, dx_raw[0], 0, FIRST_SHARE, nc.vector.tensor_copy)
        interleave(dx_grp, dx_raw[0], FIRST_SHARE, M, nc.scalar.copy)
        grouped = {0: copy_down(turned[0], 0, ("dx0", 0))}
        dq[0] = quantize(dx_grp[:], "dq0")
        project(0, 0, "p2", [0])
        project(0, 1, "p3", [0])
        project(1, 0, "p0", [0])
        dx_grp = place("dx_grp1", [P, 4 * M], BF16, ("dx0", 4096))
        interleave(dx_grp, dx_raw[1], 0, SECOND_SHARE, nc.vector.tensor_copy)
        interleave(dx_grp, dx_raw[1], SECOND_SHARE, M, nc.scalar.copy)
        quantize_down(grouped[0], 0, ("dx1", 64))
        dq[1] = quantize(dx_grp[:], "dq1")
        grouped[1] = copy_down(turned[1], 1, ("dx1", 1088))
        quantize_down(grouped[1], 1)
        high = square("sq0_high", th[0][:, 2:4, :], ("dx1", 3136))
        th[1] = place("th1", [P, 4, M], F32, ("dx1", 7232))
        tanh_slots(1, 0, 2)
        early_squares = [square("sq1_0_0", th[1][:, 0:2, 0:HALF])]
        tanh_slots(1, 2, 4)
        affine_pool(g_neg[:], g_pos, -1.0, 0.0)
        slope = slope_tile(0, 0, 4, ("dx_grp1", 0))
        slope_rows(slope, 0, 0, low, affine_pool)
        slope_rows(slope, 0, 2, high, affine_pool)
        project_pass(0, 0, 1)
        project_pass(0, 1, 1)
        project_pass(1, 0, 1)
        project(1, 1, "p1")
        project(0, 2, "p4")
        turned[2] = down_tile(2, "p5")
        project(1, 2, "p6")
        early_squares.append(square("sq1_0_1", th[1][:, 2:4, 0:HALF]))
        grouped[2] = copy_down(turned[2], 2)
        slope = slope_tile(1, 0, 2)
        for u in range(2):
            slope_rows(slope, 1, 2 * u, early_squares[u], affine_pool)
        project(0, 3, "p7")
        late_squares = square("sq1_1", th[1][:, :, HALF:M])
        turned[3] = down_tile(3, "p5")
        grouped[3] = copy_down(turned[3], 3)
        slope_rows(slope_tile(1, 2, 4, ("picked3", 0)), 1, 0, late_squares, affine_scalar)
        h[0, 0] = place("h0_0", [P, 4 * HALF], BF16, ("wd_raw3", 0))
        h[1, 0] = place("h1_0", [P, 4 * HALF], BF16, ("wd_raw3", 2048))
        tangent(0, 0)
        open_sum("p2", 0, 2, [0, 1])
        tangent(0, 1)
        open_sum("p3", 0, 2, [2, 3])
        quantize_down(grouped[2], 2, ("wd_raw3", 4096))
        quantize_tangent(0, 0, 2)
        add_down("p2", 0, [0, 1])
        open_sum("p5", 3, 4, [0, 1])
        tangent(1, 0)
        project(1, 3, "p0")
        tangent(1, 1)
        open_sum("p1", 2, 3, [0, 1, 2, 3])
        quantize_down(grouped[3], 3, ("sq1_0_1", 0))
        quantize_tangent(1, 0, 2)
        add_down("p2", 1, [0, 1])
        store("p2", nc.scalar.copy)
        add_down("p3", 0, [2, 3])
        add_down("p3", 1, [2, 3])
        store("p3", nc.scalar.copy)
        h[0, 1] = place("h0_1", [P, 4 * HALF], BF16, ("slope1_0", 0))
        h[1, 1] = place("h1_1", [P, 4 * HALF], BF16, ("slope1_0", 2048))
        tangent(0, 2)
        open_sum("p4", 3, 4, [2, 3])
        tangent(1, 2)
        quantize_tangent(0, 2, 3)
        quantize_tangent(1, 2, 3)
        add_down("p1", 0, [0, 1, 2, 3])
        add_down("p1", 1, [0, 1, 2, 3])
        store("p1", nc.scalar.copy)
        tangent(0, 3)
        tangent(1, 3)
        quantize_tangent(0, 3, 4)
        quantize_tangent(1, 3, 4)
        add_down("p5", 0, [0, 1])
        add_down("p4", 0, [2, 3])
        add_down("p5", 1, [0, 1])
        add_down("p4", 1, [2, 3])
        store("p5", nc.scalar.copy)
        store("p4", nc.vector.tensor_copy)
